import numpy as np
import ml_dtypes


def mxq(x, axis, fmt="e4m3"):
    dtype, down = {"e4m3": (ml_dtypes.float8_e4m3fn, 7), "e5m2": (ml_dtypes.float8_e5m2, 14)}[fmt]
    v = np.moveaxis(np.asarray(x, np.float32).astype(ml_dtypes.bfloat16).astype(np.float64), axis, -1)
    blocks = v.reshape(v.shape[:-1] + (-1, 32))
    amax = np.abs(blocks).max(-1, keepdims=True)
    byte = np.maximum(np.where(amax > 0, np.frexp(amax)[1] - 1 + 127, 0) - down, 1)
    scale = np.exp2(byte - 127.0)
    codes = (blocks / scale).astype(np.float32).astype(dtype).astype(np.float64)
    return np.moveaxis((codes * scale).reshape(v.shape), -1, axis)


WIDE = False


def mx_kscale(k):
    if not WIDE:
        return np.ones(k)
    levels = np.array([10, -10, 5, -5, 0])
    if k % 512:
        return np.exp2(np.random.permutation(np.resize(levels, k // 32))).repeat(32)
    a = np.empty((k // 512, 16))
    for p in range(k // 512):
        a[p, :8] = np.random.permutation(np.resize(levels, 8))
        for g in range(8):
            far = levels[np.abs(levels - a[p, g]) >= 10]
            a[p, g + 8] = far[np.random.randint(len(far))]
    return np.exp2(a.ravel()).repeat(32)


def f64(x):
    return np.asarray(x).astype(np.float64)


def striped(idx):
    return np.tile(idx.reshape(-1, 16).T, (8, 1)).astype(np.uint16)


def unstriped(offs):
    return offs[:16].T.reshape(-1).astype(np.int64)


E2M1 = np.array([0.0, 0.5, 1.0, 1.5, 2.0, 3.0, 4.0, 6.0, -0.0, -0.5, -1.0, -1.5, -2.0, -3.0, -4.0, -6.0])


def pack_weight(w, fmt):
    k, n = w.shape
    w = f64(np.asarray(w, np.float32).astype(ml_dtypes.bfloat16)).reshape(k // 32, 32, n)
    amax = np.abs(w).max(1)
    if fmt == "e4m3":
        byte = np.frexp(amax)[1] - 1 + 127 - 7
    else:
        mant, ex = np.frexp(amax / 6.0)
        byte = np.where(mant > 0.5, ex, ex - 1) + 127
    byte = np.clip(np.where(amax > 0, byte, 1), 1, 254)
    scaled = (w * np.exp2(127.0 - byte)[:, None, :]).reshape(k, n).astype(np.float32)
    by_word = np.ascontiguousarray(scaled.reshape(k // 512, 128, 4, n).transpose(0, 1, 3, 2))
    if fmt == "e4m3":
        words = by_word.astype(ml_dtypes.float8_e4m3fn).view(np.uint8)
    else:
        c = by_word.astype(ml_dtypes.float4_e2m1fn).view(np.uint8) & 0xF
        words = (c[..., 0::2] | (c[..., 1::2] << 4)).reshape(k // 512, 128, 2 * n)
    return np.ascontiguousarray(words), np.ascontiguousarray(byte.astype(np.uint8).reshape(k // 512, 16, n))


def unpack_weight(words, scales, fmt):
    g, _, n = scales.shape
    words = np.ascontiguousarray(words).reshape(g, 128, n, -1)
    if fmt == "e4m3":
        vals = words.view(ml_dtypes.float8_e4m3fn).astype(np.float64)
    else:
        nib = np.empty((g, 128, n, 4), np.uint8)
        nib[..., 0::2] = words & 0xF
        nib[..., 1::2] = words >> 4
        vals = E2M1[nib]
    vals = vals * np.repeat(np.exp2(scales.astype(np.float64) - 127.0), 8, axis=1)[..., None]
    return vals.transpose(0, 1, 3, 2).reshape(g * 512, n)


K, T, E, C, N = 2048, 640, 6, 128, 256
TOP = 3
PAD = 64


def by_expert(wq, xq):
    return np.concatenate([wq[e].T @ xq[:, e * C:(e + 1) * C] for e in range(E)], axis=1)


def setup_inputs():
    n = np.random.standard_normal
    s = mx_kscale(K)[:, None]
    slot_token = np.empty(E * C, np.int64); pos = np.tile(E * C + np.arange(T) % PAD, (TOP, 1)); taken = np.zeros(T, np.int64)
    liked = np.random.randn(T)
    for e in np.random.permutation(E):
        free = np.flatnonzero(taken < TOP); pick = np.random.permutation(free[np.argsort(-(liked[free] + np.random.gumbel(size=free.size)))[:C]]); slot_token[e * C:(e + 1) * C] = pick
        pos[taken[pick], pick] = e * C + np.arange(C); taken[pick] += 1
    g = np.random.uniform(0.2, 0.8, (TOP, T))
    w = [pack_weight(m, "e2m1") for m in n((E, K, N)) / np.sqrt(K) / s[None]]
    return {
        "xT": (n((K, T)) * s).astype(np.float32),
        "w_words": np.stack([m[0] for m in w]),
        "w_scales": np.stack([m[1] for m in w]),
        "gate": np.stack([np.tile(r, (N, 1)) for r in g]).astype(np.float32),
        "offs": striped(slot_token),
        "pos1": striped(pos[0]),
        "pos2": striped(pos[1]),
        "pos3": striped(pos[2]),
    }


def reference(xT, w_words, w_scales, gate, offs, pos1, pos2, pos3):
    idx = unstriped(offs)
    w = np.stack([unpack_weight(w_words[e], w_scales[e], "e2m1") for e in range(E)])
    xq = mxq(f64(xT)[:, idx], 0, "e4m3")
    y = by_expert(w, xq)
    y = np.concatenate([y, np.zeros((N, PAD))], axis=1)
    return sum(f64(gate[r]) * y[:, unstriped(p)] for r, p in enumerate((pos1, pos2, pos3)))

@@ -1,0 +1,206 @@
+from contextlib import ExitStack
+
+import concourse.mybir as mybir
+
+K, T, E, C, N = 2048, 640, 6, 128, 256
+TOP = 3
+PAD = 64
+S = E * C
+FLOPS = 2 * K * N * S
+
+F32 = mybir.dt.float32
+BF16 = mybir.dt.bfloat16
+I32 = mybir.dt.int32
+U32 = mybir.dt.uint32
+U16 = mybir.dt.uint16
+U8 = mybir.dt.uint8
+FP8X4 = mybir.dt.float8_e4m3fn_x4
+FP4X4 = mybir.dt.float4_e2m1fn_x4
+MULT = mybir.AluOpType.mult
+ADD = mybir.AluOpType.add
+
+P = 128
+PACK = 4
+K_PASS = P * PACK
+PASSES = K // K_PASS
+HALVES = N // P
+LIST_ROW = 16
+GROUP = 384
+SHARED_COLS = 1024
+SHIFT_ROWS = 112
+CHUNKS = (
+    ((0, 128, "s"), (128, 256, "s"), (384, 256, "v")),
+    ((0, 256, "s"), (256, 256, "s"), (512, 128, "s")),
+    ((0, 256, "s"), (256, 256, "s"), (512, 128, "v")),
+    ((0, 256, "s"), (256, 256, "s"), (512, 128, "v")),
+)
+
+
+def tile_moe_ecr_lin_none_kernel(
+    tc, xT, w_words, w_scales, gate, offs, pos1, pos2, pos3, out
+):
+    nc = tc.nc
+    with ExitStack() as ctx:
+        held = ctx.enter_context(tc.tile_pool(name="held", bufs=1))
+        psum = ctx.enter_context(tc.psum_pool(name="psum", bufs=1))
+
+        def keep(shape, dtype, name):
+            return held.tile(shape, dtype, name=name, align_bytes=64)
+
+        offs_sb = keep([P, S // LIST_ROW], U16, "offs_sb")
+        pos_sb = [keep([P, T // LIST_ROW], U16, "pos_sb%d" % r) for r in range(TOP)]
+
+        shared_bytes = keep([P, SHARED_COLS], U8, "shared_bytes")
+        last_bytes = keep([P, T], U8, "last_bytes")
+        shifted = [keep([P, S], U8, "shifted%d" % a) for a in (1, 2)]
+        w_plane = [keep([P, E * PASSES, P], U8, "w_plane%d" % h) for h in range(HALVES)]
+        y = [keep([P, S + PAD], F32, "y%d" % h) for h in range(HALVES)]
+
+        nc.gpsimd.memset(y[1][:, S:], 0.0)
+        nc.scalar.copy(y[0][:, S:], y[1][:, S:])
+        nc.vector.memset(shared_bytes[:].bitcast(I32), 0)
+        nc.vector.memset(w_plane[0][:].rearrange("p g n -> p (g n)").bitcast(I32), 0)
+        nc.gpsimd.memset(last_bytes[:].bitcast(I32), 0)
+        for plane in shifted:
+            nc.gpsimd.memset(plane[:].bitcast(I32), 0)
+        nc.vector.memset(w_plane[1][:].rearrange("p g n -> p (g n)").bitcast(I32), 0)
+
+        raw = {}
+        for a in range(PASSES):
+            rows = xT[a * K_PASS : (a + 1) * K_PASS, :].rearrange("(p j) t -> p j t", j=PACK)
+            for t0, width, unused in CHUNKS[a]:
+                raw[a, t0] = keep([P, PACK, width], F32, "raw%d_%d" % (a, t0))
+                nc.sync.dma_start(out=raw[a, t0][:], in_=rows[:, :, t0 : t0 + width])
+                if a == 0 and t0 == 0:
+                    nc.sync.dma_start(offs_sb[:], offs)
+
+        scale_rows = w_scales.bitcast(I32).rearrange("e a q n -> q (e a) n")
+        word_rows = w_words.bitcast(I32)
+
+        def load_w_plane(h):
+            for quad in range(4):
+                nc.sync.dma_start(
+                    out=w_plane[h][32 * quad : 32 * quad + 4].bitcast(I32),
+                    in_=scale_rows[4 * quad : 4 * quad + 4, :, 32 * h : 32 * (h + 1)],
+                )
+
+        w_codes = {}
+
+        def load_w_codes(h, a):
+            w_codes[h, a] = keep([P, E, 2 * P], U8, "w_codes%d_%d" % (h, a))
+            nc.sync.dma_start(
+                out=w_codes[h, a][:].bitcast(I32),
+                in_=word_rows[:, a, :, 64 * h : 64 * (h + 1)].rearrange("e p n -> p e n"),
+            )
+
+        gate_sb = {}
+
+        def load_gate(h, r):
+            gate_sb[h, r] = keep([P, T], F32, "gate%d_%d" % (h, r))
+            nc.sync.dma_start(out=gate_sb[h, r][:], in_=gate[r, h * P : (h + 1) * P, :])
+
+        load_w_plane(0)
+        for a in range(PASSES):
+            load_w_codes(0, a)
+        for tile, lst in zip(pos_sb, (pos1, pos2, pos3)):
+            nc.sync.dma_start(tile[:], lst)
+        load_gate(0, 0)
+        load_gate(0, 1)
+        load_w_plane(1)
+        for a in range(PASSES):
+            load_w_codes(1, a)
+        load_gate(0, 2)
+        for r in range(TOP):
+            load_gate(1, r)
+
+        words = [keep([P, T], U32, "words%d" % a) for a in range(PASSES)]
+        slot_words = {}
+        shared_slot_bytes = keep([P, S], U8, "shared_slot_bytes")
+        last_slot_bytes = [keep([P, GROUP], U8, "last_slot_bytes%d" % g) for g in range(2)]
+
+        def quantise(a):
+            for t0, width, eng in CHUNKS[a]:
+                grouped = keep([P, width, PACK], BF16, "grouped%d_%d" % (a, t0))
+                dst = grouped[:].rearrange("p (c i) j -> p c j i", i=4)
+                src = raw[a, t0][:].rearrange("p j (c i) -> p c j i", i=4)
+                if eng == "s":
+                    nc.scalar.copy(dst, src)
+                else:
+                    nc.vector.tensor_copy(dst, src)
+                if a == PASSES - 1:
+                    plane = last_bytes[:, t0 : t0 + width]
+                else:
+                    plane = shared_bytes[4 * a :, t0 : t0 + width]
+                nc.vector.quantize_mx(
+                    out=words[a][:, t0 : t0 + width].bitcast(FP8X4),
+                    scales=plane,
+                    in_=grouped[:].rearrange("p t j -> p (t j)"),
+                )
+
+        def group_offsets(g):
+            return offs_sb[:, g * GROUP // LIST_ROW : (g + 1) * GROUP // LIST_ROW]
+
+        def gather_words(a, g):
+            slot_words[a, g] = keep([P, GROUP], U32, "slot_words%d_%d" % (a, g))
+            nc.vector.tensor_copy(slot_words[a, g][:], words[a][:].indirect(group_offsets(g)))
+
+        quantise(0)
+        gather_words(0, 0)
+        gather_words(0, 1)
+        quantise(1)
+        gather_words(1, 0)
+        gather_words(1, 1)
+        quantise(2)
+        nc.vector.tensor_copy(shared_slot_bytes[:], shared_bytes[:].indirect(offs_sb[:]))
+        for a in (1, 2):
+            nc.scalar.dma_start(
+                out=shifted[a - 1][0:SHIFT_ROWS, :].bitcast(I32),
+                in_=shared_slot_bytes[4 * a : 4 * a + SHIFT_ROWS, :].bitcast(I32),
+            )
+        quantise(3)
+        gather_words(2, 0)
+        gather_words(2, 1)
+        for g in range(2):
+            nc.vector.tensor_copy(last_slot_bytes[g][:], last_bytes[:].indirect(group_offsets(g)))
+            gather_words(3, g)
+
+        def expert_pass(acc, h, e, a):
+            g, c0 = divmod(e * C, GROUP)
+            if a == PASSES - 1:
+                slot_plane = last_slot_bytes[g][:, c0 : c0 + C]
+            elif a == 0:
+                slot_plane = shared_slot_bytes[:, e * C : (e + 1) * C]
+            else:
+                slot_plane = shifted[a - 1][:, e * C : (e + 1) * C]
+            nc.tensor.matmul_mx(
+                out=acc,
+                lhsT=w_codes[h, a][:, e, :].bitcast(FP4X4),
+                lhsT_scale=w_plane[h][:, e * PASSES + a, :],
+                rhs=slot_words[a, g][:, c0 : c0 + C].bitcast(FP8X4),
+                rhs_scale=slot_plane,
+                start=(a == 0),
+                stop=(a == PASSES - 1),
+            )
+
+        first = [psum.tile([P, C], F32, name="first%d" % e) for e in range(E)]
+        for a in range(PASSES):
+            for e in range(E):
+                expert_pass(first[e][:], 0, e, a)
+                if a == PASSES - 1:
+                    nc.scalar.copy(y[0][:, e * C : (e + 1) * C], first[e][:])
+        second = [psum.tile([P, GROUP], F32, name="second%d" % g) for g in range(2)]
+        for g in range(2):
+            for i in range(GROUP // C):
+                for a in range(PASSES):
+                    expert_pass(second[g][:, i * C : (i + 1) * C], 1, g * GROUP // C + i, a)
+            nc.scalar.copy(y[1][:, g * GROUP : (g + 1) * GROUP], second[g][:])
+
+        for h in range(HALVES):
+            term = [keep([P, T], F32, "term%d_%d" % (h, r)) for r in range(TOP)]
+            pair = keep([P, T], F32, "pair%d" % h)
+            total = keep([P, T], F32, "total%d" % h)
+            for r in range(TOP):
+                nc.vector.tensor_tensor(term[r][:], y[h][:].indirect(pos_sb[r][:]), gate_sb[h, r][:], MULT)
+            nc.vector.tensor_tensor(pair[:], term[0][:], term[1][:], ADD)
+            nc.vector.tensor_tensor(total[:], pair[:], term[2][:], ADD)
+            nc.sync.dma_start(out=out[h * P : (h + 1) * P, :], in_=total[:])

@@ -30,10 +30,11 @@ SHARED_COLS = 1024
 SHIFT_ROWS = 112
 CHUNKS = (
     ((0, 128, "s"), (128, 256, "s"), (384, 256, "v")),
+    ((0, 256, "s"), (256, 256, "s"), (512, 128, "v")),
+    ((0, 256, "s"), (256, 256, "s"), (512, 128, "v")),
     ((0, 256, "s"), (256, 256, "s"), (512, 128, "s")),
-    ((0, 256, "s"), (256, 256, "s"), (512, 128, "v")),
-    ((0, 256, "s"), (256, 256, "s"), (512, 128, "v")),
 )
+TAIL = 384
 
 
 def tile_moe_ecr_lin_none_kernel(
@@ -50,20 +51,22 @@ def tile_moe_ecr_lin_none_kernel(
         offs_sb = keep([P, S // LIST_ROW], U16, "offs_sb")
         pos_sb = [keep([P, T // LIST_ROW], U16, "pos_sb%d" % r) for r in range(TOP)]
 
+        lists_sb = [offs_sb] + pos_sb
+        lists = (offs, pos1, pos2, pos3)
+
         shared_bytes = keep([P, SHARED_COLS], U8, "shared_bytes")
         last_bytes = keep([P, T], U8, "last_bytes")
         shifted = [keep([P, S], U8, "shifted%d" % a) for a in (1, 2)]
-        w_plane = [keep([P, E * PASSES, P], U8, "w_plane%d" % h) for h in range(HALVES)]
+        w_plane = keep([P, E * PASSES, N], U8, "w_plane")
         y = [keep([P, S + PAD], F32, "y%d" % h) for h in range(HALVES)]
 
         nc.gpsimd.memset(y[1][:, S:], 0.0)
         nc.scalar.copy(y[0][:, S:], y[1][:, S:])
         nc.vector.memset(shared_bytes[:].bitcast(I32), 0)
-        nc.vector.memset(w_plane[0][:].rearrange("p g n -> p (g n)").bitcast(I32), 0)
+        nc.vector.memset(w_plane[:].rearrange("p g n -> p (g n)").bitcast(I32), 0)
         nc.gpsimd.memset(last_bytes[:].bitcast(I32), 0)
         for plane in shifted:
             nc.gpsimd.memset(plane[:].bitcast(I32), 0)
-        nc.vector.memset(w_plane[1][:].rearrange("p g n -> p (g n)").bitcast(I32), 0)
 
         raw = {}
         for a in range(PASSES):
@@ -71,47 +74,27 @@ def tile_moe_ecr_lin_none_kernel(
             for t0, width, unused in CHUNKS[a]:
                 raw[a, t0] = keep([P, PACK, width], F32, "raw%d_%d" % (a, t0))
                 nc.sync.dma_start(out=raw[a, t0][:], in_=rows[:, :, t0 : t0 + width])
-                if a == 0 and t0 == 0:
-                    nc.sync.dma_start(offs_sb[:], offs)
+                if t0 == CHUNKS[a][1][0]:
+                    nc.sync.dma_start(lists_sb[a][:], lists[a])
 
         scale_rows = w_scales.bitcast(I32).rearrange("e a q n -> q (e a) n")
         word_rows = w_words.bitcast(I32)
 
-        def load_w_plane(h):
-            for quad in range(4):
-                nc.sync.dma_start(
-                    out=w_plane[h][32 * quad : 32 * quad + 4].bitcast(I32),
-                    in_=scale_rows[4 * quad : 4 * quad + 4, :, 32 * h : 32 * (h + 1)],
-                )
+        for r in range(4):
+            nc.sync.dma_start(out=w_plane[r:P:32].bitcast(I32), in_=scale_rows[r:16:4])
 
-        w_codes = {}
-
-        def load_w_codes(h, a):
-            w_codes[h, a] = keep([P, E, 2 * P], U8, "w_codes%d_%d" % (h, a))
+        w_codes = []
+        for a in range(PASSES):
+            w_codes.append(keep([P, E, 2 * N], U8, "w_codes%d" % a))
             nc.sync.dma_start(
-                out=w_codes[h, a][:].bitcast(I32),
-                in_=word_rows[:, a, :, 64 * h : 64 * (h + 1)].rearrange("e p n -> p e n"),
+                out=w_codes[a][:].bitcast(I32), in_=word_rows[:, a].rearrange("e p n -> p e n")
             )
 
         gate_sb = {}
-
-        def load_gate(h, r):
-            gate_sb[h, r] = keep([P, T], F32, "gate%d_%d" % (h, r))
-            nc.sync.dma_start(out=gate_sb[h, r][:], in_=gate[r, h * P : (h + 1) * P, :])
-
-        load_w_plane(0)
-        for a in range(PASSES):
-            load_w_codes(0, a)
-        for tile, lst in zip(pos_sb, (pos1, pos2, pos3)):
-            nc.sync.dma_start(tile[:], lst)
-        load_gate(0, 0)
-        load_gate(0, 1)
-        load_w_plane(1)
-        for a in range(PASSES):
-            load_w_codes(1, a)
-        load_gate(0, 2)
-        for r in range(TOP):
-            load_gate(1, r)
+        for h in range(HALVES):
+            for r in range(TOP):
+                gate_sb[h, r] = keep([P, T], F32, "gate%d_%d" % (h, r))
+                nc.sync.dma_start(out=gate_sb[h, r][:], in_=gate[r, h * P : (h + 1) * P, :])
 
         words = [keep([P, T], U32, "words%d" % a) for a in range(PASSES)]
         slot_words = {}
@@ -152,14 +135,14 @@ def tile_moe_ecr_lin_none_kernel(
         gather_words(1, 1)
         quantise(2)
         nc.vector.tensor_copy(shared_slot_bytes[:], shared_bytes[:].indirect(offs_sb[:]))
+        gather_words(2, 0)
+        gather_words(2, 1)
+        quantise(3)
         for a in (1, 2):
             nc.scalar.dma_start(
                 out=shifted[a - 1][0:SHIFT_ROWS, :].bitcast(I32),
                 in_=shared_slot_bytes[4 * a : 4 * a + SHIFT_ROWS, :].bitcast(I32),
             )
-        quantise(3)
-        gather_words(2, 0)
-        gather_words(2, 1)
         for g in range(2):
             nc.vector.tensor_copy(last_slot_bytes[g][:], last_bytes[:].indirect(group_offsets(g)))
             gather_words(3, g)
@@ -174,33 +157,50 @@ def tile_moe_ecr_lin_none_kernel(
                 slot_plane = shifted[a - 1][:, e * C : (e + 1) * C]
             nc.tensor.matmul_mx(
                 out=acc,
-                lhsT=w_codes[h, a][:, e, :].bitcast(FP4X4),
-                lhsT_scale=w_plane[h][:, e * PASSES + a, :],
+                lhsT=w_codes[a][:, e, 2 * P * h : 2 * P * (h + 1)].bitcast(FP4X4),
+                lhsT_scale=w_plane[:, e * PASSES + a, P * h : P * (h + 1)],
                 rhs=slot_words[a, g][:, c0 : c0 + C].bitcast(FP8X4),
                 rhs_scale=slot_plane,
                 start=(a == 0),
                 stop=(a == PASSES - 1),
             )
 
-        first = [psum.tile([P, C], F32, name="first%d" % e) for e in range(E)]
+        early = [(0, e) for e in range(E)] + [(1, 0), (1, 1)]
+        banks = [psum.tile([P, C], F32, name="bank%d" % b, tag="bank%d" % b) for b in range(len(early))]
         for a in range(PASSES):
-            for e in range(E):
-                expert_pass(first[e][:], 0, e, a)
+            for (h, e), bank in zip(early, banks):
+                expert_pass(bank[:], h, e, a)
                 if a == PASSES - 1:
-                    nc.scalar.copy(y[0][:, e * C : (e + 1) * C], first[e][:])
-        second = [psum.tile([P, GROUP], F32, name="second%d" % g) for g in range(2)]
-        for g in range(2):
-            for i in range(GROUP // C):
-                for a in range(PASSES):
-                    expert_pass(second[g][:, i * C : (i + 1) * C], 1, g * GROUP // C + i, a)
-            nc.scalar.copy(y[1][:, g * GROUP : (g + 1) * GROUP], second[g][:])
+                    nc.scalar.copy(y[h][:, e * C : (e + 1) * C], bank[:])
+        late = psum.tile([P, 4 * C], F32, name="late", tag="bank0")
+        for e in range(2, E):
+            for a in range(PASSES):
+                expert_pass(late[:, (e - 2) * C : (e - 1) * C], 1, e, a)
+        nc.scalar.copy(y[1][:, 2 * C : S], late[:])
 
-        for h in range(HALVES):
-            term = [keep([P, T], F32, "term%d_%d" % (h, r)) for r in range(TOP)]
-            pair = keep([P, T], F32, "pair%d" % h)
-            total = keep([P, T], F32, "total%d" % h)
-            for r in range(TOP):
-                nc.vector.tensor_tensor(term[r][:], y[h][:].indirect(pos_sb[r][:]), gate_sb[h, r][:], MULT)
-            nc.vector.tensor_tensor(pair[:], term[0][:], term[1][:], ADD)
-            nc.vector.tensor_tensor(total[:], pair[:], term[2][:], ADD)
-            nc.sync.dma_start(out=out[h * P : (h + 1) * P, :], in_=total[:])
+        term = {(h, r): keep([P, T], F32, "term%d_%d" % (h, r)) for h in range(HALVES) for r in range(TOP)}
+        pair = [keep([P, T], F32, "pair%d" % h) for h in range(HALVES)]
+        total = [keep([P, T], F32, "total%d" % h) for h in range(HALVES)]
+
+        def weigh(h, r, t0, t1):
+            picked = y[h][:].indirect(pos_sb[r][:, t0 // LIST_ROW : t1 // LIST_ROW])
+            nc.vector.tensor_tensor(term[h, r][:, t0:t1], picked, gate_sb[h, r][:, t0:t1], MULT)
+
+        def add_pair(h):
+            nc.vector.tensor_tensor(pair[h][:], term[h, 0][:], term[h, 1][:], ADD)
+
+        def finish(h, t0, t1, queue):
+            nc.vector.tensor_tensor(total[h][:, t0:t1], pair[h][:, t0:t1], term[h, 2][:, t0:t1], ADD)
+            queue.dma_start(out=out[h * P : (h + 1) * P, t0:t1], in_=total[h][:, t0:t1])
+
+        for r in range(TOP):
+            weigh(0, r, 0, T)
+        add_pair(0)
+        weigh(1, 0, 0, T)
+        finish(0, 0, T, nc.sync)
+        weigh(1, 1, 0, T)
+        weigh(1, 2, 0, TAIL)
+        add_pair(1)
+        weigh(1, 2, TAIL, T)
+        finish(1, 0, TAIL, nc.sync)
+        finish(1, TAIL, T, nc.scalar)

@@ -1,12 +1,13 @@
 from contextlib import ExitStack
 
 import concourse.mybir as mybir
+from concourse.masks import make_identity
 
 K, T, E, C, N = 2048, 640, 6, 128, 256
 TOP = 3
 PAD = 64
-S = E * C
-FLOPS = 2 * K * N * S
+SLOTS = E * C
+FLOPS = 2 * K * N * SLOTS
 
 F32 = mybir.dt.float32
 BF16 = mybir.dt.bfloat16
@@ -23,18 +24,20 @@ P = 128
 PACK = 4
 K_PASS = P * PACK
 PASSES = K // K_PASS
+LAST_PASS = PASSES - 1
 HALVES = N // P
-LIST_ROW = 16
-GROUP = 384
-SHARED_COLS = 1024
+QUADRANT = 32
+PLANE_ROWS = 4
+PER_COLUMN = 16
+RUN = 4
+
+PIECES = ((0, 256), (256, 256), (512, 128))
+VECTOR_PIECE = (1, 2, 2, 2)
+GROUP = SLOTS // 2
+WIDE = 1024
 SHIFT_ROWS = 112
-CHUNKS = (
-    ((0, 128, "s"), (128, 256, "s"), (384, 256, "v")),
-    ((0, 256, "s"), (256, 256, "s"), (512, 128, "v")),
-    ((0, 256, "s"), (256, 256, "s"), (512, 128, "v")),
-    ((0, 256, "s"), (256, 256, "s"), (512, 128, "s")),
-)
-TAIL = 384
+EARLY = 2
+SPLIT = 384
 
 
 def tile_moe_ecr_lin_none_kernel(
@@ -48,40 +51,47 @@ def tile_moe_ecr_lin_none_kernel(
         def keep(shape, dtype, name):
             return held.tile(shape, dtype, name=name, align_bytes=64)
 
-        offs_sb = keep([P, S // LIST_ROW], U16, "offs_sb")
-        pos_sb = [keep([P, T // LIST_ROW], U16, "pos_sb%d" % r) for r in range(TOP)]
+        def bank(width, name, number):
+            return psum.tile([P, width], F32, name=name, tag="bank%d" % number)
 
+        offs_sb = keep([P, SLOTS // PER_COLUMN], U16, "offs_sb")
+        pos_sb = [keep([P, T // PER_COLUMN], U16, "pos_sb%d" % r) for r in range(TOP)]
         lists_sb = [offs_sb] + pos_sb
         lists = (offs, pos1, pos2, pos3)
 
-        shared_bytes = keep([P, SHARED_COLS], U8, "shared_bytes")
+        shared_bytes = keep([P, WIDE], U8, "shared_bytes")
         last_bytes = keep([P, T], U8, "last_bytes")
-        shifted = [keep([P, S], U8, "shifted%d" % a) for a in (1, 2)]
+        shifted = {a: keep([P, SLOTS], U8, "shifted%d" % a) for a in range(1, LAST_PASS)}
         w_plane = keep([P, E * PASSES, N], U8, "w_plane")
-        y = [keep([P, S + PAD], F32, "y%d" % h) for h in range(HALVES)]
+        y = [keep([P, SLOTS + PAD], F32, "y%d" % h) for h in range(HALVES)]
 
-        nc.gpsimd.memset(y[1][:, S:], 0.0)
-        nc.scalar.copy(y[0][:, S:], y[1][:, S:])
+        nc.gpsimd.memset(y[1][:, SLOTS:], 0.0)
+        nc.scalar.copy(y[0][:, SLOTS:], y[1][:, SLOTS:])
         nc.vector.memset(shared_bytes[:].bitcast(I32), 0)
         nc.vector.memset(w_plane[:].rearrange("p g n -> p (g n)").bitcast(I32), 0)
         nc.gpsimd.memset(last_bytes[:].bitcast(I32), 0)
-        for plane in shifted:
+        for plane in shifted.values():
             nc.gpsimd.memset(plane[:].bitcast(I32), 0)
+
+        ident = keep([P, P], F32, "ident")
+        make_identity(nc, ident[:])
 
         raw = {}
         for a in range(PASSES):
             rows = xT[a * K_PASS : (a + 1) * K_PASS, :].rearrange("(p j) t -> p j t", j=PACK)
-            for t0, width, unused in CHUNKS[a]:
-                raw[a, t0] = keep([P, PACK, width], F32, "raw%d_%d" % (a, t0))
-                nc.sync.dma_start(out=raw[a, t0][:], in_=rows[:, :, t0 : t0 + width])
-                if t0 == CHUNKS[a][1][0]:
+            for i, (t0, width) in enumerate(PIECES):
+                raw[a, i] = keep([P, PACK, width], F32, "raw%d_%d" % (a, i))
+                nc.sync.dma_start(out=raw[a, i][:], in_=rows[:, :, t0 : t0 + width])
+                if i == 1:
                     nc.sync.dma_start(lists_sb[a][:], lists[a])
 
         scale_rows = w_scales.bitcast(I32).rearrange("e a q n -> q (e a) n")
         word_rows = w_words.bitcast(I32)
-
-        for r in range(4):
-            nc.sync.dma_start(out=w_plane[r:P:32].bitcast(I32), in_=scale_rows[r:16:4])
+        for r in range(PLANE_ROWS):
+            nc.sync.dma_start(
+                out=w_plane[r:P:QUADRANT].bitcast(I32),
+                in_=scale_rows[r : PLANE_ROWS * P // QUADRANT : PLANE_ROWS],
+            )
 
         w_codes = []
         for a in range(PASSES):
@@ -98,22 +108,22 @@ def tile_moe_ecr_lin_none_kernel(
 
         words = [keep([P, T], U32, "words%d" % a) for a in range(PASSES)]
         slot_words = {}
-        shared_slot_bytes = keep([P, S], U8, "shared_slot_bytes")
+        shared_slot_bytes = keep([P, SLOTS], U8, "shared_slot_bytes")
         last_slot_bytes = [keep([P, GROUP], U8, "last_slot_bytes%d" % g) for g in range(2)]
 
         def quantise(a):
-            for t0, width, eng in CHUNKS[a]:
-                grouped = keep([P, width, PACK], BF16, "grouped%d_%d" % (a, t0))
-                dst = grouped[:].rearrange("p (c i) j -> p c j i", i=4)
-                src = raw[a, t0][:].rearrange("p j (c i) -> p c j i", i=4)
-                if eng == "s":
-                    nc.scalar.copy(dst, src)
-                else:
+            for i, (t0, width) in enumerate(PIECES):
+                grouped = keep([P, width, PACK], BF16, "grouped%d_%d" % (a, i))
+                dst = grouped[:].rearrange("p (c i) j -> p c j i", i=RUN)
+                src = raw[a, i][:].rearrange("p j (c i) -> p c j i", i=RUN)
+                if i == VECTOR_PIECE[a]:
                     nc.vector.tensor_copy(dst, src)
-                if a == PASSES - 1:
+                else:
+                    nc.scalar.copy(dst, src)
+                if a == LAST_PASS:
                     plane = last_bytes[:, t0 : t0 + width]
                 else:
-                    plane = shared_bytes[4 * a :, t0 : t0 + width]
+                    plane = shared_bytes[PLANE_ROWS * a :, t0 : t0 + width]
                 nc.vector.quantize_mx(
                     out=words[a][:, t0 : t0 + width].bitcast(FP8X4),
                     scales=plane,
@@ -121,40 +131,36 @@ def tile_moe_ecr_lin_none_kernel(
                 )
 
         def group_offsets(g):
-            return offs_sb[:, g * GROUP // LIST_ROW : (g + 1) * GROUP // LIST_ROW]
+            return offs_sb[:, g * GROUP // PER_COLUMN : (g + 1) * GROUP // PER_COLUMN]
 
         def gather_words(a, g):
             slot_words[a, g] = keep([P, GROUP], U32, "slot_words%d_%d" % (a, g))
             nc.vector.tensor_copy(slot_words[a, g][:], words[a][:].indirect(group_offsets(g)))
 
-        quantise(0)
-        gather_words(0, 0)
-        gather_words(0, 1)
-        quantise(1)
-        gather_words(1, 0)
-        gather_words(1, 1)
-        quantise(2)
-        nc.vector.tensor_copy(shared_slot_bytes[:], shared_bytes[:].indirect(offs_sb[:]))
-        gather_words(2, 0)
-        gather_words(2, 1)
-        quantise(3)
-        for a in (1, 2):
+        for a in range(LAST_PASS):
+            quantise(a)
+            if a == LAST_PASS - 1:
+                nc.vector.tensor_copy(shared_slot_bytes[:], shared_bytes[:].indirect(offs_sb[:]))
+            for g in range(2):
+                gather_words(a, g)
+        quantise(LAST_PASS)
+        for a, plane in shifted.items():
             nc.scalar.dma_start(
-                out=shifted[a - 1][0:SHIFT_ROWS, :].bitcast(I32),
-                in_=shared_slot_bytes[4 * a : 4 * a + SHIFT_ROWS, :].bitcast(I32),
+                out=plane[0:SHIFT_ROWS, :].bitcast(I32),
+                in_=shared_slot_bytes[PLANE_ROWS * a : PLANE_ROWS * a + SHIFT_ROWS, :].bitcast(I32),
             )
         for g in range(2):
             nc.vector.tensor_copy(last_slot_bytes[g][:], last_bytes[:].indirect(group_offsets(g)))
-            gather_words(3, g)
+            gather_words(LAST_PASS, g)
 
         def expert_pass(acc, h, e, a):
             g, c0 = divmod(e * C, GROUP)
-            if a == PASSES - 1:
+            if a == LAST_PASS:
                 slot_plane = last_slot_bytes[g][:, c0 : c0 + C]
             elif a == 0:
                 slot_plane = shared_slot_bytes[:, e * C : (e + 1) * C]
             else:
-                slot_plane = shifted[a - 1][:, e * C : (e + 1) * C]
+                slot_plane = shifted[a][:, e * C : (e + 1) * C]
             nc.tensor.matmul_mx(
                 out=acc,
                 lhsT=w_codes[a][:, e, 2 * P * h : 2 * P * (h + 1)].bitcast(FP4X4),
@@ -162,45 +168,59 @@ def tile_moe_ecr_lin_none_kernel(
                 rhs=slot_words[a, g][:, c0 : c0 + C].bitcast(FP8X4),
                 rhs_scale=slot_plane,
                 start=(a == 0),
-                stop=(a == PASSES - 1),
+                stop=(a == LAST_PASS),
             )
 
-        early = [(0, e) for e in range(E)] + [(1, 0), (1, 1)]
-        banks = [psum.tile([P, C], F32, name="bank%d" % b, tag="bank%d" % b) for b in range(len(early))]
-        for a in range(PASSES):
-            for (h, e), bank in zip(early, banks):
-                expert_pass(bank[:], h, e, a)
-                if a == PASSES - 1:
-                    nc.scalar.copy(y[h][:, e * C : (e + 1) * C], bank[:])
-        late = psum.tile([P, 4 * C], F32, name="late", tag="bank0")
-        for e in range(2, E):
+        open_groups = [bank(C, "open%d" % b, b) for b in range(E + EARLY)]
+        for h, experts in ((0, range(E)), (1, range(EARLY))):
             for a in range(PASSES):
-                expert_pass(late[:, (e - 2) * C : (e - 1) * C], 1, e, a)
-        nc.scalar.copy(y[1][:, 2 * C : S], late[:])
+                for e in experts:
+                    acc = open_groups[h * E + e]
+                    expert_pass(acc[:], h, e, a)
+                    if a == LAST_PASS:
+                        nc.scalar.copy(y[h][:, e * C : (e + 1) * C], acc[:])
+        late = bank((E - EARLY) * C, "late", 0)
+        for e in range(EARLY, E):
+            for a in range(PASSES):
+                expert_pass(late[:, (e - EARLY) * C : (e - EARLY + 1) * C], 1, e, a)
+        nc.scalar.copy(y[1][:, EARLY * C : SLOTS], late[:])
 
         term = {(h, r): keep([P, T], F32, "term%d_%d" % (h, r)) for h in range(HALVES) for r in range(TOP)}
-        pair = [keep([P, T], F32, "pair%d" % h) for h in range(HALVES)]
         total = [keep([P, T], F32, "total%d" % h) for h in range(HALVES)]
 
         def weigh(h, r, t0, t1):
-            picked = y[h][:].indirect(pos_sb[r][:, t0 // LIST_ROW : t1 // LIST_ROW])
+            picked = y[h][:].indirect(pos_sb[r][:, t0 // PER_COLUMN : t1 // PER_COLUMN])
             nc.vector.tensor_tensor(term[h, r][:, t0:t1], picked, gate_sb[h, r][:, t0:t1], MULT)
 
-        def add_pair(h):
-            nc.vector.tensor_tensor(pair[h][:], term[h, 0][:], term[h, 1][:], ADD)
-
-        def finish(h, t0, t1, queue):
-            nc.vector.tensor_tensor(total[h][:, t0:t1], pair[h][:, t0:t1], term[h, 2][:, t0:t1], ADD)
-            queue.dma_start(out=out[h * P : (h + 1) * P, t0:t1], in_=total[h][:, t0:t1])
-
+        blocks = T // P
+        turned = [bank(P, "turned%d" % b, b + 1) for b in range(blocks)]
         for r in range(TOP):
             weigh(0, r, 0, T)
-        add_pair(0)
+            for b in range(blocks):
+                nc.tensor.matmul(
+                    turned[b][:],
+                    lhsT=term[0, r][:, b * P : (b + 1) * P],
+                    rhs=ident[:],
+                    start=(r == 0),
+                    stop=(r == TOP - 1),
+                    is_transpose=True,
+                )
+        turned_sb = keep([P, T], F32, "turned_sb")
+        back = [bank(SPLIT, "back0", blocks + 1), bank(T - SPLIT, "back1", blocks + 2)]
+        for b in range(blocks):
+            nc.scalar.copy(turned_sb[:, b * P : (b + 1) * P], turned[b][:])
+            part, c0 = divmod(b * P, SPLIT)
+            nc.tensor.transpose(back[part][:, c0 : c0 + P], turned_sb[:, b * P : (b + 1) * P], ident[:])
+        nc.scalar.copy(total[0][:, :SPLIT], back[0][:])
+        nc.scalar.copy(total[0][:, SPLIT:], back[1][:])
+        nc.sync.dma_start(out=out[0:P, :], in_=total[0][:])
+
+        pair = keep([P, T], F32, "pair")
         weigh(1, 0, 0, T)
-        finish(0, 0, T, nc.sync)
         weigh(1, 1, 0, T)
-        weigh(1, 2, 0, TAIL)
-        add_pair(1)
-        weigh(1, 2, TAIL, T)
-        finish(1, 0, TAIL, nc.sync)
-        finish(1, TAIL, T, nc.scalar)
+        weigh(1, 2, 0, SPLIT)
+        nc.vector.tensor_tensor(pair[:], term[1, 0][:], term[1, 1][:], ADD)
+        weigh(1, 2, SPLIT, T)
+        for t0, t1, queue in ((0, SPLIT, nc.sync), (SPLIT, T, nc.scalar)):
+            nc.vector.tensor_tensor(total[1][:, t0:t1], pair[:, t0:t1], term[1, 2][:, t0:t1], ADD)
+            queue.dma_start(out=out[P:N, t0:t1], in_=total[1][:, t0:t1])

@@ -26,17 +26,26 @@ K_PASS = P * PACK
 PASSES = K // K_PASS
 LAST_PASS = PASSES - 1
 HALVES = N // P
+BLOCKS = T // P
+BANK = 512
 QUADRANT = 32
 PLANE_ROWS = 4
 PER_COLUMN = 16
 RUN = 4
 
-PIECES = ((0, 256), (256, 256), (512, 128))
-VECTOR_PIECE = (1, 2, 2, 2)
-GROUP = SLOTS // 2
+PIECES = 4 * (((0, 256), (256, 256), (512, 128)),)
+CASTS = (
+    ((0, 256, False), (256, 512, True), (512, 640, False)),
+    ((0, 256, False), (256, 512, False), (512, 640, True)),
+    ((0, 256, False), (256, 512, False), (512, 640, True)),
+    ((0, 256, False), (256, 512, False), (512, 640, True)),
+)
+LAST_GROUPS = ((0, 384), (384, 256), (640, 128))
 WIDE = 1024
 SHIFT_ROWS = 112
 EARLY = 2
+REST = 256
+LAST = 512
 SPLIT = 384
 
 
@@ -56,42 +65,34 @@ def tile_moe_ecr_lin_none_kernel(
 
         offs_sb = keep([P, SLOTS // PER_COLUMN], U16, "offs_sb")
         pos_sb = [keep([P, T // PER_COLUMN], U16, "pos_sb%d" % r) for r in range(TOP)]
-        lists_sb = [offs_sb] + pos_sb
-        lists = (offs, pos1, pos2, pos3)
 
         shared_bytes = keep([P, WIDE], U8, "shared_bytes")
-        last_bytes = keep([P, T], U8, "last_bytes")
-        shifted = {a: keep([P, SLOTS], U8, "shifted%d" % a) for a in range(1, LAST_PASS)}
-        w_plane = keep([P, E * PASSES, N], U8, "w_plane")
+        last_bytes = keep([P, WIDE], U8, "last_bytes")
+        words = keep([P, LAST_PASS * T + WIDE], U32, "words")
         y = [keep([P, SLOTS + PAD], F32, "y%d" % h) for h in range(HALVES)]
 
         nc.gpsimd.memset(y[1][:, SLOTS:], 0.0)
         nc.scalar.copy(y[0][:, SLOTS:], y[1][:, SLOTS:])
         nc.vector.memset(shared_bytes[:].bitcast(I32), 0)
-        nc.vector.memset(w_plane[:].rearrange("p g n -> p (g n)").bitcast(I32), 0)
         nc.gpsimd.memset(last_bytes[:].bitcast(I32), 0)
-        for plane in shifted.values():
-            nc.gpsimd.memset(plane[:].bitcast(I32), 0)
+        nc.gpsimd.memset(words[:, PASSES * T :].bitcast(I32), 0)
 
         ident = keep([P, P], F32, "ident")
         make_identity(nc, ident[:])
 
+        scale_rows = w_scales.bitcast(I32).rearrange("e a q n -> q (e a) n")
+        word_rows = w_words.bitcast(I32)
+
+        lists_sb = [offs_sb] + pos_sb
+        lists = (offs, pos1, pos2, pos3)
         raw = {}
         for a in range(PASSES):
             rows = xT[a * K_PASS : (a + 1) * K_PASS, :].rearrange("(p j) t -> p j t", j=PACK)
-            for i, (t0, width) in enumerate(PIECES):
+            for i, (t0, width) in enumerate(PIECES[a]):
                 raw[a, i] = keep([P, PACK, width], F32, "raw%d_%d" % (a, i))
                 nc.sync.dma_start(out=raw[a, i][:], in_=rows[:, :, t0 : t0 + width])
                 if i == 1:
                     nc.sync.dma_start(lists_sb[a][:], lists[a])
-
-        scale_rows = w_scales.bitcast(I32).rearrange("e a q n -> q (e a) n")
-        word_rows = w_words.bitcast(I32)
-        for r in range(PLANE_ROWS):
-            nc.sync.dma_start(
-                out=w_plane[r:P:QUADRANT].bitcast(I32),
-                in_=scale_rows[r : PLANE_ROWS * P // QUADRANT : PLANE_ROWS],
-            )
 
         w_codes = []
         for a in range(PASSES):
@@ -100,72 +101,86 @@ def tile_moe_ecr_lin_none_kernel(
                 out=w_codes[a][:].bitcast(I32), in_=word_rows[:, a].rearrange("e p n -> p e n")
             )
 
-        gate_sb = {}
-        for h in range(HALVES):
-            for r in range(TOP):
-                gate_sb[h, r] = keep([P, T], F32, "gate%d_%d" % (h, r))
-                nc.sync.dma_start(out=gate_sb[h, r][:], in_=gate[r, h * P : (h + 1) * P, :])
+        gate_sb = []
+        for r in range(TOP):
+            gate_sb.append(keep([P, T], F32, "gate%d" % r))
+            nc.sync.dma_start(out=gate_sb[r][:], in_=gate[r, 0:P, :])
 
-        words = [keep([P, T], U32, "words%d" % a) for a in range(PASSES)]
-        slot_words = {}
+        slot_words = [keep([P, SLOTS], U32, "slot_words%d" % a) for a in range(LAST_PASS)]
+        last_slot_words = [keep([P, n], U32, "last_slot_words%d" % s0) for s0, n in LAST_GROUPS]
         shared_slot_bytes = keep([P, SLOTS], U8, "shared_slot_bytes")
-        last_slot_bytes = [keep([P, GROUP], U8, "last_slot_bytes%d" % g) for g in range(2)]
+        last_slot_bytes = keep([P, SLOTS], U8, "last_slot_bytes")
+
+        def word_column(a):
+            return (LAST_PASS - a) * T
 
         def quantise(a):
-            for i, (t0, width) in enumerate(PIECES):
-                grouped = keep([P, width, PACK], BF16, "grouped%d_%d" % (a, i))
-                dst = grouped[:].rearrange("p (c i) j -> p c j i", i=RUN)
-                src = raw[a, i][:].rearrange("p j (c i) -> p c j i", i=RUN)
-                if i == VECTOR_PIECE[a]:
-                    nc.vector.tensor_copy(dst, src)
+            grouped = keep([P, T * PACK], BF16, "grouped%d" % a)
+
+            def views(t0, t1):
+                i = max(i for i, (first, width) in enumerate(PIECES[a]) if first <= t0)
+                c0 = t0 - PIECES[a][i][0]
+                dst = grouped[:, t0 * PACK : t1 * PACK].rearrange("p (c i j) -> p c j i", i=RUN, j=PACK)
+                src = raw[a, i][:, :, c0 : c0 + t1 - t0].rearrange("p j (c i) -> p c j i", i=RUN)
+                return dst, src
+
+            for t0, t1, on_vector in CASTS[a]:
+                if on_vector:
+                    nc.vector.tensor_copy(*views(t0, t1))
                 else:
-                    nc.scalar.copy(dst, src)
+                    nc.scalar.copy(*views(t0, t1))
+            for t0, width in PIECES[a]:
                 if a == LAST_PASS:
                     plane = last_bytes[:, t0 : t0 + width]
                 else:
                     plane = shared_bytes[PLANE_ROWS * a :, t0 : t0 + width]
+                c0 = word_column(a) + t0
                 nc.vector.quantize_mx(
-                    out=words[a][:, t0 : t0 + width].bitcast(FP8X4),
+                    out=words[:, c0 : c0 + width].bitcast(FP8X4),
                     scales=plane,
-                    in_=grouped[:].rearrange("p t j -> p (t j)"),
+                    in_=grouped[:, t0 * PACK : (t0 + width) * PACK],
                 )
-
-        def group_offsets(g):
-            return offs_sb[:, g * GROUP // PER_COLUMN : (g + 1) * GROUP // PER_COLUMN]
-
-        def gather_words(a, g):
-            slot_words[a, g] = keep([P, GROUP], U32, "slot_words%d_%d" % (a, g))
-            nc.vector.tensor_copy(slot_words[a, g][:], words[a][:].indirect(group_offsets(g)))
 
         for a in range(LAST_PASS):
             quantise(a)
             if a == LAST_PASS - 1:
                 nc.vector.tensor_copy(shared_slot_bytes[:], shared_bytes[:].indirect(offs_sb[:]))
-            for g in range(2):
-                gather_words(a, g)
+            window = words[:, word_column(a) : word_column(a) + WIDE]
+            nc.vector.tensor_copy(slot_words[a][:], window.indirect(offs_sb[:]))
         quantise(LAST_PASS)
+        w_plane = held.tile([P, E * PASSES, N], U8, name="w_plane", tag="raw1_0", align_bytes=64)
+        for r in range(PLANE_ROWS):
+            nc.gpsimd.dma_start(
+                out=w_plane[r:P:QUADRANT].bitcast(I32),
+                in_=scale_rows[r : PLANE_ROWS * P // QUADRANT : PLANE_ROWS],
+            )
+        moved = held.tile([P, (LAST_PASS - 1) * SLOTS], U8, name="moved", tag="raw%d_1" % LAST_PASS, align_bytes=64)
+        shifted = {a: moved[:, (a - 1) * SLOTS : a * SLOTS] for a in range(1, LAST_PASS)}
         for a, plane in shifted.items():
             nc.scalar.dma_start(
                 out=plane[0:SHIFT_ROWS, :].bitcast(I32),
                 in_=shared_slot_bytes[PLANE_ROWS * a : PLANE_ROWS * a + SHIFT_ROWS, :].bitcast(I32),
             )
-        for g in range(2):
-            nc.vector.tensor_copy(last_slot_bytes[g][:], last_bytes[:].indirect(group_offsets(g)))
-            gather_words(LAST_PASS, g)
+        nc.vector.tensor_copy(last_slot_bytes[:], last_bytes[:].indirect(offs_sb[:]))
+        for g, (s0, n) in enumerate(LAST_GROUPS):
+            entries = offs_sb[:, s0 // PER_COLUMN : (s0 + n) // PER_COLUMN]
+            nc.vector.tensor_copy(last_slot_words[g][:], words[:, 0:T].indirect(entries))
 
         def expert_pass(acc, h, e, a):
-            g, c0 = divmod(e * C, GROUP)
+            slots = slice(e * C, (e + 1) * C)
             if a == LAST_PASS:
-                slot_plane = last_slot_bytes[g][:, c0 : c0 + C]
-            elif a == 0:
-                slot_plane = shared_slot_bytes[:, e * C : (e + 1) * C]
+                g = max(i for i, (s0, n) in enumerate(LAST_GROUPS) if s0 <= e * C)
+                c0 = e * C - LAST_GROUPS[g][0]
+                moving = last_slot_words[g][:, c0 : c0 + C]
+                slot_plane = last_slot_bytes[:, slots]
             else:
-                slot_plane = shifted[a][:, e * C : (e + 1) * C]
+                moving = slot_words[a][:, slots]
+                slot_plane = (shared_slot_bytes if a == 0 else shifted[a])[:, slots]
             nc.tensor.matmul_mx(
                 out=acc,
                 lhsT=w_codes[a][:, e, 2 * P * h : 2 * P * (h + 1)].bitcast(FP4X4),
                 lhsT_scale=w_plane[:, e * PASSES + a, P * h : P * (h + 1)],
-                rhs=slot_words[a, g][:, c0 : c0 + C].bitcast(FP8X4),
+                rhs=moving.bitcast(FP8X4),
                 rhs_scale=slot_plane,
                 start=(a == 0),
                 stop=(a == LAST_PASS),
@@ -178,7 +193,10 @@ def tile_moe_ecr_lin_none_kernel(
                     acc = open_groups[h * E + e]
                     expert_pass(acc[:], h, e, a)
                     if a == LAST_PASS:
-                        nc.scalar.copy(y[h][:, e * C : (e + 1) * C], acc[:])
+                        if h == 0 and e in (E - 3, E - 2):
+                            nc.vector.tensor_copy(y[h][:, e * C : (e + 1) * C], acc[:])
+                        else:
+                            nc.scalar.copy(y[h][:, e * C : (e + 1) * C], acc[:])
         late = bank((E - EARLY) * C, "late", 0)
         for e in range(EARLY, E):
             for a in range(PASSES):
@@ -190,37 +208,42 @@ def tile_moe_ecr_lin_none_kernel(
 
         def weigh(h, r, t0, t1):
             picked = y[h][:].indirect(pos_sb[r][:, t0 // PER_COLUMN : t1 // PER_COLUMN])
-            nc.vector.tensor_tensor(term[h, r][:, t0:t1], picked, gate_sb[h, r][:, t0:t1], MULT)
+            nc.vector.tensor_tensor(term[h, r][:, t0:t1], picked, gate_sb[r][:, t0:t1], MULT)
 
-        blocks = T // P
-        turned = [bank(P, "turned%d" % b, b + 1) for b in range(blocks)]
-        for r in range(TOP):
-            weigh(0, r, 0, T)
-            for b in range(blocks):
-                nc.tensor.matmul(
-                    turned[b][:],
-                    lhsT=term[0, r][:, b * P : (b + 1) * P],
-                    rhs=ident[:],
-                    start=(r == 0),
-                    stop=(r == TOP - 1),
-                    is_transpose=True,
-                )
-        turned_sb = keep([P, T], F32, "turned_sb")
-        back = [bank(SPLIT, "back0", blocks + 1), bank(T - SPLIT, "back1", blocks + 2)]
-        for b in range(blocks):
-            nc.scalar.copy(turned_sb[:, b * P : (b + 1) * P], turned[b][:])
-            part, c0 = divmod(b * P, SPLIT)
-            nc.tensor.transpose(back[part][:, c0 : c0 + P], turned_sb[:, b * P : (b + 1) * P], ident[:])
-        nc.scalar.copy(total[0][:, :SPLIT], back[0][:])
-        nc.scalar.copy(total[0][:, SPLIT:], back[1][:])
-        nc.sync.dma_start(out=out[0:P, :], in_=total[0][:])
+        def add_in_psum(h, blocks, turn_banks, back_banks):
+            turned = [bank(P, "turned%d_%d" % (h, b), turn_banks[i]) for i, b in enumerate(blocks)]
+            t0, t1 = blocks[0] * P, (blocks[-1] + 1) * P
+            for r in range(TOP):
+                weigh(h, r, t0, t1)
+                for i, b in enumerate(blocks):
+                    nc.tensor.matmul(
+                        turned[i][:],
+                        lhsT=term[h, r][:, b * P : (b + 1) * P],
+                        rhs=ident[:],
+                        start=(r == 0),
+                        stop=(r == TOP - 1),
+                        is_transpose=True,
+                    )
+            turned_sb = keep([P, t1 - t0], F32, "turned_sb%d" % h)
+            parts = [(c0, min(SPLIT, t1 - t0 - c0)) for c0 in range(0, t1 - t0, SPLIT)]
+            back = [bank(width, "back%d_%d" % (h, c0), back_banks[i]) for i, (c0, width) in enumerate(parts)]
+            for i in range(len(blocks)):
+                nc.scalar.copy(turned_sb[:, i * P : (i + 1) * P], turned[i][:])
+                part, c0 = divmod(i * P, SPLIT)
+                nc.tensor.transpose(back[part][:, c0 : c0 + P], turned_sb[:, i * P : (i + 1) * P], ident[:])
+            for (c0, width), part in zip(parts, back):
+                nc.scalar.copy(total[h][:, t0 + c0 : t0 + c0 + width], part[:])
+            nc.sync.dma_start(out=out[h * P : (h + 1) * P, t0:t1], in_=total[h][:, t0:t1])
+
+        add_in_psum(0, list(range(BLOCKS)), (1, 2, 3, 4, 5), (6, 7))
+        add_in_psum(1, [0, 1], (0, 1), (2,))
 
         pair = keep([P, T], F32, "pair")
-        weigh(1, 0, 0, T)
-        weigh(1, 1, 0, T)
-        weigh(1, 2, 0, SPLIT)
-        nc.vector.tensor_tensor(pair[:], term[1, 0][:], term[1, 1][:], ADD)
-        weigh(1, 2, SPLIT, T)
-        for t0, t1, queue in ((0, SPLIT, nc.sync), (SPLIT, T, nc.scalar)):
+        weigh(1, 0, REST, T)
+        weigh(1, 1, REST, T)
+        weigh(1, 2, REST, LAST)
+        nc.vector.tensor_tensor(pair[:, REST:], term[1, 0][:, REST:], term[1, 1][:, REST:], ADD)
+        weigh(1, 2, LAST, T)
+        for t0, t1, queue in ((REST, LAST, nc.sync), (LAST, T, nc.sync)):
             nc.vector.tensor_tensor(total[1][:, t0:t1], pair[:, t0:t1], term[1, 2][:, t0:t1], ADD)
             queue.dma_start(out=out[P:N, t0:t1], in_=total[1][:, t0:t1])

@@ -34,18 +34,17 @@ PER_COLUMN = 16
 RUN = 4
 
 PIECES = 4 * (((0, 256), (256, 256), (512, 128)),)
+QUANT_CALLS = ((0, 256), (256, 256), (512, 128))
 CASTS = (
     ((0, 256, False), (256, 512, True), (512, 640, False)),
     ((0, 256, False), (256, 512, False), (512, 640, True)),
     ((0, 256, False), (256, 512, False), (512, 640, True)),
-    ((0, 256, False), (256, 512, False), (512, 640, True)),
+    ((0, 256, False), (256, 512, False), (512, 640, False)),
 )
 LAST_GROUPS = ((0, 384), (384, 256), (640, 128))
 WIDE = 1024
 SHIFT_ROWS = 112
-EARLY = 2
-REST = 256
-LAST = 512
+LATE = 3
 SPLIT = 384
 
 
@@ -85,6 +84,14 @@ def tile_moe_ecr_lin_none_kernel(
 
         lists_sb = [offs_sb] + pos_sb
         lists = (offs, pos1, pos2, pos3)
+        w_plane = keep([P, E * PASSES, N], U8, "w_plane")
+
+        def load_scales(r):
+            nc.sync.dma_start(
+                out=w_plane[r:P:QUADRANT].bitcast(I32),
+                in_=scale_rows[r : PLANE_ROWS * P // QUADRANT : PLANE_ROWS],
+            )
+
         raw = {}
         for a in range(PASSES):
             rows = xT[a * K_PASS : (a + 1) * K_PASS, :].rearrange("(p j) t -> p j t", j=PACK)
@@ -94,17 +101,8 @@ def tile_moe_ecr_lin_none_kernel(
                 if i == 1:
                     nc.sync.dma_start(lists_sb[a][:], lists[a])
 
-        w_codes = []
-        for a in range(PASSES):
-            w_codes.append(keep([P, E, 2 * N], U8, "w_codes%d" % a))
-            nc.sync.dma_start(
-                out=w_codes[a][:].bitcast(I32), in_=word_rows[:, a].rearrange("e p n -> p e n")
-            )
-
-        gate_sb = []
-        for r in range(TOP):
-            gate_sb.append(keep([P, T], F32, "gate%d" % r))
-            nc.sync.dma_start(out=gate_sb[r][:], in_=gate[r, 0:P, :])
+        for r in range(PLANE_ROWS):
+            load_scales(r)
 
         slot_words = [keep([P, SLOTS], U32, "slot_words%d" % a) for a in range(LAST_PASS)]
         last_slot_words = [keep([P, n], U32, "last_slot_words%d" % s0) for s0, n in LAST_GROUPS]
@@ -129,7 +127,7 @@ def tile_moe_ecr_lin_none_kernel(
                     nc.vector.tensor_copy(*views(t0, t1))
                 else:
                     nc.scalar.copy(*views(t0, t1))
-            for t0, width in PIECES[a]:
+            for t0, width in QUANT_CALLS:
                 if a == LAST_PASS:
                     plane = last_bytes[:, t0 : t0 + width]
                 else:
@@ -147,20 +145,26 @@ def tile_moe_ecr_lin_none_kernel(
                 nc.vector.tensor_copy(shared_slot_bytes[:], shared_bytes[:].indirect(offs_sb[:]))
             window = words[:, word_column(a) : word_column(a) + WIDE]
             nc.vector.tensor_copy(slot_words[a][:], window.indirect(offs_sb[:]))
-        quantise(LAST_PASS)
-        w_plane = held.tile([P, E * PASSES, N], U8, name="w_plane", tag="raw1_0", align_bytes=64)
-        for r in range(PLANE_ROWS):
-            nc.gpsimd.dma_start(
-                out=w_plane[r:P:QUADRANT].bitcast(I32),
-                in_=scale_rows[r : PLANE_ROWS * P // QUADRANT : PLANE_ROWS],
-            )
-        moved = held.tile([P, (LAST_PASS - 1) * SLOTS], U8, name="moved", tag="raw%d_1" % LAST_PASS, align_bytes=64)
+        moved = keep([P, (LAST_PASS - 1) * SLOTS], U8, "moved")
         shifted = {a: moved[:, (a - 1) * SLOTS : a * SLOTS] for a in range(1, LAST_PASS)}
-        for a, plane in shifted.items():
-            nc.scalar.dma_start(
-                out=plane[0:SHIFT_ROWS, :].bitcast(I32),
-                in_=shared_slot_bytes[PLANE_ROWS * a : PLANE_ROWS * a + SHIFT_ROWS, :].bitcast(I32),
+        w_codes = []
+        for a in range(PASSES):
+            if a + 1 in shifted:
+                nc.sync.dma_start(
+                    out=shifted[a + 1][0:SHIFT_ROWS, :].bitcast(I32),
+                    in_=shared_slot_bytes[PLANE_ROWS * (a + 1) : PLANE_ROWS * (a + 1) + SHIFT_ROWS, :].bitcast(I32),
+                )
+            w_codes.append(keep([P, E, 2 * N], U8, "w_codes%d" % a))
+            nc.sync.dma_start(
+                out=w_codes[a][:].bitcast(I32), in_=word_rows[:, a].rearrange("e p n -> p e n")
             )
+
+        gate_sb = []
+        for r in range(TOP):
+            gate_sb.append(keep([P, T], F32, "gate%d" % r))
+            nc.sync.dma_start(out=gate_sb[r][:], in_=gate[r, 0:P, :])
+
+        quantise(LAST_PASS)
         nc.vector.tensor_copy(last_slot_bytes[:], last_bytes[:].indirect(offs_sb[:]))
         for g, (s0, n) in enumerate(LAST_GROUPS):
             entries = offs_sb[:, s0 // PER_COLUMN : (s0 + n) // PER_COLUMN]
@@ -186,22 +190,18 @@ def tile_moe_ecr_lin_none_kernel(
                 stop=(a == LAST_PASS),
             )
 
-        open_groups = [bank(C, "open%d" % b, b) for b in range(E + EARLY)]
-        for h, experts in ((0, range(E)), (1, range(EARLY))):
-            for a in range(PASSES):
-                for e in experts:
-                    acc = open_groups[h * E + e]
-                    expert_pass(acc[:], h, e, a)
-                    if a == LAST_PASS:
-                        if h == 0 and e in (E - 3, E - 2):
-                            nc.vector.tensor_copy(y[h][:, e * C : (e + 1) * C], acc[:])
-                        else:
-                            nc.scalar.copy(y[h][:, e * C : (e + 1) * C], acc[:])
-        late = bank((E - EARLY) * C, "late", 0)
-        for e in range(EARLY, E):
-            for a in range(PASSES):
-                expert_pass(late[:, (e - EARLY) * C : (e - EARLY + 1) * C], 1, e, a)
-        nc.scalar.copy(y[1][:, EARLY * C : SLOTS], late[:])
+        open_groups = [bank(C, "open%d" % e, e) for e in range(E)]
+        for a in range(PASSES):
+            for e in range(E):
+                expert_pass(open_groups[e][:], 0, e, a)
+                if a == LAST_PASS:
+                    nc.scalar.copy(y[0][:, e * C : (e + 1) * C], open_groups[e][:])
+        for b, e0 in enumerate(range(0, E, LATE)):
+            late = bank(LATE * C, "late%d" % b, E + b)
+            for i in range(LATE):
+                for a in range(PASSES):
+                    expert_pass(late[:, i * C : (i + 1) * C], 1, e0 + i, a)
+            nc.scalar.copy(y[1][:, e0 * C : (e0 + LATE) * C], late[:])
 
         term = {(h, r): keep([P, T], F32, "term%d_%d" % (h, r)) for h in range(HALVES) for r in range(TOP)}
         total = [keep([P, T], F32, "total%d" % h) for h in range(HALVES)]
@@ -210,40 +210,35 @@ def tile_moe_ecr_lin_none_kernel(
             picked = y[h][:].indirect(pos_sb[r][:, t0 // PER_COLUMN : t1 // PER_COLUMN])
             nc.vector.tensor_tensor(term[h, r][:, t0:t1], picked, gate_sb[r][:, t0:t1], MULT)
 
-        def add_in_psum(h, blocks, turn_banks, back_banks):
-            turned = [bank(P, "turned%d_%d" % (h, b), turn_banks[i]) for i, b in enumerate(blocks)]
-            t0, t1 = blocks[0] * P, (blocks[-1] + 1) * P
-            for r in range(TOP):
-                weigh(h, r, t0, t1)
-                for i, b in enumerate(blocks):
-                    nc.tensor.matmul(
-                        turned[i][:],
-                        lhsT=term[h, r][:, b * P : (b + 1) * P],
-                        rhs=ident[:],
-                        start=(r == 0),
-                        stop=(r == TOP - 1),
-                        is_transpose=True,
-                    )
-            turned_sb = keep([P, t1 - t0], F32, "turned_sb%d" % h)
-            parts = [(c0, min(SPLIT, t1 - t0 - c0)) for c0 in range(0, t1 - t0, SPLIT)]
-            back = [bank(width, "back%d_%d" % (h, c0), back_banks[i]) for i, (c0, width) in enumerate(parts)]
-            for i in range(len(blocks)):
-                nc.scalar.copy(turned_sb[:, i * P : (i + 1) * P], turned[i][:])
-                part, c0 = divmod(i * P, SPLIT)
-                nc.tensor.transpose(back[part][:, c0 : c0 + P], turned_sb[:, i * P : (i + 1) * P], ident[:])
-            for (c0, width), part in zip(parts, back):
-                nc.scalar.copy(total[h][:, t0 + c0 : t0 + c0 + width], part[:])
-            nc.sync.dma_start(out=out[h * P : (h + 1) * P, t0:t1], in_=total[h][:, t0:t1])
-
-        add_in_psum(0, list(range(BLOCKS)), (1, 2, 3, 4, 5), (6, 7))
-        add_in_psum(1, [0, 1], (0, 1), (2,))
+        blocks = T // P
+        turned = [bank(P, "turned%d" % b, b + 1) for b in range(blocks)]
+        for r in range(TOP):
+            weigh(0, r, 0, T)
+            for b in range(blocks):
+                nc.tensor.matmul(
+                    turned[b][:],
+                    lhsT=term[0, r][:, b * P : (b + 1) * P],
+                    rhs=ident[:],
+                    start=(r == 0),
+                    stop=(r == TOP - 1),
+                    is_transpose=True,
+                )
+        turned_sb = keep([P, T], F32, "turned_sb")
+        back = [bank(SPLIT, "back0", blocks + 1), bank(T - SPLIT, "back1", blocks + 2)]
+        for b in range(blocks):
+            nc.scalar.copy(turned_sb[:, b * P : (b + 1) * P], turned[b][:])
+            part, c0 = divmod(b * P, SPLIT)
+            nc.tensor.transpose(back[part][:, c0 : c0 + P], turned_sb[:, b * P : (b + 1) * P], ident[:])
+        nc.scalar.copy(total[0][:, :SPLIT], back[0][:])
+        nc.scalar.copy(total[0][:, SPLIT:], back[1][:])
+        nc.sync.dma_start(out=out[0:P, :], in_=total[0][:])
 
         pair = keep([P, T], F32, "pair")
-        weigh(1, 0, REST, T)
-        weigh(1, 1, REST, T)
-        weigh(1, 2, REST, LAST)
-        nc.vector.tensor_tensor(pair[:, REST:], term[1, 0][:, REST:], term[1, 1][:, REST:], ADD)
-        weigh(1, 2, LAST, T)
-        for t0, t1, queue in ((REST, LAST, nc.sync), (LAST, T, nc.sync)):
+        weigh(1, 0, 0, T)
+        weigh(1, 1, 0, T)
+        weigh(1, 2, 0, SPLIT)
+        nc.vector.tensor_tensor(pair[:], term[1, 0][:], term[1, 1][:], ADD)
+        weigh(1, 2, SPLIT, T)
+        for t0, t1, queue in ((0, SPLIT, nc.sync), (SPLIT, T, nc.scalar)):
             nc.vector.tensor_tensor(total[1][:, t0:t1], pair[:, t0:t1], term[1, 2][:, t0:t1], ADD)
             queue.dma_start(out=out[P:N, t0:t1], in_=total[1][:, t0:t1])

@@ -33,12 +33,16 @@ PLANE_ROWS = 4
 PER_COLUMN = 16
 RUN = 4
 
-PIECES = 4 * (((0, 256), (256, 256), (512, 128)),)
-QUANT_CALLS = ((0, 256), (256, 256), (512, 128))
+PIECES = (
+    ((0, 256), (256, 256), (512, 128)),
+    ((0, 256), (256, 384)),
+    ((0, 640),),
+    ((0, 640),),
+)
 CASTS = (
     ((0, 256, False), (256, 512, True), (512, 640, False)),
-    ((0, 256, False), (256, 512, False), (512, 640, True)),
-    ((0, 256, False), (256, 512, False), (512, 640, True)),
+    ((0, 256, False), (512, 640, True), (256, 512, False)),
+    ((0, 256, False), (256, 512, True), (512, 640, False)),
     ((0, 256, False), (256, 512, False), (512, 640, False)),
 )
 LAST_GROUPS = ((0, 384), (384, 256), (640, 128))
@@ -56,8 +60,8 @@ def tile_moe_ecr_lin_none_kernel(
         held = ctx.enter_context(tc.tile_pool(name="held", bufs=1))
         psum = ctx.enter_context(tc.psum_pool(name="psum", bufs=1))
 
-        def keep(shape, dtype, name):
-            return held.tile(shape, dtype, name=name, align_bytes=64)
+        def keep(shape, dtype, name, tag=None):
+            return held.tile(shape, dtype, name=name, tag=tag or name, align_bytes=64)
 
         def bank(width, name, number):
             return psum.tile([P, width], F32, name=name, tag="bank%d" % number)
@@ -98,7 +102,7 @@ def tile_moe_ecr_lin_none_kernel(
             for i, (t0, width) in enumerate(PIECES[a]):
                 raw[a, i] = keep([P, PACK, width], F32, "raw%d_%d" % (a, i))
                 nc.sync.dma_start(out=raw[a, i][:], in_=rows[:, :, t0 : t0 + width])
-                if i == 1:
+                if i == min(1, len(PIECES[a]) - 1):
                     nc.sync.dma_start(lists_sb[a][:], lists[a])
 
         for r in range(PLANE_ROWS):
@@ -113,21 +117,27 @@ def tile_moe_ecr_lin_none_kernel(
             return (LAST_PASS - a) * T
 
         def quantise(a):
-            grouped = keep([P, T * PACK], BF16, "grouped%d" % a)
+            grouped = {}
 
-            def views(t0, t1):
+            def views(t0, t1, on_vector):
+                if on_vector and a > 0:
+                    tag = "grouped%d_%d" % (a - 1, CASTS[a - 1][-1][0])
+                else:
+                    tag = None
+                grouped[t0] = keep([P, (t1 - t0) * PACK], BF16, "grouped%d_%d" % (a, t0), tag)
                 i = max(i for i, (first, width) in enumerate(PIECES[a]) if first <= t0)
                 c0 = t0 - PIECES[a][i][0]
-                dst = grouped[:, t0 * PACK : t1 * PACK].rearrange("p (c i j) -> p c j i", i=RUN, j=PACK)
+                dst = grouped[t0][:].rearrange("p (c i j) -> p c j i", i=RUN, j=PACK)
                 src = raw[a, i][:, :, c0 : c0 + t1 - t0].rearrange("p j (c i) -> p c j i", i=RUN)
                 return dst, src
 
             for t0, t1, on_vector in CASTS[a]:
                 if on_vector:
-                    nc.vector.tensor_copy(*views(t0, t1))
+                    nc.vector.tensor_copy(*views(t0, t1, True))
                 else:
-                    nc.scalar.copy(*views(t0, t1))
-            for t0, width in QUANT_CALLS:
+                    nc.scalar.copy(*views(t0, t1, False))
+            for t0, t1, on_vector in CASTS[a]:
+                width = t1 - t0
                 if a == LAST_PASS:
                     plane = last_bytes[:, t0 : t0 + width]
                 else:
@@ -136,7 +146,7 @@ def tile_moe_ecr_lin_none_kernel(
                 nc.vector.quantize_mx(
                     out=words[:, c0 : c0 + width].bitcast(FP8X4),
                     scales=plane,
-                    in_=grouped[:, t0 * PACK : (t0 + width) * PACK],
+                    in_=grouped[t0][:],
                 )
 
         for a in range(LAST_PASS):
@@ -147,24 +157,25 @@ def tile_moe_ecr_lin_none_kernel(
             nc.vector.tensor_copy(slot_words[a][:], window.indirect(offs_sb[:]))
         moved = keep([P, (LAST_PASS - 1) * SLOTS], U8, "moved")
         shifted = {a: moved[:, (a - 1) * SLOTS : a * SLOTS] for a in range(1, LAST_PASS)}
-        w_codes = []
+        w_early = keep([P, 2, E, 2 * N], U8, "w_early", "grouped2_%d" % CASTS[2][-1][0])
+        w_late = keep([P, 2, E, 2 * N], U8, "w_late", "shared_bytes")
+        w_codes = [w_early[:, 0], w_early[:, 1], w_late[:, 0], w_late[:, 1]]
         for a in range(PASSES):
-            if a + 1 in shifted:
+            if a - 1 in shifted:
                 nc.sync.dma_start(
-                    out=shifted[a + 1][0:SHIFT_ROWS, :].bitcast(I32),
-                    in_=shared_slot_bytes[PLANE_ROWS * (a + 1) : PLANE_ROWS * (a + 1) + SHIFT_ROWS, :].bitcast(I32),
+                    out=shifted[a - 1][0:SHIFT_ROWS, :].bitcast(I32),
+                    in_=shared_slot_bytes[PLANE_ROWS * (a - 1) : PLANE_ROWS * (a - 1) + SHIFT_ROWS, :].bitcast(I32),
                 )
-            w_codes.append(keep([P, E, 2 * N], U8, "w_codes%d" % a))
             nc.sync.dma_start(
-                out=w_codes[a][:].bitcast(I32), in_=word_rows[:, a].rearrange("e p n -> p e n")
+                out=w_codes[a].bitcast(I32), in_=word_rows[:, a].rearrange("e p n -> p e n")
             )
 
-        gate_sb = []
-        for r in range(TOP):
-            gate_sb.append(keep([P, T], F32, "gate%d" % r))
-            nc.sync.dma_start(out=gate_sb[r][:], in_=gate[r, 0:P, :])
-
         quantise(LAST_PASS)
+        gates = keep([P, TOP, T], F32, "gates", "raw%d_0" % LAST_PASS)
+        gate_sb = [gates[:, r] for r in range(TOP)]
+        for r in range(TOP):
+            nc.sync.dma_start(out=gate_sb[r], in_=gate[r, 0:P, :])
+
         nc.vector.tensor_copy(last_slot_bytes[:], last_bytes[:].indirect(offs_sb[:]))
         for g, (s0, n) in enumerate(LAST_GROUPS):
             entries = offs_sb[:, s0 // PER_COLUMN : (s0 + n) // PER_COLUMN]

@@ -34,21 +34,21 @@ PER_COLUMN = 16
 RUN = 4
 
 PIECES = (
-    ((0, 256), (256, 256), (512, 128)),
-    ((0, 256), (256, 384)),
+    ((0, 384), (384, 256)),
+    ((0, 640),),
     ((0, 640),),
     ((0, 640),),
 )
 CASTS = (
-    ((0, 256, False), (256, 512, True), (512, 640, False)),
-    ((0, 256, False), (512, 640, True), (256, 512, False)),
+    ((0, 256, True), (256, 384, False), (384, 512, True), (512, 640, False)),
+    ((256, 512, True), (0, 256, False), (512, 640, False)),
     ((0, 256, False), (256, 512, True), (512, 640, False)),
     ((0, 256, False), (256, 512, False), (512, 640, False)),
 )
 LAST_GROUPS = ((0, 384), (384, 256), (640, 128))
 WIDE = 1024
 SHIFT_ROWS = 112
-LATE = 3
+LATE = 2
 SPLIT = 384
 
 
@@ -86,8 +86,6 @@ def tile_moe_ecr_lin_none_kernel(
         scale_rows = w_scales.bitcast(I32).rearrange("e a q n -> q (e a) n")
         word_rows = w_words.bitcast(I32)
 
-        lists_sb = [offs_sb] + pos_sb
-        lists = (offs, pos1, pos2, pos3)
         w_plane = keep([P, E * PASSES, N], U8, "w_plane")
 
         def load_scales(r):
@@ -102,11 +100,13 @@ def tile_moe_ecr_lin_none_kernel(
             for i, (t0, width) in enumerate(PIECES[a]):
                 raw[a, i] = keep([P, PACK, width], F32, "raw%d_%d" % (a, i))
                 nc.sync.dma_start(out=raw[a, i][:], in_=rows[:, :, t0 : t0 + width])
-                if i == min(1, len(PIECES[a]) - 1):
-                    nc.sync.dma_start(lists_sb[a][:], lists[a])
+            if a == 0:
+                nc.sync.dma_start(offs_sb[:], offs)
 
         for r in range(PLANE_ROWS):
             load_scales(r)
+        for tile, entries in zip(pos_sb, (pos1, pos2, pos3)):
+            nc.sync.dma_start(tile[:], entries)
 
         slot_words = [keep([P, SLOTS], U32, "slot_words%d" % a) for a in range(LAST_PASS)]
         last_slot_words = [keep([P, n], U32, "last_slot_words%d" % s0) for s0, n in LAST_GROUPS]
@@ -201,14 +201,15 @@ def tile_moe_ecr_lin_none_kernel(
                 stop=(a == LAST_PASS),
             )
 
-        open_groups = [bank(C, "open%d" % e, e) for e in range(E)]
+        early = [(0, e) for e in range(E)] + [(1, e) for e in range(LATE)]
+        open_groups = [bank(C, "open%d" % b, b) for b in range(len(early))]
         for a in range(PASSES):
-            for e in range(E):
-                expert_pass(open_groups[e][:], 0, e, a)
+            for b, (h, e) in enumerate(early):
+                expert_pass(open_groups[b][:], h, e, a)
                 if a == LAST_PASS:
-                    nc.scalar.copy(y[0][:, e * C : (e + 1) * C], open_groups[e][:])
-        for b, e0 in enumerate(range(0, E, LATE)):
-            late = bank(LATE * C, "late%d" % b, E + b)
+                    nc.scalar.copy(y[h][:, e * C : (e + 1) * C], open_groups[b][:])
+        for b, e0 in zip((0, E - 1), range(LATE, E, LATE)):
+            late = bank(LATE * C, "late%d" % b, b)
             for i in range(LATE):
                 for a in range(PASSES):
                     expert_pass(late[:, i * C : (i + 1) * C], 1, e0 + i, a)
@@ -222,34 +223,50 @@ def tile_moe_ecr_lin_none_kernel(
             nc.vector.tensor_tensor(term[h, r][:, t0:t1], picked, gate_sb[r][:, t0:t1], MULT)
 
         blocks = T // P
+
+        def turn(banks, h, r, b, start, stop):
+            nc.tensor.matmul(
+                banks[b][:],
+                lhsT=term[h, r][:, b * P : (b + 1) * P],
+                rhs=ident[:],
+                start=start,
+                stop=stop,
+                is_transpose=True,
+            )
+
+        def turn_back(banks, staged, back, b):
+            nc.scalar.copy(staged[:, b * P : (b + 1) * P], banks[b][:])
+            part, c0 = divmod(b * P, SPLIT)
+            nc.tensor.transpose(back[part][:, c0 : c0 + P], staged[:, b * P : (b + 1) * P], ident[:])
+
         turned = [bank(P, "turned%d" % b, b + 1) for b in range(blocks)]
         for r in range(TOP):
             weigh(0, r, 0, T)
             for b in range(blocks):
-                nc.tensor.matmul(
-                    turned[b][:],
-                    lhsT=term[0, r][:, b * P : (b + 1) * P],
-                    rhs=ident[:],
-                    start=(r == 0),
-                    stop=(r == TOP - 1),
-                    is_transpose=True,
-                )
-        turned_sb = keep([P, T], F32, "turned_sb")
+                turn(turned, 0, r, b, r == 0, r == TOP - 1)
+        staged = keep([P, T], F32, "staged0")
         back = [bank(SPLIT, "back0", blocks + 1), bank(T - SPLIT, "back1", blocks + 2)]
         for b in range(blocks):
-            nc.scalar.copy(turned_sb[:, b * P : (b + 1) * P], turned[b][:])
-            part, c0 = divmod(b * P, SPLIT)
-            nc.tensor.transpose(back[part][:, c0 : c0 + P], turned_sb[:, b * P : (b + 1) * P], ident[:])
+            turn_back(turned, staged, back, b)
         nc.scalar.copy(total[0][:, :SPLIT], back[0][:])
-        nc.scalar.copy(total[0][:, SPLIT:], back[1][:])
-        nc.sync.dma_start(out=out[0:P, :], in_=total[0][:])
+        nc.sync.dma_start(out=out[0:P, :SPLIT], in_=total[0][:, :SPLIT])
 
-        pair = keep([P, T], F32, "pair")
-        weigh(1, 0, 0, T)
-        weigh(1, 1, 0, T)
-        weigh(1, 2, 0, SPLIT)
-        nc.vector.tensor_tensor(pair[:], term[1, 0][:], term[1, 1][:], ADD)
-        weigh(1, 2, SPLIT, T)
-        for t0, t1, queue in ((0, SPLIT, nc.sync), (SPLIT, T, nc.scalar)):
-            nc.vector.tensor_tensor(total[1][:, t0:t1], pair[:, t0:t1], term[1, 2][:, t0:t1], ADD)
+        turned = [bank(P, "turned_late%d" % b, b + 1) for b in range(blocks)]
+        staged = keep([P, T], F32, "staged1")
+        pair = [bank(SPLIT, "pair0", 0), bank(T - SPLIT, "pair1", blocks + 1)]
+        weigh(1, 2, 0, T)
+        for b in range(blocks):
+            turn(turned, 1, 2, b, True, False)
+        for t0, t1 in ((0, SPLIT), (SPLIT, T)):
+            weigh(1, 1, t0, t1)
+            for b in range(t0 // P, t1 // P):
+                turn(turned, 1, 1, b, False, True)
+            for b in range(t0 // P, t1 // P):
+                turn_back(turned, staged, pair, b)
+        nc.scalar.copy(total[0][:, SPLIT:], back[1][:])
+        nc.sync.dma_start(out=out[0:P, SPLIT:], in_=total[0][:, SPLIT:])
+        weigh(1, 0, 0, SPLIT)
+        weigh(1, 0, SPLIT, T)
+        for part, (t0, t1, queue) in enumerate(((0, SPLIT, nc.sync), (SPLIT, T, nc.scalar))):
+            nc.vector.tensor_tensor(total[1][:, t0:t1], pair[part][:], term[1, 0][:, t0:t1], ADD)
             queue.dma_start(out=out[P:N, t0:t1], in_=total[1][:, t0:t1])

@@ -49,6 +49,8 @@ LAST_GROUPS = ((0, 384), (384, 256), (640, 128))
 WIDE = 1024
 SHIFT_ROWS = 112
 LATE = 2
+TURN_BANKS = (1, 2, 3, 4, 6)
+WARM_UPS = 3
 SPLIT = 384
 
 
@@ -215,6 +217,18 @@ def tile_moe_ecr_lin_none_kernel(
                     expert_pass(late[:, i * C : (i + 1) * C], 1, e0 + i, a)
             nc.scalar.copy(y[1][:, e0 * C : (e0 + LATE) * C], late[:])
 
+        unread = bank(BANK, "unread", E - 1)
+        for a in range(WARM_UPS):
+            nc.tensor.matmul_mx(
+                out=unread[:],
+                lhsT=w_codes[0][:, 0, 0 : 2 * P].bitcast(FP4X4),
+                lhsT_scale=w_plane[:, 0, 0:P],
+                rhs=slot_words[0][:, 0:BANK].bitcast(FP8X4),
+                rhs_scale=shared_slot_bytes[:, 0:BANK],
+                start=True,
+                stop=True,
+            )
+
         term = {(h, r): keep([P, T], F32, "term%d_%d" % (h, r)) for h in range(HALVES) for r in range(TOP)}
         total = [keep([P, T], F32, "total%d" % h) for h in range(HALVES)]
 
@@ -239,21 +253,21 @@ def tile_moe_ecr_lin_none_kernel(
             part, c0 = divmod(b * P, SPLIT)
             nc.tensor.transpose(back[part][:, c0 : c0 + P], staged[:, b * P : (b + 1) * P], ident[:])
 
-        turned = [bank(P, "turned%d" % b, b + 1) for b in range(blocks)]
+        turned = [bank(P, "turned%d" % b, number) for b, number in enumerate(TURN_BANKS)]
         for r in range(TOP):
             weigh(0, r, 0, T)
             for b in range(blocks):
                 turn(turned, 0, r, b, r == 0, r == TOP - 1)
         staged = keep([P, T], F32, "staged0")
-        back = [bank(SPLIT, "back0", blocks + 1), bank(T - SPLIT, "back1", blocks + 2)]
+        back = [bank(SPLIT, "back0", 7), bank(T - SPLIT, "back1", 0)]
         for b in range(blocks):
             turn_back(turned, staged, back, b)
         nc.scalar.copy(total[0][:, :SPLIT], back[0][:])
         nc.sync.dma_start(out=out[0:P, :SPLIT], in_=total[0][:, :SPLIT])
 
-        turned = [bank(P, "turned_late%d" % b, b + 1) for b in range(blocks)]
+        turned = [bank(P, "turned_late%d" % b, number) for b, number in enumerate(TURN_BANKS)]
         staged = keep([P, T], F32, "staged1")
-        pair = [bank(SPLIT, "pair0", 0), bank(T - SPLIT, "pair1", blocks + 1)]
+        pair = [bank(SPLIT, "pair0", 5), bank(T - SPLIT, "pair1", 7)]
         weigh(1, 2, 0, T)
         for b in range(blocks):
             turn(turned, 1, 2, b, True, False)

@@ -19,39 +19,30 @@ FP8X4 = mybir.dt.float8_e4m3fn_x4
 FP4X4 = mybir.dt.float4_e2m1fn_x4
 MULT = mybir.AluOpType.mult
 ADD = mybir.AluOpType.add
+COPY = mybir.ActivationFunctionType.Copy
 
 P = 128
 PACK = 4
 K_PASS = P * PACK
 PASSES = K // K_PASS
-LAST_PASS = PASSES - 1
+LAST = PASSES - 1
 HALVES = N // P
-BLOCKS = T // P
-BANK = 512
 QUADRANT = 32
 PLANE_ROWS = 4
 PER_COLUMN = 16
 RUN = 4
-
-PIECES = (
-    ((0, 384), (384, 256)),
-    ((0, 640),),
-    ((0, 640),),
-    ((0, 640),),
-)
-CASTS = (
-    ((0, 256, True), (256, 384, False), (384, 512, True), (512, 640, False)),
-    ((256, 512, True), (0, 256, False), (512, 640, False)),
-    ((0, 256, False), (256, 512, True), (512, 640, False)),
-    ((0, 256, False), (256, 512, False), (512, 640, False)),
-)
-LAST_GROUPS = ((0, 384), (384, 256), (640, 128))
 WIDE = 1024
-SHIFT_ROWS = 112
-LATE = 2
-TURN_BANKS = (1, 2, 3, 4, 6)
-WARM_UPS = 3
-SPLIT = 384
+LIVE_ROWS = 3 * QUADRANT + PLANE_ROWS
+
+LOADS = (((0, 384), (384, 640)), ((0, 640),), ((0, 640),), ((0, 640),))
+ROUNDS = (
+    ((0, 256, "v"), (256, 384, "s"), (384, 512, "v"), (512, 640, "s")),
+    ((256, 512, "v"), (0, 256, "s"), (512, 640, "s")),
+    ((0, 256, "s"), (256, 512, "v"), (512, 640, "s")),
+    ((0, 256, "s"), (256, 512, "s"), (512, 640, "s")),
+)
+GROUPS = ((0, 3), (3, 5), (5, 6))
+PARTS = ((0, 384), (384, 640))
 
 
 def tile_moe_ecr_lin_none_kernel(
@@ -70,217 +61,187 @@ def tile_moe_ecr_lin_none_kernel(
 
         offs_sb = keep([P, SLOTS // PER_COLUMN], U16, "offs_sb")
         pos_sb = [keep([P, T // PER_COLUMN], U16, "pos_sb%d" % r) for r in range(TOP)]
-
-        shared_bytes = keep([P, WIDE], U8, "shared_bytes")
+        early_bytes = keep([P, WIDE], U8, "early_bytes")
         last_bytes = keep([P, WIDE], U8, "last_bytes")
-        words = keep([P, LAST_PASS * T + WIDE], U32, "words")
+        words = keep([P, LAST * T + WIDE], U32, "words")
         y = [keep([P, SLOTS + PAD], F32, "y%d" % h) for h in range(HALVES)]
 
         nc.gpsimd.memset(y[1][:, SLOTS:], 0.0)
         nc.scalar.copy(y[0][:, SLOTS:], y[1][:, SLOTS:])
-        nc.vector.memset(shared_bytes[:].bitcast(I32), 0)
+        nc.vector.memset(early_bytes[:].bitcast(I32), 0)
         nc.gpsimd.memset(last_bytes[:].bitcast(I32), 0)
         nc.gpsimd.memset(words[:, PASSES * T :].bitcast(I32), 0)
-
         ident = keep([P, P], F32, "ident")
         make_identity(nc, ident[:])
-
-        scale_rows = w_scales.bitcast(I32).rearrange("e a q n -> q (e a) n")
-        word_rows = w_words.bitcast(I32)
-
-        w_plane = keep([P, E * PASSES, N], U8, "w_plane")
-
-        def load_scales(r):
-            nc.sync.dma_start(
-                out=w_plane[r:P:QUADRANT].bitcast(I32),
-                in_=scale_rows[r : PLANE_ROWS * P // QUADRANT : PLANE_ROWS],
-            )
 
         raw = {}
         for a in range(PASSES):
             rows = xT[a * K_PASS : (a + 1) * K_PASS, :].rearrange("(p j) t -> p j t", j=PACK)
-            for i, (t0, width) in enumerate(PIECES[a]):
-                raw[a, i] = keep([P, PACK, width], F32, "raw%d_%d" % (a, i))
-                nc.sync.dma_start(out=raw[a, i][:], in_=rows[:, :, t0 : t0 + width])
+            for t0, t1 in LOADS[a]:
+                raw[a, t0] = keep([P, PACK, t1 - t0], F32, "raw%d_%d" % (a, t0))
+                nc.sync.dma_start(out=raw[a, t0][:], in_=rows[:, :, t0:t1])
             if a == 0:
                 nc.sync.dma_start(offs_sb[:], offs)
 
+        scale_rows = w_scales.bitcast(I32).rearrange("e a q n -> q (e a) n")
+        w_plane = keep([P, E * PASSES, N], U8, "w_plane")
         for r in range(PLANE_ROWS):
-            load_scales(r)
+            nc.sync.dma_start(
+                out=w_plane[r:P:QUADRANT].bitcast(I32),
+                in_=scale_rows[r : PLANE_ROWS * P // QUADRANT : PLANE_ROWS],
+            )
         for tile, entries in zip(pos_sb, (pos1, pos2, pos3)):
             nc.sync.dma_start(tile[:], entries)
 
-        slot_words = [keep([P, SLOTS], U32, "slot_words%d" % a) for a in range(LAST_PASS)]
-        last_slot_words = [keep([P, n], U32, "last_slot_words%d" % s0) for s0, n in LAST_GROUPS]
-        shared_slot_bytes = keep([P, SLOTS], U8, "shared_slot_bytes")
-        last_slot_bytes = keep([P, SLOTS], U8, "last_slot_bytes")
+        slot_words = [keep([P, SLOTS], U32, "slot_words%d" % a) for a in range(LAST)]
+        last_slot_words = [keep([P, (e1 - e0) * C], U32, "last_slot_words%d" % e0) for e0, e1 in GROUPS]
+        early_slot_bytes = keep([P, SLOTS], U8, "early_slot_bytes")
+        last_slot_bytes = [keep([P, (e1 - e0) * C], U8, "last_slot_bytes%d" % e0) for e0, e1 in GROUPS]
 
         def word_column(a):
-            return (LAST_PASS - a) * T
+            return (LAST - a) * T
 
         def quantise(a):
             grouped = {}
-
-            def views(t0, t1, on_vector):
-                if on_vector and a > 0:
-                    tag = "grouped%d_%d" % (a - 1, CASTS[a - 1][-1][0])
-                else:
-                    tag = None
+            for t0, t1, engine in ROUNDS[a]:
+                tag = "grouped%d_%d" % (a - 1, ROUNDS[a - 1][-1][0]) if engine == "v" and a > 0 else None
                 grouped[t0] = keep([P, (t1 - t0) * PACK], BF16, "grouped%d_%d" % (a, t0), tag)
-                i = max(i for i, (first, width) in enumerate(PIECES[a]) if first <= t0)
-                c0 = t0 - PIECES[a][i][0]
+                first = max(first for first, end in LOADS[a] if first <= t0)
                 dst = grouped[t0][:].rearrange("p (c i j) -> p c j i", i=RUN, j=PACK)
-                src = raw[a, i][:, :, c0 : c0 + t1 - t0].rearrange("p j (c i) -> p c j i", i=RUN)
-                return dst, src
-
-            for t0, t1, on_vector in CASTS[a]:
-                if on_vector:
-                    nc.vector.tensor_copy(*views(t0, t1, True))
+                src = raw[a, first][:, :, t0 - first : t1 - first].rearrange("p j (c i) -> p c j i", i=RUN)
+                if engine == "v":
+                    nc.vector.tensor_copy(dst, src)
                 else:
-                    nc.scalar.copy(*views(t0, t1, False))
-            for t0, t1, on_vector in CASTS[a]:
-                width = t1 - t0
-                if a == LAST_PASS:
-                    plane = last_bytes[:, t0 : t0 + width]
-                else:
-                    plane = shared_bytes[PLANE_ROWS * a :, t0 : t0 + width]
-                c0 = word_column(a) + t0
-                nc.vector.quantize_mx(
-                    out=words[:, c0 : c0 + width].bitcast(FP8X4),
-                    scales=plane,
-                    in_=grouped[t0][:],
-                )
+                    nc.scalar.copy(dst, src)
+            for t0, t1, engine in ROUNDS[a]:
+                plane = last_bytes[:, t0:t1] if a == LAST else early_bytes[PLANE_ROWS * a :, t0:t1]
+                c0 = word_column(a)
+                nc.vector.quantize_mx(out=words[:, c0 + t0 : c0 + t1].bitcast(FP8X4), scales=plane, in_=grouped[t0][:])
 
-        for a in range(LAST_PASS):
+        for a in range(LAST):
             quantise(a)
-            if a == LAST_PASS - 1:
-                nc.vector.tensor_copy(shared_slot_bytes[:], shared_bytes[:].indirect(offs_sb[:]))
+            if a == LAST - 1:
+                nc.vector.tensor_copy(early_slot_bytes[:], early_bytes[:].indirect(offs_sb[:]))
             window = words[:, word_column(a) : word_column(a) + WIDE]
             nc.vector.tensor_copy(slot_words[a][:], window.indirect(offs_sb[:]))
-        moved = keep([P, (LAST_PASS - 1) * SLOTS], U8, "moved")
-        shifted = {a: moved[:, (a - 1) * SLOTS : a * SLOTS] for a in range(1, LAST_PASS)}
-        w_early = keep([P, 2, E, 2 * N], U8, "w_early", "grouped2_%d" % CASTS[2][-1][0])
-        w_late = keep([P, 2, E, 2 * N], U8, "w_late", "shared_bytes")
+
+        word_rows = w_words.bitcast(I32)
+        moved = keep([P, (LAST - 1) * SLOTS], U8, "moved")
+        shifted = {a: moved[:, (a - 1) * SLOTS : a * SLOTS] for a in range(1, LAST)}
+        w_early = keep([P, 2, E, 2 * N], U8, "w_early", "grouped2_%d" % ROUNDS[2][-1][0])
+        w_late = keep([P, 2, E, 2 * N], U8, "w_late", "early_bytes")
         w_codes = [w_early[:, 0], w_early[:, 1], w_late[:, 0], w_late[:, 1]]
         for a in range(PASSES):
             if a - 1 in shifted:
+                first = PLANE_ROWS * (a - 1)
                 nc.sync.dma_start(
-                    out=shifted[a - 1][0:SHIFT_ROWS, :].bitcast(I32),
-                    in_=shared_slot_bytes[PLANE_ROWS * (a - 1) : PLANE_ROWS * (a - 1) + SHIFT_ROWS, :].bitcast(I32),
+                    out=shifted[a - 1][0:LIVE_ROWS, :].bitcast(I32),
+                    in_=early_slot_bytes[first : first + LIVE_ROWS, :].bitcast(I32),
                 )
-            nc.sync.dma_start(
-                out=w_codes[a].bitcast(I32), in_=word_rows[:, a].rearrange("e p n -> p e n")
-            )
+            nc.sync.dma_start(out=w_codes[a].bitcast(I32), in_=word_rows[:, a].rearrange("e p n -> p e n"))
 
-        quantise(LAST_PASS)
-        gates = keep([P, TOP, T], F32, "gates", "raw%d_0" % LAST_PASS)
-        gate_sb = [gates[:, r] for r in range(TOP)]
+        quantise(LAST)
+        gates = keep([P, TOP, T], F32, "gates", "raw%d_0" % LAST)
         for r in range(TOP):
-            nc.sync.dma_start(out=gate_sb[r], in_=gate[r, 0:P, :])
+            nc.sync.dma_start(out=gates[:, r], in_=gate[r, 0:P, :])
 
-        nc.vector.tensor_copy(last_slot_bytes[:], last_bytes[:].indirect(offs_sb[:]))
-        for g, (s0, n) in enumerate(LAST_GROUPS):
-            entries = offs_sb[:, s0 // PER_COLUMN : (s0 + n) // PER_COLUMN]
+        for g, (e0, e1) in enumerate(GROUPS):
+            entries = offs_sb[:, e0 * C // PER_COLUMN : e1 * C // PER_COLUMN]
+            nc.vector.tensor_copy(last_slot_bytes[g][:], last_bytes[:].indirect(entries))
             nc.vector.tensor_copy(last_slot_words[g][:], words[:, 0:T].indirect(entries))
 
-        def expert_pass(acc, h, e, a):
-            slots = slice(e * C, (e + 1) * C)
-            if a == LAST_PASS:
-                g = max(i for i, (s0, n) in enumerate(LAST_GROUPS) if s0 <= e * C)
-                c0 = e * C - LAST_GROUPS[g][0]
-                moving = last_slot_words[g][:, c0 : c0 + C]
-                slot_plane = last_slot_bytes[:, slots]
-            else:
-                moving = slot_words[a][:, slots]
-                slot_plane = (shared_slot_bytes if a == 0 else shifted[a])[:, slots]
-            nc.tensor.matmul_mx(
-                out=acc,
-                lhsT=w_codes[a][:, e, 2 * P * h : 2 * P * (h + 1)].bitcast(FP4X4),
-                lhsT_scale=w_plane[:, e * PASSES + a, P * h : P * (h + 1)],
-                rhs=moving.bitcast(FP8X4),
-                rhs_scale=slot_plane,
-                start=(a == 0),
-                stop=(a == LAST_PASS),
-            )
-
-        early = [(0, e) for e in range(E)] + [(1, e) for e in range(LATE)]
-        open_groups = [bank(C, "open%d" % b, b) for b in range(len(early))]
+        sums = {
+            (h, g): bank((e1 - e0) * C, "sums%d_%d" % (h, g), len(GROUPS) * h + g)
+            for h in range(HALVES)
+            for g, (e0, e1) in enumerate(GROUPS)
+        }
         for a in range(PASSES):
-            for b, (h, e) in enumerate(early):
-                expert_pass(open_groups[b][:], h, e, a)
-                if a == LAST_PASS:
-                    nc.scalar.copy(y[h][:, e * C : (e + 1) * C], open_groups[b][:])
-        for b, e0 in zip((0, E - 1), range(LATE, E, LATE)):
-            late = bank(LATE * C, "late%d" % b, b)
-            for i in range(LATE):
-                for a in range(PASSES):
-                    expert_pass(late[:, i * C : (i + 1) * C], 1, e0 + i, a)
-            nc.scalar.copy(y[1][:, e0 * C : (e0 + LATE) * C], late[:])
+            for g, (e0, e1) in enumerate(GROUPS):
+                for h in range(HALVES):
+                    for e in range(e0, e1):
+                        slots = slice(e * C, (e + 1) * C)
+                        local = slice((e - e0) * C, (e - e0 + 1) * C)
+                        if a == LAST:
+                            moving, plane = last_slot_words[g][:, local], last_slot_bytes[g][:, local]
+                        else:
+                            moving = slot_words[a][:, slots]
+                            plane = (early_slot_bytes if a == 0 else shifted[a])[:, slots]
+                        nc.tensor.matmul_mx(
+                            out=sums[h, g][:, local],
+                            lhsT=w_codes[a][:, e, 2 * P * h : 2 * P * (h + 1)].bitcast(FP4X4),
+                            lhsT_scale=w_plane[:, e * PASSES + a, P * h : P * (h + 1)],
+                            rhs=moving.bitcast(FP8X4),
+                            rhs_scale=plane,
+                            start=(a == 0 and e == e0),
+                            stop=(a == LAST and e == e1 - 1),
+                        )
+                    if a == LAST:
+                        if h == 0 and g == len(GROUPS) - 1:
+                            nc.vector.tensor_copy(y[h][:, e0 * C : e1 * C], sums[h, g][:])
+                        else:
+                            nc.scalar.copy(y[h][:, e0 * C : e1 * C], sums[h, g][:])
 
-        unread = bank(BANK, "unread", E - 1)
-        for a in range(WARM_UPS):
-            nc.tensor.matmul_mx(
-                out=unread[:],
-                lhsT=w_codes[0][:, 0, 0 : 2 * P].bitcast(FP4X4),
-                lhsT_scale=w_plane[:, 0, 0:P],
-                rhs=slot_words[0][:, 0:BANK].bitcast(FP8X4),
-                rhs_scale=shared_slot_bytes[:, 0:BANK],
-                start=True,
-                stop=True,
-            )
+        plain = {(h, r): keep([P, T], F32, "plain%d_%d" % (h, r)) for h, r in ((0, 2), (0, 1), (1, 2))}
+        places = {(1, 0): "plain1_2"}
+        term = {(h, r): keep([P, T], F32, "term%d_%d" % (h, r), places.get((h, r))) for h in range(HALVES) for r in range(TOP)}
 
-        term = {(h, r): keep([P, T], F32, "term%d_%d" % (h, r)) for h in range(HALVES) for r in range(TOP)}
+        def entries_of(r, t0, t1):
+            return pos_sb[r][:, t0 // PER_COLUMN : t1 // PER_COLUMN]
+
+        def weigh(h, r, t0=0, t1=T):
+            nc.vector.tensor_tensor(term[h, r][:, t0:t1], y[h][:].indirect(entries_of(r, t0, t1)), gates[:, r, t0:t1], MULT)
+
+        def fetch(h, r):
+            nc.scalar.activation(plain[h, r][:], y[h][:].indirect(pos_sb[r][:]), COPY)
+
+        def scale(h, r, t0=0, t1=T):
+            nc.vector.tensor_tensor(term[h, r][:, t0:t1], plain[h, r][:, t0:t1], gates[:, r, t0:t1], MULT)
+
+        turned = {(h, t0): bank(t1 - t0, "turned%d_%d" % (h, t0), number)
+                  for h, numbers in ((0, (6, 7)), (1, (0, 1))) for (t0, t1), number in zip(PARTS, numbers)}
+        back = {(h, t0): bank(t1 - t0, "back%d_%d" % (h, t0), number)
+                for h, numbers in ((0, (2, 3)), (1, (4, 5))) for (t0, t1), number in zip(PARTS, numbers)}
+        staged = [keep([P, T], F32, "staged%d" % h) for h in range(HALVES)]
         total = [keep([P, T], F32, "total%d" % h) for h in range(HALVES)]
 
-        def weigh(h, r, t0, t1):
-            picked = y[h][:].indirect(pos_sb[r][:, t0 // PER_COLUMN : t1 // PER_COLUMN])
-            nc.vector.tensor_tensor(term[h, r][:, t0:t1], picked, gate_sb[r][:, t0:t1], MULT)
+        def turn(h, r, first, last):
+            for t0, t1 in PARTS:
+                for c in range(t0, t1, P):
+                    nc.tensor.matmul(
+                        turned[h, t0][:, c - t0 : c - t0 + P],
+                        lhsT=term[h, r][:, c : c + P],
+                        rhs=ident[:],
+                        start=(first and c == t0),
+                        stop=(last and c == t1 - P),
+                        is_transpose=True,
+                    )
 
-        blocks = T // P
+        def turn_back(h):
+            for t0, t1 in PARTS:
+                nc.scalar.copy(staged[h][:, t0:t1], turned[h, t0][:])
+                for c in range(t0, t1, P):
+                    nc.tensor.transpose(back[h, t0][:, c - t0 : c - t0 + P], staged[h][:, c : c + P], ident[:])
 
-        def turn(banks, h, r, b, start, stop):
-            nc.tensor.matmul(
-                banks[b][:],
-                lhsT=term[h, r][:, b * P : (b + 1) * P],
-                rhs=ident[:],
-                start=start,
-                stop=stop,
-                is_transpose=True,
-            )
-
-        def turn_back(banks, staged, back, b):
-            nc.scalar.copy(staged[:, b * P : (b + 1) * P], banks[b][:])
-            part, c0 = divmod(b * P, SPLIT)
-            nc.tensor.transpose(back[part][:, c0 : c0 + P], staged[:, b * P : (b + 1) * P], ident[:])
-
-        turned = [bank(P, "turned%d" % b, number) for b, number in enumerate(TURN_BANKS)]
-        for r in range(TOP):
-            weigh(0, r, 0, T)
-            for b in range(blocks):
-                turn(turned, 0, r, b, r == 0, r == TOP - 1)
-        staged = keep([P, T], F32, "staged0")
-        back = [bank(SPLIT, "back0", 7), bank(T - SPLIT, "back1", 0)]
-        for b in range(blocks):
-            turn_back(turned, staged, back, b)
-        nc.scalar.copy(total[0][:, :SPLIT], back[0][:])
-        nc.sync.dma_start(out=out[0:P, :SPLIT], in_=total[0][:, :SPLIT])
-
-        turned = [bank(P, "turned_late%d" % b, number) for b, number in enumerate(TURN_BANKS)]
-        staged = keep([P, T], F32, "staged1")
-        pair = [bank(SPLIT, "pair0", 5), bank(T - SPLIT, "pair1", 7)]
-        weigh(1, 2, 0, T)
-        for b in range(blocks):
-            turn(turned, 1, 2, b, True, False)
-        for t0, t1 in ((0, SPLIT), (SPLIT, T)):
-            weigh(1, 1, t0, t1)
-            for b in range(t0 // P, t1 // P):
-                turn(turned, 1, 1, b, False, True)
-            for b in range(t0 // P, t1 // P):
-                turn_back(turned, staged, pair, b)
-        nc.scalar.copy(total[0][:, SPLIT:], back[1][:])
-        nc.sync.dma_start(out=out[0:P, SPLIT:], in_=total[0][:, SPLIT:])
-        weigh(1, 0, 0, SPLIT)
-        weigh(1, 0, SPLIT, T)
-        for part, (t0, t1, queue) in enumerate(((0, SPLIT, nc.sync), (SPLIT, T, nc.scalar))):
-            nc.vector.tensor_tensor(total[1][:, t0:t1], pair[part][:], term[1, 0][:, t0:t1], ADD)
+        fetch(0, 2)
+        fetch(0, 1)
+        fetch(1, 2)
+        weigh(0, 0)
+        turn(0, 0, True, False)
+        scale(0, 2)
+        turn(0, 2, False, False)
+        weigh(1, 1)
+        turn(1, 1, True, False)
+        scale(0, 1)
+        turn(0, 1, False, True)
+        scale(1, 2)
+        turn(1, 2, False, True)
+        turn_back(0)
+        turn_back(1)
+        for t0, t1 in PARTS:
+            nc.scalar.copy(total[0][:, t0:t1], back[0, t0][:])
+            nc.sync.dma_start(out=out[0:P, t0:t1], in_=total[0][:, t0:t1])
+        for t0, t1 in PARTS:
+            weigh(1, 0, t0, t1)
+        for (t0, t1), queue in zip(PARTS, (nc.sync, nc.scalar)):
+            nc.vector.tensor_tensor(total[1][:, t0:t1], back[1, t0][:], term[1, 0][:, t0:t1], ADD)
             queue.dma_start(out=out[P:N, t0:t1], in_=total[1][:, t0:t1])

@@ -19,7 +19,6 @@ FP8X4 = mybir.dt.float8_e4m3fn_x4
 FP4X4 = mybir.dt.float4_e2m1fn_x4
 MULT = mybir.AluOpType.mult
 ADD = mybir.AluOpType.add
-COPY = mybir.ActivationFunctionType.Copy
 
 P = 128
 PACK = 4
@@ -31,16 +30,19 @@ QUADRANT = 32
 PLANE_ROWS = 4
 PER_COLUMN = 16
 RUN = 4
+BANK = 512
 WIDE = 1024
 LIVE_ROWS = 3 * QUADRANT + PLANE_ROWS
 
-LOADS = (((0, 384), (384, 640)), ((0, 640),), ((0, 640),), ((0, 640),))
 ROUNDS = (
-    ((0, 256, "v"), (256, 384, "s"), (384, 512, "v"), (512, 640, "s")),
-    ((256, 512, "v"), (0, 256, "s"), (512, 640, "s")),
-    ((0, 256, "s"), (256, 512, "v"), (512, 640, "s")),
-    ((0, 256, "s"), (256, 512, "s"), (512, 640, "s")),
+    ((0, 256, "v"), (256, 384, "s"), (384, 512, "g"), (512, 640, "s")),
+    ((0, 256, "s"), (256, 512, "g"), (512, 640, "s")),
+    ((0, 256, "s"), (256, 512, "g"), (512, 640, "s")),
+    ((0, 384, "s"), (384, 640, "g")),
 )
+BLOCKS = T // P
+SCALE_LOADS = 2
+WHOLE = 2
 GROUPS = ((0, 3), (3, 5), (5, 6))
 PARTS = ((0, 384), (384, 640))
 
@@ -66,37 +68,37 @@ def tile_moe_ecr_lin_none_kernel(
         words = keep([P, LAST * T + WIDE], U32, "words")
         y = [keep([P, SLOTS + PAD], F32, "y%d" % h) for h in range(HALVES)]
 
-        nc.gpsimd.memset(y[1][:, SLOTS:], 0.0)
+        gate_rows = keep([P, TOP, P], F32, "gate_rows")
+        nc.gpsimd.memset(gate_rows[:], 0.0)
+        nc.vector.memset(y[1][:, SLOTS:], 0.0)
         nc.scalar.copy(y[0][:, SLOTS:], y[1][:, SLOTS:])
         nc.vector.memset(early_bytes[:].bitcast(I32), 0)
-        nc.gpsimd.memset(last_bytes[:].bitcast(I32), 0)
-        nc.gpsimd.memset(words[:, PASSES * T :].bitcast(I32), 0)
+        nc.vector.memset(last_bytes[:].bitcast(I32), 0)
+        nc.vector.memset(words[:, PASSES * T :].bitcast(I32), 0)
         ident = keep([P, P], F32, "ident")
         make_identity(nc, ident[:])
 
-        raw = {}
+        raw = [keep([P, PACK, T], F32, "raw%d" % a) for a in range(PASSES)]
         for a in range(PASSES):
             rows = xT[a * K_PASS : (a + 1) * K_PASS, :].rearrange("(p j) t -> p j t", j=PACK)
-            for t0, t1 in LOADS[a]:
-                raw[a, t0] = keep([P, PACK, t1 - t0], F32, "raw%d_%d" % (a, t0))
-                nc.sync.dma_start(out=raw[a, t0][:], in_=rows[:, :, t0:t1])
+            nc.sync.dma_start(out=raw[a][:], in_=rows)
             if a == 0:
                 nc.sync.dma_start(offs_sb[:], offs)
+                nc.sync.dma_start(out=gate_rows[0:BLOCKS], in_=gate[:, 0, :].rearrange("r (b i) -> b r i", i=P))
 
         scale_rows = w_scales.bitcast(I32).rearrange("e a q n -> q (e a) n")
         w_plane = keep([P, E * PASSES, N], U8, "w_plane")
-        for r in range(PLANE_ROWS):
-            nc.sync.dma_start(
-                out=w_plane[r:P:QUADRANT].bitcast(I32),
-                in_=scale_rows[r : PLANE_ROWS * P // QUADRANT : PLANE_ROWS],
-            )
-        for tile, entries in zip(pos_sb, (pos1, pos2, pos3)):
-            nc.sync.dma_start(tile[:], entries)
-
+        share = E * PASSES // SCALE_LOADS
+        for i in range(SCALE_LOADS):
+            for r in range(PLANE_ROWS):
+                nc.sync.dma_start(
+                    out=w_plane[r:P:QUADRANT, i * share : (i + 1) * share].bitcast(I32),
+                    in_=scale_rows[r : PLANE_ROWS * P // QUADRANT : PLANE_ROWS, i * share : (i + 1) * share],
+                )
         slot_words = [keep([P, SLOTS], U32, "slot_words%d" % a) for a in range(LAST)]
         last_slot_words = [keep([P, (e1 - e0) * C], U32, "last_slot_words%d" % e0) for e0, e1 in GROUPS]
         early_slot_bytes = keep([P, SLOTS], U8, "early_slot_bytes")
-        last_slot_bytes = [keep([P, (e1 - e0) * C], U8, "last_slot_bytes%d" % e0) for e0, e1 in GROUPS]
+        last_slot_bytes = keep([P, SLOTS], U8, "last_slot_bytes")
 
         def word_column(a):
             return (LAST - a) * T
@@ -104,11 +106,13 @@ def tile_moe_ecr_lin_none_kernel(
         def quantise(a):
             grouped = {}
             for t0, t1, engine in ROUNDS[a]:
-                tag = "grouped%d_%d" % (a - 1, ROUNDS[a - 1][-1][0]) if engine == "v" and a > 0 else None
-                grouped[t0] = keep([P, (t1 - t0) * PACK], BF16, "grouped%d_%d" % (a, t0), tag)
-                first = max(first for first, end in LOADS[a] if first <= t0)
+                grouped[t0] = keep([P, (t1 - t0) * PACK], BF16, "grouped%d_%d" % (a, t0))
+                if engine == "g":
+                    dst = grouped[t0][:].rearrange("p (t j) -> p t j", j=PACK)
+                    nc.gpsimd.tensor_copy(dst, raw[a][:, :, t0:t1].rearrange("p j t -> p t j"))
+                    continue
                 dst = grouped[t0][:].rearrange("p (c i j) -> p c j i", i=RUN, j=PACK)
-                src = raw[a, first][:, :, t0 - first : t1 - first].rearrange("p j (c i) -> p c j i", i=RUN)
+                src = raw[a][:, :, t0:t1].rearrange("p j (c i) -> p c j i", i=RUN)
                 if engine == "v":
                     nc.vector.tensor_copy(dst, src)
                 else:
@@ -125,65 +129,77 @@ def tile_moe_ecr_lin_none_kernel(
             window = words[:, word_column(a) : word_column(a) + WIDE]
             nc.vector.tensor_copy(slot_words[a][:], window.indirect(offs_sb[:]))
 
-        word_rows = w_words.bitcast(I32)
+        turned_rows = bank(TOP * P, "turned_rows", 0)
+        for r in range(TOP):
+            nc.tensor.transpose(turned_rows[:, r * P : (r + 1) * P], gate_rows[:, r], ident[:])
+        gate_columns = keep([P, TOP, BLOCKS], F32, "gate_columns", "raw0")
+        nc.scalar.copy(gate_columns[:], turned_rows[:].rearrange("p (r i) -> p r i", i=P)[:, :, 0:BLOCKS])
+        spread = [bank(min(BANK, TOP * T - c), "spread%d" % c, 4 + c // BANK) for c in range(0, TOP * T, BANK)]
+        for m in range(TOP * BLOCKS):
+            b, c = divmod(m * P, BANK)
+            column = gate_columns[:].rearrange("p r b -> p (r b)")[:, m : m + 1]
+            nc.tensor.transpose(spread[b][:, c : c + P], column.to_broadcast([P, P]), ident[:])
+
+        quantise(LAST)
         moved = keep([P, (LAST - 1) * SLOTS], U8, "moved")
         shifted = {a: moved[:, (a - 1) * SLOTS : a * SLOTS] for a in range(1, LAST)}
-        w_early = keep([P, 2, E, 2 * N], U8, "w_early", "grouped2_%d" % ROUNDS[2][-1][0])
-        w_late = keep([P, 2, E, 2 * N], U8, "w_late", "early_bytes")
-        w_codes = [w_early[:, 0], w_early[:, 1], w_late[:, 0], w_late[:, 1]]
-        for a in range(PASSES):
-            if a - 1 in shifted:
+        word_rows = w_words.bitcast(I32)
+        w_whole = keep([P, WHOLE, E, 2 * N], U8, "w_whole")
+        w_codes = {(h, a): w_whole[:, a, :, 2 * P * h : 2 * P * (h + 1)] for h in range(HALVES) for a in range(WHOLE)}
+        for a in range(WHOLE):
+            nc.sync.dma_start(out=w_whole[:, a].bitcast(I32), in_=word_rows[:, a].rearrange("e p n -> p e n"))
+        order = [(h, a) for h in range(HALVES) for a in range(WHOLE, PASSES)]
+        w_halves = keep([P, len(order), E, 2 * P], U8, "w_halves", "early_bytes")
+        for i, (h, a) in enumerate(order):
+            if h == 0:
                 first = PLANE_ROWS * (a - 1)
                 nc.sync.dma_start(
                     out=shifted[a - 1][0:LIVE_ROWS, :].bitcast(I32),
                     in_=early_slot_bytes[first : first + LIVE_ROWS, :].bitcast(I32),
                 )
-            nc.sync.dma_start(out=w_codes[a].bitcast(I32), in_=word_rows[:, a].rearrange("e p n -> p e n"))
+            w_codes[h, a] = w_halves[:, i]
+            columns = word_rows[:, a, :, h * P // 2 : (h + 1) * P // 2]
+            nc.sync.dma_start(out=w_codes[h, a].bitcast(I32), in_=columns.rearrange("e p n -> p e n"))
+        for tile, entries in zip(pos_sb, (pos1, pos2, pos3)):
+            nc.sync.dma_start(tile[:], entries)
+        gates = keep([P, TOP, T], F32, "gates", "raw%d" % LAST)
+        flat_gates = gates[:].rearrange("p r t -> p (r t)")
+        for b, c in enumerate(range(0, TOP * T, BANK)):
+            nc.scalar.copy(flat_gates[:, c : min(c + BANK, TOP * T)], spread[b][:])
 
-        quantise(LAST)
-        gates = keep([P, TOP, T], F32, "gates", "raw%d_0" % LAST)
-        for r in range(TOP):
-            nc.sync.dma_start(out=gates[:, r], in_=gate[r, 0:P, :])
-
+        nc.vector.tensor_copy(last_slot_bytes[:], last_bytes[:].indirect(offs_sb[:]))
         for g, (e0, e1) in enumerate(GROUPS):
             entries = offs_sb[:, e0 * C // PER_COLUMN : e1 * C // PER_COLUMN]
-            nc.vector.tensor_copy(last_slot_bytes[g][:], last_bytes[:].indirect(entries))
             nc.vector.tensor_copy(last_slot_words[g][:], words[:, 0:T].indirect(entries))
 
         sums = {
-            (h, g): bank((e1 - e0) * C, "sums%d_%d" % (h, g), len(GROUPS) * h + g)
+            (h, g): bank((e1 - e0) * C, "sums%d_%d" % (h, g), 1 + len(GROUPS) * h + g)
             for h in range(HALVES)
             for g, (e0, e1) in enumerate(GROUPS)
         }
-        for a in range(PASSES):
+        for h, a in [(h, a) for a in range(WHOLE) for h in range(HALVES)] + order:
             for g, (e0, e1) in enumerate(GROUPS):
-                for h in range(HALVES):
-                    for e in range(e0, e1):
-                        slots = slice(e * C, (e + 1) * C)
-                        local = slice((e - e0) * C, (e - e0 + 1) * C)
-                        if a == LAST:
-                            moving, plane = last_slot_words[g][:, local], last_slot_bytes[g][:, local]
-                        else:
-                            moving = slot_words[a][:, slots]
-                            plane = (early_slot_bytes if a == 0 else shifted[a])[:, slots]
-                        nc.tensor.matmul_mx(
-                            out=sums[h, g][:, local],
-                            lhsT=w_codes[a][:, e, 2 * P * h : 2 * P * (h + 1)].bitcast(FP4X4),
-                            lhsT_scale=w_plane[:, e * PASSES + a, P * h : P * (h + 1)],
-                            rhs=moving.bitcast(FP8X4),
-                            rhs_scale=plane,
-                            start=(a == 0 and e == e0),
-                            stop=(a == LAST and e == e1 - 1),
-                        )
+                for e in range(e0, e1):
+                    slots = slice(e * C, (e + 1) * C)
+                    local = slice((e - e0) * C, (e - e0 + 1) * C)
                     if a == LAST:
-                        if h == 0 and g == len(GROUPS) - 1:
-                            nc.vector.tensor_copy(y[h][:, e0 * C : e1 * C], sums[h, g][:])
-                        else:
-                            nc.scalar.copy(y[h][:, e0 * C : e1 * C], sums[h, g][:])
+                        moving, plane = last_slot_words[g][:, local], last_slot_bytes[:, slots]
+                    else:
+                        moving = slot_words[a][:, slots]
+                        plane = (early_slot_bytes if a == 0 else shifted[a])[:, slots]
+                    nc.tensor.matmul_mx(
+                        out=sums[h, g][:, local],
+                        lhsT=w_codes[h, a][:, e].bitcast(FP4X4),
+                        lhsT_scale=w_plane[:, e * PASSES + a, P * h : P * (h + 1)],
+                        rhs=moving.bitcast(FP8X4),
+                        rhs_scale=plane,
+                        start=(a == 0 and e == e0),
+                        stop=(a == LAST and e == e1 - 1),
+                    )
+                if a == LAST:
+                    nc.scalar.copy(y[h][:, e0 * C : e1 * C], sums[h, g][:])
 
-        plain = {(h, r): keep([P, T], F32, "plain%d_%d" % (h, r)) for h, r in ((0, 2), (0, 1), (1, 2))}
-        places = {(1, 0): "plain1_2"}
-        term = {(h, r): keep([P, T], F32, "term%d_%d" % (h, r), places.get((h, r))) for h in range(HALVES) for r in range(TOP)}
+        term = {(h, r): keep([P, T], F32, "term%d_%d" % (h, r)) for h in range(HALVES) for r in range(TOP)}
 
         def entries_of(r, t0, t1):
             return pos_sb[r][:, t0 // PER_COLUMN : t1 // PER_COLUMN]
@@ -191,22 +207,17 @@ def tile_moe_ecr_lin_none_kernel(
         def weigh(h, r, t0=0, t1=T):
             nc.vector.tensor_tensor(term[h, r][:, t0:t1], y[h][:].indirect(entries_of(r, t0, t1)), gates[:, r, t0:t1], MULT)
 
-        def fetch(h, r):
-            nc.scalar.activation(plain[h, r][:], y[h][:].indirect(pos_sb[r][:]), COPY)
-
-        def scale(h, r, t0=0, t1=T):
-            nc.vector.tensor_tensor(term[h, r][:, t0:t1], plain[h, r][:, t0:t1], gates[:, r, t0:t1], MULT)
-
+        pieces = {h: tuple((c, c + P) for c in range(0, T, P)) for h in range(HALVES)}
         turned = {(h, t0): bank(t1 - t0, "turned%d_%d" % (h, t0), number)
-                  for h, numbers in ((0, (6, 7)), (1, (0, 1))) for (t0, t1), number in zip(PARTS, numbers)}
+                  for h, numbers in ((0, (4, 5, 6, 7, 3)), (1, (4, 5, 6, 7, 3))) for (t0, t1), number in zip(pieces[h], numbers)}
         back = {(h, t0): bank(t1 - t0, "back%d_%d" % (h, t0), number)
-                for h, numbers in ((0, (2, 3)), (1, (4, 5))) for (t0, t1), number in zip(PARTS, numbers)}
+                for h, numbers in ((0, (0, 1)), (1, (2, 0))) for (t0, t1), number in zip(PARTS, numbers)}
         staged = [keep([P, T], F32, "staged%d" % h) for h in range(HALVES)]
         total = [keep([P, T], F32, "total%d" % h) for h in range(HALVES)]
 
-        def turn(h, r, first, last):
-            for t0, t1 in PARTS:
-                for c in range(t0, t1, P):
+        def turn(h, r, first, last, start=0, end=T):
+            for t0, t1 in pieces[h]:
+                for c in range(max(t0, start), min(t1, end), P):
                     nc.tensor.matmul(
                         turned[h, t0][:, c - t0 : c - t0 + P],
                         lhsT=term[h, r][:, c : c + P],
@@ -216,30 +227,27 @@ def tile_moe_ecr_lin_none_kernel(
                         is_transpose=True,
                     )
 
-        def turn_back(h):
-            for t0, t1 in PARTS:
-                nc.scalar.copy(staged[h][:, t0:t1], turned[h, t0][:])
-                for c in range(t0, t1, P):
-                    nc.tensor.transpose(back[h, t0][:, c - t0 : c - t0 + P], staged[h][:, c : c + P], ident[:])
+        def turn_back(h, start=0, end=T):
+            for t0, t1 in pieces[h]:
+                if start <= t0 < end:
+                    nc.scalar.copy(staged[h][:, t0:t1], turned[h, t0][:])
+                    for c in range(t0, t1, P):
+                        first = max(first for first, last in PARTS if first <= c)
+                        nc.tensor.transpose(back[h, first][:, c - first : c - first + P], staged[h][:, c : c + P], ident[:])
 
-        fetch(0, 2)
-        fetch(0, 1)
-        fetch(1, 2)
-        weigh(0, 0)
-        turn(0, 0, True, False)
-        scale(0, 2)
-        turn(0, 2, False, False)
-        weigh(1, 1)
-        turn(1, 1, True, False)
-        scale(0, 1)
-        turn(0, 1, False, True)
-        scale(1, 2)
-        turn(1, 2, False, True)
+        for r in range(TOP):
+            weigh(0, r)
+            turn(0, r, r == 0, r == TOP - 1)
         turn_back(0)
-        turn_back(1)
         for t0, t1 in PARTS:
             nc.scalar.copy(total[0][:, t0:t1], back[0, t0][:])
             nc.sync.dma_start(out=out[0:P, t0:t1], in_=total[0][:, t0:t1])
+        weigh(1, 2)
+        turn(1, 2, True, False)
+        for t0, t1 in PARTS:
+            weigh(1, 1, t0, t1)
+            turn(1, 1, False, True, t0, t1)
+            turn_back(1, t0, t1)
         for t0, t1 in PARTS:
             weigh(1, 0, t0, t1)
         for (t0, t1), queue in zip(PARTS, (nc.sync, nc.scalar)):

@@ -19,6 +19,7 @@ FP8X4 = mybir.dt.float8_e4m3fn_x4
 FP4X4 = mybir.dt.float4_e2m1fn_x4
 MULT = mybir.AluOpType.mult
 ADD = mybir.AluOpType.add
+COPY = mybir.ActivationFunctionType.Copy
 
 P = 128
 PACK = 4
@@ -200,56 +201,50 @@ def tile_moe_ecr_lin_none_kernel(
                     nc.scalar.copy(y[h][:, e0 * C : e1 * C], sums[h, g][:])
 
         term = {(h, r): keep([P, T], F32, "term%d_%d" % (h, r)) for h in range(HALVES) for r in range(TOP)}
+        plain = {(h, r): keep([P, T], F32, "plain%d_%d" % (h, r)) for h, r in ((0, 0), (1, 0), (1, 1))}
 
-        def entries_of(r, t0, t1):
-            return pos_sb[r][:, t0 // PER_COLUMN : t1 // PER_COLUMN]
+        def weigh(h, r):
+            nc.vector.tensor_tensor(term[h, r][:], y[h][:].indirect(pos_sb[r][:]), gates[:, r], MULT)
 
-        def weigh(h, r, t0=0, t1=T):
-            nc.vector.tensor_tensor(term[h, r][:, t0:t1], y[h][:].indirect(entries_of(r, t0, t1)), gates[:, r, t0:t1], MULT)
+        def fetch(h, r):
+            nc.scalar.activation(plain[h, r][:], y[h][:].indirect(pos_sb[r][:]), COPY)
 
-        pieces = {h: tuple((c, c + P) for c in range(0, T, P)) for h in range(HALVES)}
-        turned = {(h, t0): bank(t1 - t0, "turned%d_%d" % (h, t0), number)
-                  for h, numbers in ((0, (4, 5, 6, 7, 3)), (1, (4, 5, 6, 7, 3))) for (t0, t1), number in zip(pieces[h], numbers)}
-        back = {(h, t0): bank(t1 - t0, "back%d_%d" % (h, t0), number)
-                for h, numbers in ((0, (0, 1)), (1, (2, 0))) for (t0, t1), number in zip(PARTS, numbers)}
-        staged = [keep([P, T], F32, "staged%d" % h) for h in range(HALVES)]
+        def scale(h, r, t0=0, t1=T):
+            nc.vector.tensor_tensor(term[h, r][:, t0:t1], plain[h, r][:, t0:t1], gates[:, r, t0:t1], MULT)
+
+        turned = [bank(P, "turned%d" % b, number) for b, number in enumerate((4, 5, 6, 7, 3))]
+        back = {t0: bank(t1 - t0, "back%d" % t0, number) for (t0, t1), number in zip(PARTS, (0, 1))}
+        staged = keep([P, T], F32, "staged")
+        pair = keep([P, T], F32, "pair")
         total = [keep([P, T], F32, "total%d" % h) for h in range(HALVES)]
 
-        def turn(h, r, first, last, start=0, end=T):
-            for t0, t1 in pieces[h]:
-                for c in range(max(t0, start), min(t1, end), P):
-                    nc.tensor.matmul(
-                        turned[h, t0][:, c - t0 : c - t0 + P],
-                        lhsT=term[h, r][:, c : c + P],
-                        rhs=ident[:],
-                        start=(first and c == t0),
-                        stop=(last and c == t1 - P),
-                        is_transpose=True,
-                    )
+        def turn(r, first, last):
+            for b in range(BLOCKS):
+                nc.tensor.matmul(
+                    turned[b][:], lhsT=term[0, r][:, b * P : (b + 1) * P], rhs=ident[:], start=first, stop=last, is_transpose=True
+                )
 
-        def turn_back(h, start=0, end=T):
-            for t0, t1 in pieces[h]:
-                if start <= t0 < end:
-                    nc.scalar.copy(staged[h][:, t0:t1], turned[h, t0][:])
-                    for c in range(t0, t1, P):
-                        first = max(first for first, last in PARTS if first <= c)
-                        nc.tensor.transpose(back[h, first][:, c - first : c - first + P], staged[h][:, c : c + P], ident[:])
-
-        for r in range(TOP):
-            weigh(0, r)
-            turn(0, r, r == 0, r == TOP - 1)
-        turn_back(0)
+        fetch(0, 0)
+        fetch(1, 0)
+        fetch(1, 1)
+        weigh(0, 2)
+        turn(2, True, False)
+        weigh(0, 1)
+        turn(1, False, False)
+        scale(0, 0)
+        turn(0, False, True)
         for t0, t1 in PARTS:
-            nc.scalar.copy(total[0][:, t0:t1], back[0, t0][:])
+            for c in range(t0, t1, P):
+                nc.scalar.copy(staged[:, c : c + P], turned[c // P][:])
+                nc.tensor.transpose(back[t0][:, c - t0 : c - t0 + P], staged[:, c : c + P], ident[:])
+        for t0, t1 in PARTS:
+            nc.scalar.copy(total[0][:, t0:t1], back[t0][:])
             nc.sync.dma_start(out=out[0:P, t0:t1], in_=total[0][:, t0:t1])
         weigh(1, 2)
-        turn(1, 2, True, False)
-        for t0, t1 in PARTS:
-            weigh(1, 1, t0, t1)
-            turn(1, 1, False, True, t0, t1)
-            turn_back(1, t0, t1)
-        for t0, t1 in PARTS:
-            weigh(1, 0, t0, t1)
+        scale(1, 0)
+        scale(1, 1, *PARTS[0])
+        nc.vector.tensor_tensor(pair[:], term[1, 2][:], term[1, 0][:], ADD)
+        scale(1, 1, *PARTS[1])
         for (t0, t1), queue in zip(PARTS, (nc.sync, nc.scalar)):
-            nc.vector.tensor_tensor(total[1][:, t0:t1], back[1, t0][:], term[1, 0][:, t0:t1], ADD)
+            nc.vector.tensor_tensor(total[1][:, t0:t1], pair[:, t0:t1], term[1, 1][:, t0:t1], ADD)
             queue.dma_start(out=out[P:N, t0:t1], in_=total[1][:, t0:t1])

@@ -43,7 +43,7 @@ ROUNDS = (
 )
 BLOCKS = T // P
 SCALE_LOADS = 2
-WHOLE = 2
+WHOLE = 3
 GROUPS = ((0, 3), (3, 5), (5, 6))
 PARTS = ((0, 384), (384, 640))
 
@@ -145,20 +145,25 @@ def tile_moe_ecr_lin_none_kernel(
         moved = keep([P, (LAST - 1) * SLOTS], U8, "moved")
         shifted = {a: moved[:, (a - 1) * SLOTS : a * SLOTS] for a in range(1, LAST)}
         word_rows = w_words.bitcast(I32)
-        w_whole = keep([P, WHOLE, E, 2 * N], U8, "w_whole")
-        w_codes = {(h, a): w_whole[:, a, :, 2 * P * h : 2 * P * (h + 1)] for h in range(HALVES) for a in range(WHOLE)}
+        w_first = keep([P, 2, E, 2 * N], U8, "w_first")
+        w_rest = keep([P, 2, E * 2 * N], U8, "w_rest", "early_bytes")
+        whole = [w_first[:, 0], w_first[:, 1], w_rest[:, 0].rearrange("p (e n) -> p e n", e=E)]
+        w_codes = {(h, a): whole[a][:, :, 2 * P * h : 2 * P * (h + 1)] for h in range(HALVES) for a in range(WHOLE)}
+        order = [(h, LAST) for h in range(HALVES)]
+
+        def shift(a):
+            nc.sync.dma_start(
+                out=shifted[a][0:LIVE_ROWS, :].bitcast(I32),
+                in_=early_slot_bytes[PLANE_ROWS * a : PLANE_ROWS * a + LIVE_ROWS, :].bitcast(I32),
+            )
+
         for a in range(WHOLE):
-            nc.sync.dma_start(out=w_whole[:, a].bitcast(I32), in_=word_rows[:, a].rearrange("e p n -> p e n"))
-        order = [(h, a) for h in range(HALVES) for a in range(WHOLE, PASSES)]
-        w_halves = keep([P, len(order), E, 2 * P], U8, "w_halves", "early_bytes")
-        for i, (h, a) in enumerate(order):
-            if h == 0:
-                first = PLANE_ROWS * (a - 1)
-                nc.sync.dma_start(
-                    out=shifted[a - 1][0:LIVE_ROWS, :].bitcast(I32),
-                    in_=early_slot_bytes[first : first + LIVE_ROWS, :].bitcast(I32),
-                )
-            w_codes[h, a] = w_halves[:, i]
+            if a - 1 in shifted:
+                shift(a - 1)
+            nc.sync.dma_start(out=whole[a].bitcast(I32), in_=word_rows[:, a].rearrange("e p n -> p e n"))
+        shift(LAST - 1)
+        for h, a in order:
+            w_codes[h, a] = w_rest[:, 1].rearrange("p (h e n) -> p h e n", h=HALVES, e=E)[:, h]
             columns = word_rows[:, a, :, h * P // 2 : (h + 1) * P // 2]
             nc.sync.dma_start(out=w_codes[h, a].bitcast(I32), in_=columns.rearrange("e p n -> p e n"))
         for tile, entries in zip(pos_sb, (pos1, pos2, pos3)):
@@ -212,8 +217,8 @@ def tile_moe_ecr_lin_none_kernel(
         def scale(h, r, t0=0, t1=T):
             nc.vector.tensor_tensor(term[h, r][:, t0:t1], plain[h, r][:, t0:t1], gates[:, r, t0:t1], MULT)
 
-        turned = [bank(P, "turned%d" % b, number) for b, number in enumerate((4, 5, 6, 7, 3))]
-        back = {t0: bank(t1 - t0, "back%d" % t0, number) for (t0, t1), number in zip(PARTS, (0, 1))}
+        turned = [bank(P, "turned%d" % b, number) for b, number in enumerate((0, 7, 1, 2, 3))]
+        back = {t0: bank(t1 - t0, "back%d" % t0, number) for (t0, t1), number in zip(PARTS, (4, 5))}
         staged = keep([P, T], F32, "staged")
         pair = keep([P, T], F32, "pair")
         total = [keep([P, T], F32, "total%d" % h) for h in range(HALVES)]
@@ -225,8 +230,8 @@ def tile_moe_ecr_lin_none_kernel(
                 )
 
         fetch(0, 0)
-        fetch(1, 0)
         fetch(1, 1)
+        fetch(1, 0)
         weigh(0, 2)
         turn(2, True, False)
         weigh(0, 1)
@@ -241,10 +246,12 @@ def tile_moe_ecr_lin_none_kernel(
             nc.scalar.copy(total[0][:, t0:t1], back[t0][:])
             nc.sync.dma_start(out=out[0:P, t0:t1], in_=total[0][:, t0:t1])
         weigh(1, 2)
-        scale(1, 0)
-        scale(1, 1, *PARTS[0])
-        nc.vector.tensor_tensor(pair[:], term[1, 2][:], term[1, 0][:], ADD)
-        scale(1, 1, *PARTS[1])
+        for t0, t1 in PARTS:
+            scale(1, 1, t0, t1)
+        for t0, t1 in PARTS:
+            nc.vector.tensor_tensor(pair[:, t0:t1], term[1, 2][:, t0:t1], term[1, 1][:, t0:t1], ADD)
+        for t0, t1 in PARTS:
+            scale(1, 0, t0, t1)
         for (t0, t1), queue in zip(PARTS, (nc.sync, nc.scalar)):
-            nc.vector.tensor_tensor(total[1][:, t0:t1], pair[:, t0:t1], term[1, 1][:, t0:t1], ADD)
+            nc.vector.tensor_tensor(total[1][:, t0:t1], pair[:, t0:t1], term[1, 0][:, t0:t1], ADD)
             queue.dma_start(out=out[P:N, t0:t1], in_=total[1][:, t0:t1])

@@ -42,9 +42,10 @@ ROUNDS = (
     ((0, 384, "s"), (384, 640, "g")),
 )
 BLOCKS = T // P
-SCALE_LOADS = 2
-WHOLE = 3
+GATE_STEP = N * T // BLOCKS
+ORDER = (0, 2, 1, 3)
 GROUPS = ((0, 3), (3, 5), (5, 6))
+BANKED = (GROUPS, ((0, 3), (3, 6)))
 PARTS = ((0, 384), (384, 640))
 
 
@@ -69,7 +70,7 @@ def tile_moe_ecr_lin_none_kernel(
         words = keep([P, LAST * T + WIDE], U32, "words")
         y = [keep([P, SLOTS + PAD], F32, "y%d" % h) for h in range(HALVES)]
 
-        gate_rows = keep([P, TOP, P], F32, "gate_rows")
+        gate_rows = keep([P, P], F32, "gate_rows")
         nc.gpsimd.memset(gate_rows[:], 0.0)
         nc.vector.memset(y[1][:, SLOTS:], 0.0)
         nc.scalar.copy(y[0][:, SLOTS:], y[1][:, SLOTS:])
@@ -85,17 +86,31 @@ def tile_moe_ecr_lin_none_kernel(
             nc.sync.dma_start(out=raw[a][:], in_=rows)
             if a == 0:
                 nc.sync.dma_start(offs_sb[:], offs)
-                nc.sync.dma_start(out=gate_rows[0:BLOCKS], in_=gate[:, 0, :].rearrange("r (b i) -> b r i", i=P))
+                pieces = gate.rearrange("r n t -> (r n t)").rearrange("(m s) -> m s", s=GATE_STEP)
+                nc.sync.dma_start(out=gate_rows[0 : TOP * BLOCKS], in_=pieces[:, 0:P])
 
-        scale_rows = w_scales.bitcast(I32).rearrange("e a q n -> q (e a) n")
-        w_plane = keep([P, E * PASSES, N], U8, "w_plane")
-        share = E * PASSES // SCALE_LOADS
-        for i in range(SCALE_LOADS):
+        for tile, entries in zip(pos_sb, (pos1, pos2, pos3)):
+            nc.sync.dma_start(tile[:], entries)
+
+        scale_rows = w_scales.bitcast(I32).rearrange("e (b s) q n -> s q (e b) n", s=2)
+        word_rows = w_words.bitcast(I32)
+
+        def load_scales(plane, parity):
             for r in range(PLANE_ROWS):
                 nc.sync.dma_start(
-                    out=w_plane[r:P:QUADRANT, i * share : (i + 1) * share].bitcast(I32),
-                    in_=scale_rows[r : PLANE_ROWS * P // QUADRANT : PLANE_ROWS, i * share : (i + 1) * share],
+                    out=plane[r:P:QUADRANT].bitcast(I32),
+                    in_=scale_rows[parity, r : PLANE_ROWS * P // QUADRANT : PLANE_ROWS],
                 )
+
+        def load_codes(codes, a):
+            nc.sync.dma_start(out=codes.bitcast(I32), in_=word_rows[:, a].rearrange("e p n -> p e n"))
+
+        even_plane = keep([P, 2 * E, N], U8, "even_plane")
+        even_codes = keep([P, 2, E, 2 * N], U8, "even_codes")
+        load_scales(even_plane[:], 0)
+        load_codes(even_codes[:, 0], 0)
+        load_codes(even_codes[:, 1], 2)
+
         slot_words = [keep([P, SLOTS], U32, "slot_words%d" % a) for a in range(LAST)]
         last_slot_words = [keep([P, (e1 - e0) * C], U32, "last_slot_words%d" % e0) for e0, e1 in GROUPS]
         early_slot_bytes = keep([P, SLOTS], U8, "early_slot_bytes")
@@ -123,33 +138,41 @@ def tile_moe_ecr_lin_none_kernel(
                 c0 = word_column(a)
                 nc.vector.quantize_mx(out=words[:, c0 + t0 : c0 + t1].bitcast(FP8X4), scales=plane, in_=grouped[t0][:])
 
-        for a in range(LAST):
-            quantise(a)
-            if a == LAST - 1:
-                nc.vector.tensor_copy(early_slot_bytes[:], early_bytes[:].indirect(offs_sb[:]))
+        def gather_words(a):
             window = words[:, word_column(a) : word_column(a) + WIDE]
             nc.vector.tensor_copy(slot_words[a][:], window.indirect(offs_sb[:]))
 
-        turned_rows = bank(TOP * P, "turned_rows", 0)
-        for r in range(TOP):
-            nc.tensor.transpose(turned_rows[:, r * P : (r + 1) * P], gate_rows[:, r], ident[:])
-        gate_columns = keep([P, TOP, BLOCKS], F32, "gate_columns", "raw0")
-        nc.scalar.copy(gate_columns[:], turned_rows[:].rearrange("p (r i) -> p r i", i=P)[:, :, 0:BLOCKS])
+        quantise(0)
+        gather_words(0)
+
+        turned_rows = bank(P, "turned_rows", 0)
+        nc.tensor.transpose(turned_rows[:], gate_rows[:], ident[:])
+        gate_columns = keep([P, TOP * BLOCKS], F32, "gate_columns", "raw0")
+        nc.scalar.copy(gate_columns[:], turned_rows[:, 0 : TOP * BLOCKS])
         spread = [bank(min(BANK, TOP * T - c), "spread%d" % c, 4 + c // BANK) for c in range(0, TOP * T, BANK)]
         for m in range(TOP * BLOCKS):
             b, c = divmod(m * P, BANK)
-            column = gate_columns[:].rearrange("p r b -> p (r b)")[:, m : m + 1]
-            nc.tensor.transpose(spread[b][:, c : c + P], column.to_broadcast([P, P]), ident[:])
+            nc.tensor.transpose(spread[b][:, c : c + P], gate_columns[:, m : m + 1].to_broadcast([P, P]), ident[:])
 
+        def copy_gates(tile, c0, c1):
+            for b in range(c0 // BANK, (c1 - 1) // BANK + 1):
+                lo, hi = max(c0, b * BANK), min(c1, (b + 1) * BANK)
+                nc.scalar.copy(tile[:, lo - c0 : hi - c0], spread[b][:, lo - b * BANK : hi - b * BANK])
+
+        quantise(1)
+        gather_words(1)
+        first_gate = keep([P, T], F32, "first_gate", "raw1")
+        copy_gates(first_gate, 0, T)
+        quantise(2)
+        nc.vector.tensor_copy(early_slot_bytes[:], early_bytes[:].indirect(offs_sb[:]))
+        gather_words(2)
+        other_gates = keep([P, (TOP - 1) * T], F32, "other_gates", "raw2")
+        copy_gates(other_gates, T, TOP * T)
+        gates = [first_gate[:]] + [other_gates[:, r * T : (r + 1) * T] for r in range(TOP - 1)]
         quantise(LAST)
+
         moved = keep([P, (LAST - 1) * SLOTS], U8, "moved")
         shifted = {a: moved[:, (a - 1) * SLOTS : a * SLOTS] for a in range(1, LAST)}
-        word_rows = w_words.bitcast(I32)
-        w_first = keep([P, 2, E, 2 * N], U8, "w_first")
-        w_rest = keep([P, 2, E * 2 * N], U8, "w_rest", "early_bytes")
-        whole = [w_first[:, 0], w_first[:, 1], w_rest[:, 0].rearrange("p (e n) -> p e n", e=E)]
-        w_codes = {(h, a): whole[a][:, :, 2 * P * h : 2 * P * (h + 1)] for h in range(HALVES) for a in range(WHOLE)}
-        order = [(h, LAST) for h in range(HALVES)]
 
         def shift(a):
             nc.sync.dma_start(
@@ -157,21 +180,16 @@ def tile_moe_ecr_lin_none_kernel(
                 in_=early_slot_bytes[PLANE_ROWS * a : PLANE_ROWS * a + LIVE_ROWS, :].bitcast(I32),
             )
 
-        for a in range(WHOLE):
-            if a - 1 in shifted:
-                shift(a - 1)
-            nc.sync.dma_start(out=whole[a].bitcast(I32), in_=word_rows[:, a].rearrange("e p n -> p e n"))
-        shift(LAST - 1)
-        for h, a in order:
-            w_codes[h, a] = w_rest[:, 1].rearrange("p (h e n) -> p h e n", h=HALVES, e=E)[:, h]
-            columns = word_rows[:, a, :, h * P // 2 : (h + 1) * P // 2]
-            nc.sync.dma_start(out=w_codes[h, a].bitcast(I32), in_=columns.rearrange("e p n -> p e n"))
-        for tile, entries in zip(pos_sb, (pos1, pos2, pos3)):
-            nc.sync.dma_start(tile[:], entries)
-        gates = keep([P, TOP, T], F32, "gates", "raw%d" % LAST)
-        flat_gates = gates[:].rearrange("p r t -> p (r t)")
-        for b, c in enumerate(range(0, TOP * T, BANK)):
-            nc.scalar.copy(flat_gates[:, c : min(c + BANK, TOP * T)], spread[b][:])
+        odd = keep([P, 3, E * 2 * N], U8, "odd", "early_bytes")
+        odd_plane = odd[:, 0].rearrange("p (m n) -> p m n", n=N)
+        odd_codes = [odd[:, 1 + b].rearrange("p (e n) -> p e n", e=E) for b in range(2)]
+        shift(2)
+        load_scales(odd_plane, 1)
+        shift(1)
+        load_codes(odd_codes[0], 1)
+        load_codes(odd_codes[1], 3)
+        w_codes = [even_codes[:, 0], odd_codes[0], even_codes[:, 1], odd_codes[1]]
+        w_planes = [even_plane[:], odd_plane]
 
         nc.vector.tensor_copy(last_slot_bytes[:], last_bytes[:].indirect(offs_sb[:]))
         for g, (e0, e1) in enumerate(GROUPS):
@@ -181,41 +199,52 @@ def tile_moe_ecr_lin_none_kernel(
         sums = {
             (h, g): bank((e1 - e0) * C, "sums%d_%d" % (h, g), 1 + len(GROUPS) * h + g)
             for h in range(HALVES)
-            for g, (e0, e1) in enumerate(GROUPS)
+            for g, (e0, e1) in enumerate(BANKED[h])
         }
-        for h, a in [(h, a) for a in range(WHOLE) for h in range(HALVES)] + order:
-            for g, (e0, e1) in enumerate(GROUPS):
-                for e in range(e0, e1):
-                    slots = slice(e * C, (e + 1) * C)
-                    local = slice((e - e0) * C, (e - e0 + 1) * C)
-                    if a == LAST:
-                        moving, plane = last_slot_words[g][:, local], last_slot_bytes[:, slots]
-                    else:
-                        moving = slot_words[a][:, slots]
-                        plane = (early_slot_bytes if a == 0 else shifted[a])[:, slots]
-                    nc.tensor.matmul_mx(
-                        out=sums[h, g][:, local],
-                        lhsT=w_codes[h, a][:, e].bitcast(FP4X4),
-                        lhsT_scale=w_plane[:, e * PASSES + a, P * h : P * (h + 1)],
-                        rhs=moving.bitcast(FP8X4),
-                        rhs_scale=plane,
-                        start=(a == 0 and e == e0),
-                        stop=(a == LAST and e == e1 - 1),
-                    )
+        last_words = {e: last_slot_words[g][:, (e - e0) * C : (e - e0 + 1) * C] for g, (e0, e1) in enumerate(GROUPS) for e in range(e0, e1)}
+
+        def multiply(a, h, g):
+            e0, e1 = BANKED[h][g]
+            for e in range(e0, e1):
+                slots = slice(e * C, (e + 1) * C)
                 if a == LAST:
-                    nc.scalar.copy(y[h][:, e0 * C : e1 * C], sums[h, g][:])
+                    moving, plane = last_words[e], last_slot_bytes[:, slots]
+                else:
+                    moving = slot_words[a][:, slots]
+                    plane = (early_slot_bytes if a == 0 else shifted[a])[:, slots]
+                nc.tensor.matmul_mx(
+                    out=sums[h, g][:, (e - e0) * C : (e - e0 + 1) * C],
+                    lhsT=w_codes[a][:, e, 2 * P * h : 2 * P * (h + 1)].bitcast(FP4X4),
+                    lhsT_scale=w_planes[a % 2][:, 2 * e + a // 2, P * h : P * (h + 1)],
+                    rhs=moving.bitcast(FP8X4),
+                    rhs_scale=plane,
+                    start=(a == ORDER[0] and e == e0),
+                    stop=(a == LAST and e == e1 - 1),
+                )
+
+        for a in ORDER[:LAST]:
+            for h in range(HALVES):
+                for g in range(len(BANKED[h])):
+                    multiply(a, h, g)
+        for h, g in ((0, 0), (1, 0), (0, 1), (0, 2), (1, 1)):
+            multiply(LAST, h, g)
+            e0, e1 = BANKED[h][g]
+            if (h, g) == (1, 0):
+                nc.vector.tensor_copy(y[h][:, e0 * C : e1 * C], sums[h, g][:])
+            else:
+                nc.scalar.copy(y[h][:, e0 * C : e1 * C], sums[h, g][:])
 
         term = {(h, r): keep([P, T], F32, "term%d_%d" % (h, r)) for h in range(HALVES) for r in range(TOP)}
         plain = {(h, r): keep([P, T], F32, "plain%d_%d" % (h, r)) for h, r in ((0, 0), (1, 0), (1, 1))}
 
         def weigh(h, r):
-            nc.vector.tensor_tensor(term[h, r][:], y[h][:].indirect(pos_sb[r][:]), gates[:, r], MULT)
+            nc.vector.tensor_tensor(term[h, r][:], y[h][:].indirect(pos_sb[r][:]), gates[r], MULT)
 
         def fetch(h, r):
             nc.scalar.activation(plain[h, r][:], y[h][:].indirect(pos_sb[r][:]), COPY)
 
         def scale(h, r, t0=0, t1=T):
-            nc.vector.tensor_tensor(term[h, r][:, t0:t1], plain[h, r][:, t0:t1], gates[:, r, t0:t1], MULT)
+            nc.vector.tensor_tensor(term[h, r][:, t0:t1], plain[h, r][:, t0:t1], gates[r][:, t0:t1], MULT)
 
         turned = [bank(P, "turned%d" % b, number) for b, number in enumerate((0, 7, 1, 2, 3))]
         back = {t0: bank(t1 - t0, "back%d" % t0, number) for (t0, t1), number in zip(PARTS, (4, 5))}

@@ -43,9 +43,10 @@ ROUNDS = (
 )
 BLOCKS = T // P
 GATE_STEP = N * T // BLOCKS
-ORDER = (0, 2, 1, 3)
-GROUPS = ((0, 3), (3, 5), (5, 6))
-BANKED = (GROUPS, ((0, 3), (3, 6)))
+SPACING = QUADRANT // PLANE_ROWS
+GROUPS = ((0, 2), (2, 4), (4, 5), (5, 6))
+BANKED = (GROUPS, ((0, 2), (2, 6)))
+PUT_OFF = 128
 PARTS = ((0, 384), (384, 640))
 
 
@@ -55,6 +56,7 @@ def tile_moe_ecr_lin_none_kernel(
     nc = tc.nc
     with ExitStack() as ctx:
         held = ctx.enter_context(tc.tile_pool(name="held", bufs=1))
+        shared = ctx.enter_context(tc.tile_pool(name="shared", bufs=1))
         psum = ctx.enter_context(tc.psum_pool(name="psum", bufs=1))
 
         def keep(shape, dtype, name, tag=None):
@@ -80,10 +82,17 @@ def tile_moe_ecr_lin_none_kernel(
         ident = keep([P, P], F32, "ident")
         make_identity(nc, ident[:])
 
-        raw = [keep([P, PACK, T], F32, "raw%d" % a) for a in range(PASSES)]
+        w_plane = keep([P, E * PASSES * N], U8, "w_plane")
+        raw = [keep([P, PACK, T], F32, "raw%d" % a) for a in range(LAST)]
+        raw.append(shared.tile([P, PACK, T], F32, name="raw_last", offset=0))
         for a in range(PASSES):
             rows = xT[a * K_PASS : (a + 1) * K_PASS, :].rearrange("(p j) t -> p j t", j=PACK)
             nc.sync.dma_start(out=raw[a][:], in_=rows)
+            if a == LAST - 1:
+                nc.sync.dma_start(
+                    out=w_plane[0:P:SPACING].bitcast(I32).rearrange("q (m n) -> q m n", m=E * PASSES),
+                    in_=w_scales.bitcast(I32).rearrange("e a q n -> q (e a) n"),
+                )
             if a == 0:
                 nc.sync.dma_start(offs_sb[:], offs)
                 pieces = gate.rearrange("r n t -> (r n t)").rearrange("(m s) -> m s", s=GATE_STEP)
@@ -92,26 +101,14 @@ def tile_moe_ecr_lin_none_kernel(
         for tile, entries in zip(pos_sb, (pos1, pos2, pos3)):
             nc.sync.dma_start(tile[:], entries)
 
-        scale_rows = w_scales.bitcast(I32).rearrange("e (b s) q n -> s q (e b) n", s=2)
+        for r in range(1, PLANE_ROWS):
+            nc.sync.dma_start(out=w_plane[r:P:QUADRANT].bitcast(I32), in_=w_plane[SPACING * r : P : QUADRANT].bitcast(I32))
         word_rows = w_words.bitcast(I32)
-
-        def load_scales(plane, parity):
-            for r in range(PLANE_ROWS):
-                nc.sync.dma_start(
-                    out=plane[r:P:QUADRANT].bitcast(I32),
-                    in_=scale_rows[parity, r : PLANE_ROWS * P // QUADRANT : PLANE_ROWS],
-                )
 
         def load_codes(codes, a):
             nc.sync.dma_start(out=codes.bitcast(I32), in_=word_rows[:, a].rearrange("e p n -> p e n"))
 
-        even_plane = keep([P, 2 * E, N], U8, "even_plane")
-        even_codes = keep([P, 2, E, 2 * N], U8, "even_codes")
-        load_scales(even_plane[:], 0)
-        load_codes(even_codes[:, 0], 0)
-        load_codes(even_codes[:, 1], 2)
-
-        slot_words = [keep([P, SLOTS], U32, "slot_words%d" % a) for a in range(LAST)]
+        slot_words = [keep([P, SLOTS - (PUT_OFF if a == 2 else 0)], U32, "slot_words%d" % a) for a in range(LAST)]
         last_slot_words = [keep([P, (e1 - e0) * C], U32, "last_slot_words%d" % e0) for e0, e1 in GROUPS]
         early_slot_bytes = keep([P, SLOTS], U8, "early_slot_bytes")
         last_slot_bytes = keep([P, SLOTS], U8, "last_slot_bytes")
@@ -154,22 +151,21 @@ def tile_moe_ecr_lin_none_kernel(
             b, c = divmod(m * P, BANK)
             nc.tensor.transpose(spread[b][:, c : c + P], gate_columns[:, m : m + 1].to_broadcast([P, P]), ident[:])
 
-        def copy_gates(tile, c0, c1):
-            for b in range(c0 // BANK, (c1 - 1) // BANK + 1):
-                lo, hi = max(c0, b * BANK), min(c1, (b + 1) * BANK)
-                nc.scalar.copy(tile[:, lo - c0 : hi - c0], spread[b][:, lo - b * BANK : hi - b * BANK])
-
         quantise(1)
         gather_words(1)
-        first_gate = keep([P, T], F32, "first_gate", "raw1")
-        copy_gates(first_gate, 0, T)
         quantise(2)
         nc.vector.tensor_copy(early_slot_bytes[:], early_bytes[:].indirect(offs_sb[:]))
-        gather_words(2)
-        other_gates = keep([P, (TOP - 1) * T], F32, "other_gates", "raw2")
-        copy_gates(other_gates, T, TOP * T)
-        gates = [first_gate[:]] + [other_gates[:, r * T : (r + 1) * T] for r in range(TOP - 1)]
+        early = (SLOTS - PUT_OFF) // PER_COLUMN
+        window = words[:, word_column(2) : word_column(2) + WIDE]
+        nc.vector.tensor_copy(slot_words[2][:], window.indirect(offs_sb[:, 0:early]))
         quantise(LAST)
+        late_window = words[:, word_column(2) : word_column(2) + T]
+        all_gates = shared.tile([P, TOP * T], F32, name="all_gates", offset=0)
+        for b, c in enumerate(range(0, TOP * T, BANK)):
+            nc.scalar.copy(all_gates[:, c : min(c + BANK, TOP * T)], spread[b][:])
+        gates = [all_gates[:, r * T : (r + 1) * T] for r in range(TOP)]
+        put_off = shared.tile([P, PUT_OFF], U32, name="put_off", offset=4 * TOP * T, align_bytes=64)
+        nc.vector.tensor_copy(put_off[:], late_window.indirect(offs_sb[:, early:]))
 
         moved = keep([P, (LAST - 1) * SLOTS], U8, "moved")
         shifted = {a: moved[:, (a - 1) * SLOTS : a * SLOTS] for a in range(1, LAST)}
@@ -180,16 +176,15 @@ def tile_moe_ecr_lin_none_kernel(
                 in_=early_slot_bytes[PLANE_ROWS * a : PLANE_ROWS * a + LIVE_ROWS, :].bitcast(I32),
             )
 
-        odd = keep([P, 3, E * 2 * N], U8, "odd", "early_bytes")
-        odd_plane = odd[:, 0].rearrange("p (m n) -> p m n", n=N)
-        odd_codes = [odd[:, 1 + b].rearrange("p (e n) -> p e n", e=E) for b in range(2)]
-        shift(2)
-        load_scales(odd_plane, 1)
+        w_first = keep([P, 2, E, 2 * N], U8, "w_first", "grouped2_0")
+        w_rest = keep([P, 2, E, 2 * N], U8, "w_rest", "early_bytes")
+        w_codes = [w_first[:, 0], w_first[:, 1], w_rest[:, 0], w_rest[:, 1]]
+        load_codes(w_codes[0], 0)
+        load_codes(w_codes[1], 1)
         shift(1)
-        load_codes(odd_codes[0], 1)
-        load_codes(odd_codes[1], 3)
-        w_codes = [even_codes[:, 0], odd_codes[0], even_codes[:, 1], odd_codes[1]]
-        w_planes = [even_plane[:], odd_plane]
+        load_codes(w_codes[2], 2)
+        shift(2)
+        load_codes(w_codes[LAST], LAST)
 
         nc.vector.tensor_copy(last_slot_bytes[:], last_bytes[:].indirect(offs_sb[:]))
         for g, (e0, e1) in enumerate(GROUPS):
@@ -210,23 +205,23 @@ def tile_moe_ecr_lin_none_kernel(
                 if a == LAST:
                     moving, plane = last_words[e], last_slot_bytes[:, slots]
                 else:
-                    moving = slot_words[a][:, slots]
+                    moving = put_off[:] if (a, e) == (2, E - 1) else slot_words[a][:, slots]
                     plane = (early_slot_bytes if a == 0 else shifted[a])[:, slots]
                 nc.tensor.matmul_mx(
                     out=sums[h, g][:, (e - e0) * C : (e - e0 + 1) * C],
                     lhsT=w_codes[a][:, e, 2 * P * h : 2 * P * (h + 1)].bitcast(FP4X4),
-                    lhsT_scale=w_planes[a % 2][:, 2 * e + a // 2, P * h : P * (h + 1)],
+                    lhsT_scale=w_plane[:, (e * PASSES + a) * N + P * h : (e * PASSES + a) * N + P * (h + 1)],
                     rhs=moving.bitcast(FP8X4),
                     rhs_scale=plane,
-                    start=(a == ORDER[0] and e == e0),
+                    start=(a == 0 and e == e0),
                     stop=(a == LAST and e == e1 - 1),
                 )
 
-        for a in ORDER[:LAST]:
+        for a in range(LAST):
             for h in range(HALVES):
                 for g in range(len(BANKED[h])):
                     multiply(a, h, g)
-        for h, g in ((0, 0), (1, 0), (0, 1), (0, 2), (1, 1)):
+        for h, g in ((0, 0), (1, 0), (0, 1), (0, 2), (0, 3), (1, 1)):
             multiply(LAST, h, g)
             e0, e1 = BANKED[h][g]
             if (h, g) == (1, 0):

@@ -44,8 +44,8 @@ ROUNDS = (
 BLOCKS = T // P
 GATE_STEP = N * T // BLOCKS
 SPACING = QUADRANT // PLANE_ROWS
-GROUPS = ((0, 2), (2, 4), (4, 5), (5, 6))
-BANKED = (GROUPS, ((0, 2), (2, 6)))
+GROUPS = ((0, 3), (3, 5), (5, 6))
+BANKED = (GROUPS, ((0, 3), (3, 6)))
 PUT_OFF = 128
 PARTS = ((0, 384), (384, 640))
 
@@ -177,14 +177,18 @@ def tile_moe_ecr_lin_none_kernel(
             )
 
         w_first = keep([P, 2, E, 2 * N], U8, "w_first", "grouped2_0")
-        w_rest = keep([P, 2, E, 2 * N], U8, "w_rest", "early_bytes")
-        w_codes = [w_first[:, 0], w_first[:, 1], w_rest[:, 0], w_rest[:, 1]]
-        load_codes(w_codes[0], 0)
-        load_codes(w_codes[1], 1)
+        w_rest = keep([P, 2, E * 2 * N], U8, "w_rest", "early_bytes")
+        whole = [w_first[:, 0], w_first[:, 1], w_rest[:, 0].rearrange("p (e n) -> p e n", e=E)]
+        w_codes = {(a, h): whole[a][:, :, 2 * P * h : 2 * P * (h + 1)] for a in range(LAST) for h in range(HALVES)}
+        load_codes(whole[0], 0)
+        load_codes(whole[1], 1)
         shift(1)
-        load_codes(w_codes[2], 2)
+        load_codes(whole[2], 2)
         shift(2)
-        load_codes(w_codes[LAST], LAST)
+        for h in range(HALVES):
+            w_codes[LAST, h] = w_rest[:, 1].rearrange("p (h e n) -> p h e n", h=HALVES, e=E)[:, h]
+            columns = word_rows[:, LAST, :, h * P // 2 : (h + 1) * P // 2]
+            nc.sync.dma_start(out=w_codes[LAST, h].bitcast(I32), in_=columns.rearrange("e p n -> p e n"))
 
         nc.vector.tensor_copy(last_slot_bytes[:], last_bytes[:].indirect(offs_sb[:]))
         for g, (e0, e1) in enumerate(GROUPS):
@@ -209,7 +213,7 @@ def tile_moe_ecr_lin_none_kernel(
                     plane = (early_slot_bytes if a == 0 else shifted[a])[:, slots]
                 nc.tensor.matmul_mx(
                     out=sums[h, g][:, (e - e0) * C : (e - e0 + 1) * C],
-                    lhsT=w_codes[a][:, e, 2 * P * h : 2 * P * (h + 1)].bitcast(FP4X4),
+                    lhsT=w_codes[a, h][:, e].bitcast(FP4X4),
                     lhsT_scale=w_plane[:, (e * PASSES + a) * N + P * h : (e * PASSES + a) * N + P * (h + 1)],
                     rhs=moving.bitcast(FP8X4),
                     rhs_scale=plane,
@@ -221,26 +225,29 @@ def tile_moe_ecr_lin_none_kernel(
             for h in range(HALVES):
                 for g in range(len(BANKED[h])):
                     multiply(a, h, g)
-        for h, g in ((0, 0), (1, 0), (0, 1), (0, 2), (0, 3), (1, 1)):
-            multiply(LAST, h, g)
-            e0, e1 = BANKED[h][g]
-            if (h, g) == (1, 0):
-                nc.vector.tensor_copy(y[h][:, e0 * C : e1 * C], sums[h, g][:])
-            else:
+        def finish(h):
+            for g, (e0, e1) in enumerate(BANKED[h]):
+                multiply(LAST, h, g)
                 nc.scalar.copy(y[h][:, e0 * C : e1 * C], sums[h, g][:])
 
         term = {(h, r): keep([P, T], F32, "term%d_%d" % (h, r)) for h in range(HALVES) for r in range(TOP)}
         plain = {(h, r): keep([P, T], F32, "plain%d_%d" % (h, r)) for h, r in ((0, 0), (1, 0), (1, 1))}
 
-        def weigh(h, r):
-            nc.vector.tensor_tensor(term[h, r][:], y[h][:].indirect(pos_sb[r][:]), gates[r], MULT)
+        def picked(h, r, t0, t1):
+            return y[h][:].indirect(pos_sb[r][:, t0 // PER_COLUMN : t1 // PER_COLUMN])
 
-        def fetch(h, r):
-            nc.scalar.activation(plain[h, r][:], y[h][:].indirect(pos_sb[r][:]), COPY)
+        def weigh(h, r, t0=0, t1=T):
+            nc.vector.tensor_tensor(term[h, r][:, t0:t1], picked(h, r, t0, t1), gates[r][:, t0:t1], MULT)
+
+        def fetch(h, r, t0=0, t1=T):
+            nc.scalar.activation(plain[h, r][:, t0:t1], picked(h, r, t0, t1), COPY)
 
         def scale(h, r, t0=0, t1=T):
             nc.vector.tensor_tensor(term[h, r][:, t0:t1], plain[h, r][:, t0:t1], gates[r][:, t0:t1], MULT)
 
+        finish(0)
+        fetch(0, 0)
+        finish(1)
         turned = [bank(P, "turned%d" % b, number) for b, number in enumerate((0, 7, 1, 2, 3))]
         back = {t0: bank(t1 - t0, "back%d" % t0, number) for (t0, t1), number in zip(PARTS, (4, 5))}
         staged = keep([P, T], F32, "staged")
@@ -253,8 +260,7 @@ def tile_moe_ecr_lin_none_kernel(
                     turned[b][:], lhsT=term[0, r][:, b * P : (b + 1) * P], rhs=ident[:], start=first, stop=last, is_transpose=True
                 )
 
-        fetch(0, 0)
-        fetch(1, 1)
+        fetch(1, 1, *PARTS[0])
         fetch(1, 0)
         weigh(0, 2)
         turn(2, True, False)
@@ -270,8 +276,8 @@ def tile_moe_ecr_lin_none_kernel(
             nc.scalar.copy(total[0][:, t0:t1], back[t0][:])
             nc.sync.dma_start(out=out[0:P, t0:t1], in_=total[0][:, t0:t1])
         weigh(1, 2)
-        for t0, t1 in PARTS:
-            scale(1, 1, t0, t1)
+        scale(1, 1, *PARTS[0])
+        weigh(1, 1, *PARTS[1])
         for t0, t1 in PARTS:
             nc.vector.tensor_tensor(pair[:, t0:t1], term[1, 2][:, t0:t1], term[1, 1][:, t0:t1], ADD)
         for t0, t1 in PARTS:

@@ -39,7 +39,7 @@ ROUNDS = (
     ((0, 256, "v"), (256, 384, "s"), (384, 512, "g"), (512, 640, "s")),
     ((0, 256, "s"), (256, 512, "g"), (512, 640, "s")),
     ((0, 256, "s"), (256, 512, "g"), (512, 640, "s")),
-    ((0, 384, "s"), (384, 640, "g")),
+    ((0, 256, "s"), (256, 512, "s"), (512, 640, "s")),
 )
 BLOCKS = T // P
 GATE_STEP = N * T // BLOCKS
@@ -146,10 +146,15 @@ def tile_moe_ecr_lin_none_kernel(
         nc.tensor.transpose(turned_rows[:], gate_rows[:], ident[:])
         gate_columns = keep([P, TOP * BLOCKS], F32, "gate_columns", "raw0")
         nc.scalar.copy(gate_columns[:], turned_rows[:, 0 : TOP * BLOCKS])
-        spread = [bank(min(BANK, TOP * T - c), "spread%d" % c, 4 + c // BANK) for c in range(0, TOP * T, BANK)]
+        spread = [bank(min(BANK, TOP * T - c), "spread%d" % c, number) for c, number in zip(range(0, TOP * T, BANK), (5, 6, 7, 0))]
         for m in range(TOP * BLOCKS):
             b, c = divmod(m * P, BANK)
             nc.tensor.transpose(spread[b][:, c : c + P], gate_columns[:, m : m + 1].to_broadcast([P, P]), ident[:])
+
+        def copy_gates(tile, c0, c1):
+            for b in range(c0 // BANK, (c1 - 1) // BANK + 1):
+                lo, hi = max(c0, b * BANK), min(c1, (b + 1) * BANK)
+                nc.scalar.copy(tile[:, lo - c0 : hi - c0], spread[b][:, lo - b * BANK : hi - b * BANK])
 
         quantise(1)
         gather_words(1)
@@ -158,12 +163,13 @@ def tile_moe_ecr_lin_none_kernel(
         early = (SLOTS - PUT_OFF) // PER_COLUMN
         window = words[:, word_column(2) : word_column(2) + WIDE]
         nc.vector.tensor_copy(slot_words[2][:], window.indirect(offs_sb[:, 0:early]))
+        first_gate = keep([P, T], F32, "first_gate", "raw2")
+        copy_gates(first_gate, 0, T)
         quantise(LAST)
         late_window = words[:, word_column(2) : word_column(2) + T]
-        all_gates = shared.tile([P, TOP * T], F32, name="all_gates", offset=0)
-        for b, c in enumerate(range(0, TOP * T, BANK)):
-            nc.scalar.copy(all_gates[:, c : min(c + BANK, TOP * T)], spread[b][:])
-        gates = [all_gates[:, r * T : (r + 1) * T] for r in range(TOP)]
+        other_gates = shared.tile([P, (TOP - 1) * T], F32, name="other_gates", offset=0)
+        copy_gates(other_gates, T, TOP * T)
+        gates = [first_gate[:]] + [other_gates[:, r * T : (r + 1) * T] for r in range(TOP - 1)]
         put_off = shared.tile([P, PUT_OFF], U32, name="put_off", offset=4 * TOP * T, align_bytes=64)
         nc.vector.tensor_copy(put_off[:], late_window.indirect(offs_sb[:, early:]))
 

@@ -39,14 +39,20 @@ ROUNDS = (
     ((0, 256, "v"), (256, 384, "s"), (384, 512, "g"), (512, 640, "s")),
     ((0, 256, "s"), (256, 512, "g"), (512, 640, "s")),
     ((0, 256, "s"), (256, 512, "g"), (512, 640, "s")),
-    ((0, 256, "s"), (256, 512, "s"), (512, 640, "s")),
+    ((0, 384, "s"), (384, 640, "g")),
 )
 BLOCKS = T // P
 GATE_STEP = N * T // BLOCKS
 SPACING = QUADRANT // PLANE_ROWS
 GROUPS = ((0, 3), (3, 5), (5, 6))
-BANKED = (GROUPS, ((0, 3), (3, 6)))
-PUT_OFF = 128
+BANKED = (GROUPS, ((0, 2), (2, 6)))
+SPREAD = {
+    5: ((1, 0), (1, 1), (1, 2)),
+    7: ((0, 3), (0, 4), (1, 3), (1, 4)),
+    6: ((0, 0), (0, 1), (0, 2), (2, 4)),
+    0: ((2, 0), (2, 1), (2, 2), (2, 3)),
+}
+TURNS = ((0, 128), (128, 256), (256, 384), (384, 640))
 PARTS = ((0, 384), (384, 640))
 
 
@@ -56,7 +62,6 @@ def tile_moe_ecr_lin_none_kernel(
     nc = tc.nc
     with ExitStack() as ctx:
         held = ctx.enter_context(tc.tile_pool(name="held", bufs=1))
-        shared = ctx.enter_context(tc.tile_pool(name="shared", bufs=1))
         psum = ctx.enter_context(tc.psum_pool(name="psum", bufs=1))
 
         def keep(shape, dtype, name, tag=None):
@@ -83,8 +88,7 @@ def tile_moe_ecr_lin_none_kernel(
         make_identity(nc, ident[:])
 
         w_plane = keep([P, E * PASSES * N], U8, "w_plane")
-        raw = [keep([P, PACK, T], F32, "raw%d" % a) for a in range(LAST)]
-        raw.append(shared.tile([P, PACK, T], F32, name="raw_last", offset=0))
+        raw = [keep([P, PACK, T], F32, "raw%d" % a) for a in range(PASSES)]
         for a in range(PASSES):
             rows = xT[a * K_PASS : (a + 1) * K_PASS, :].rearrange("(p j) t -> p j t", j=PACK)
             nc.sync.dma_start(out=raw[a][:], in_=rows)
@@ -108,7 +112,7 @@ def tile_moe_ecr_lin_none_kernel(
         def load_codes(codes, a):
             nc.sync.dma_start(out=codes.bitcast(I32), in_=word_rows[:, a].rearrange("e p n -> p e n"))
 
-        slot_words = [keep([P, SLOTS - (PUT_OFF if a == 2 else 0)], U32, "slot_words%d" % a) for a in range(LAST)]
+        slot_words = [keep([P, SLOTS], U32, "slot_words%d" % a) for a in range(LAST)]
         last_slot_words = [keep([P, (e1 - e0) * C], U32, "last_slot_words%d" % e0) for e0, e1 in GROUPS]
         early_slot_bytes = keep([P, SLOTS], U8, "early_slot_bytes")
         last_slot_bytes = keep([P, SLOTS], U8, "last_slot_bytes")
@@ -146,32 +150,29 @@ def tile_moe_ecr_lin_none_kernel(
         nc.tensor.transpose(turned_rows[:], gate_rows[:], ident[:])
         gate_columns = keep([P, TOP * BLOCKS], F32, "gate_columns", "raw0")
         nc.scalar.copy(gate_columns[:], turned_rows[:, 0 : TOP * BLOCKS])
-        spread = [bank(min(BANK, TOP * T - c), "spread%d" % c, number) for c, number in zip(range(0, TOP * T, BANK), (5, 6, 7, 0))]
-        for m in range(TOP * BLOCKS):
-            b, c = divmod(m * P, BANK)
-            nc.tensor.transpose(spread[b][:, c : c + P], gate_columns[:, m : m + 1].to_broadcast([P, P]), ident[:])
+        spread = {number: bank(len(blocks) * P, "spread%d" % number, number) for number, blocks in SPREAD.items()}
+        for number, blocks in SPREAD.items():
+            for i, (r, b) in enumerate(blocks):
+                column = gate_columns[:, r * BLOCKS + b : r * BLOCKS + b + 1]
+                nc.tensor.transpose(spread[number][:, i * P : (i + 1) * P], column.to_broadcast([P, P]), ident[:])
 
-        def copy_gates(tile, c0, c1):
-            for b in range(c0 // BANK, (c1 - 1) // BANK + 1):
-                lo, hi = max(c0, b * BANK), min(c1, (b + 1) * BANK)
-                nc.scalar.copy(tile[:, lo - c0 : hi - c0], spread[b][:, lo - b * BANK : hi - b * BANK])
+        def banked_gate(r, t0, t1):
+            number = [n for n, blocks in SPREAD.items() if (r, t0 // P) in blocks][0]
+            c = SPREAD[number].index((r, t0 // P)) * P
+            return spread[number][:, c : c + t1 - t0]
 
         quantise(1)
         gather_words(1)
         quantise(2)
         nc.vector.tensor_copy(early_slot_bytes[:], early_bytes[:].indirect(offs_sb[:]))
-        early = (SLOTS - PUT_OFF) // PER_COLUMN
-        window = words[:, word_column(2) : word_column(2) + WIDE]
-        nc.vector.tensor_copy(slot_words[2][:], window.indirect(offs_sb[:, 0:early]))
-        first_gate = keep([P, T], F32, "first_gate", "raw2")
-        copy_gates(first_gate, 0, T)
+        gather_words(2)
+        gates = {1: keep([P, T], F32, "second_gate", "raw2")}
+        for t0, t1 in PARTS:
+            nc.scalar.copy(gates[1][:, t0:t1], banked_gate(1, t0, t1))
         quantise(LAST)
-        late_window = words[:, word_column(2) : word_column(2) + T]
-        other_gates = shared.tile([P, (TOP - 1) * T], F32, name="other_gates", offset=0)
-        copy_gates(other_gates, T, TOP * T)
-        gates = [first_gate[:]] + [other_gates[:, r * T : (r + 1) * T] for r in range(TOP - 1)]
-        put_off = shared.tile([P, PUT_OFF], U32, name="put_off", offset=4 * TOP * T, align_bytes=64)
-        nc.vector.tensor_copy(put_off[:], late_window.indirect(offs_sb[:, early:]))
+        gates[2] = keep([P, T], F32, "third_gate", "raw%d" % LAST)
+        for t0, t1 in ((0, BANK), (BANK, T)):
+            nc.scalar.copy(gates[2][:, t0:t1], banked_gate(2, t0, t1))
 
         moved = keep([P, (LAST - 1) * SLOTS], U8, "moved")
         shifted = {a: moved[:, (a - 1) * SLOTS : a * SLOTS] for a in range(1, LAST)}
@@ -183,18 +184,14 @@ def tile_moe_ecr_lin_none_kernel(
             )
 
         w_first = keep([P, 2, E, 2 * N], U8, "w_first", "grouped2_0")
-        w_rest = keep([P, 2, E * 2 * N], U8, "w_rest", "early_bytes")
-        whole = [w_first[:, 0], w_first[:, 1], w_rest[:, 0].rearrange("p (e n) -> p e n", e=E)]
-        w_codes = {(a, h): whole[a][:, :, 2 * P * h : 2 * P * (h + 1)] for a in range(LAST) for h in range(HALVES)}
-        load_codes(whole[0], 0)
-        load_codes(whole[1], 1)
+        w_rest = keep([P, 2, E, 2 * N], U8, "w_rest", "early_bytes")
+        w_codes = [w_first[:, 0], w_first[:, 1], w_rest[:, 0], w_rest[:, 1]]
+        load_codes(w_codes[0], 0)
+        load_codes(w_codes[1], 1)
         shift(1)
-        load_codes(whole[2], 2)
+        load_codes(w_codes[2], 2)
         shift(2)
-        for h in range(HALVES):
-            w_codes[LAST, h] = w_rest[:, 1].rearrange("p (h e n) -> p h e n", h=HALVES, e=E)[:, h]
-            columns = word_rows[:, LAST, :, h * P // 2 : (h + 1) * P // 2]
-            nc.sync.dma_start(out=w_codes[LAST, h].bitcast(I32), in_=columns.rearrange("e p n -> p e n"))
+        load_codes(w_codes[LAST], LAST)
 
         nc.vector.tensor_copy(last_slot_bytes[:], last_bytes[:].indirect(offs_sb[:]))
         for g, (e0, e1) in enumerate(GROUPS):
@@ -215,11 +212,11 @@ def tile_moe_ecr_lin_none_kernel(
                 if a == LAST:
                     moving, plane = last_words[e], last_slot_bytes[:, slots]
                 else:
-                    moving = put_off[:] if (a, e) == (2, E - 1) else slot_words[a][:, slots]
+                    moving = slot_words[a][:, slots]
                     plane = (early_slot_bytes if a == 0 else shifted[a])[:, slots]
                 nc.tensor.matmul_mx(
                     out=sums[h, g][:, (e - e0) * C : (e - e0 + 1) * C],
-                    lhsT=w_codes[a, h][:, e].bitcast(FP4X4),
+                    lhsT=w_codes[a][:, e, 2 * P * h : 2 * P * (h + 1)].bitcast(FP4X4),
                     lhsT_scale=w_plane[:, (e * PASSES + a) * N + P * h : (e * PASSES + a) * N + P * (h + 1)],
                     rhs=moving.bitcast(FP8X4),
                     rhs_scale=plane,
@@ -231,10 +228,16 @@ def tile_moe_ecr_lin_none_kernel(
             for h in range(HALVES):
                 for g in range(len(BANKED[h])):
                     multiply(a, h, g)
-        def finish(h):
-            for g, (e0, e1) in enumerate(BANKED[h]):
-                multiply(LAST, h, g)
-                nc.scalar.copy(y[h][:, e0 * C : e1 * C], sums[h, g][:])
+        for h, g in ((0, 0), (1, 0), (0, 1), (0, 2), (1, 1)):
+            multiply(LAST, h, g)
+
+        def empty(h, g, copy):
+            e0, e1 = BANKED[h][g]
+            copy(y[h][:, e0 * C : e1 * C], sums[h, g][:])
+
+        for g in range(len(GROUPS)):
+            empty(0, g, nc.scalar.copy)
+        empty(1, 0, nc.vector.tensor_copy)
 
         term = {(h, r): keep([P, T], F32, "term%d_%d" % (h, r)) for h in range(HALVES) for r in range(TOP)}
         plain = {(h, r): keep([P, T], F32, "plain%d_%d" % (h, r)) for h, r in ((0, 0), (1, 0), (1, 1))}
@@ -248,46 +251,55 @@ def tile_moe_ecr_lin_none_kernel(
         def fetch(h, r, t0=0, t1=T):
             nc.scalar.activation(plain[h, r][:, t0:t1], picked(h, r, t0, t1), COPY)
 
-        def scale(h, r, t0=0, t1=T):
-            nc.vector.tensor_tensor(term[h, r][:, t0:t1], plain[h, r][:, t0:t1], gates[r][:, t0:t1], MULT)
+        def scale(h, r, t0, t1):
+            gate_part = gates[r][:, t0:t1] if (r, t0) == (1, 0) else banked_gate(r, t0, t1)
+            nc.vector.tensor_tensor(term[h, r][:, t0:t1], plain[h, r][:, t0:t1], gate_part, MULT)
 
-        finish(0)
         fetch(0, 0)
-        finish(1)
-        turned = [bank(P, "turned%d" % b, number) for b, number in enumerate((0, 7, 1, 2, 3))]
+        empty(1, 1, nc.scalar.copy)
+        turned = {c0: bank(c1 - c0, "turned%d" % c0, number) for number, (c0, c1) in enumerate(TURNS)}
         back = {t0: bank(t1 - t0, "back%d" % t0, number) for (t0, t1), number in zip(PARTS, (4, 5))}
         staged = keep([P, T], F32, "staged")
         pair = keep([P, T], F32, "pair")
         total = [keep([P, T], F32, "total%d" % h) for h in range(HALVES)]
 
         def turn(r, first, last):
-            for b in range(BLOCKS):
-                nc.tensor.matmul(
-                    turned[b][:], lhsT=term[0, r][:, b * P : (b + 1) * P], rhs=ident[:], start=first, stop=last, is_transpose=True
-                )
+            for c0, c1 in TURNS:
+                for c in range(c0, c1, P):
+                    nc.tensor.matmul(
+                        turned[c0][:, c - c0 : c - c0 + P],
+                        lhsT=term[0, r][:, c : c + P],
+                        rhs=ident[:],
+                        start=first and c == c0,
+                        stop=last and c + P == c1,
+                        is_transpose=True,
+                    )
 
-        fetch(1, 1, *PARTS[0])
+        fetch(1, 1)
         fetch(1, 0)
         weigh(0, 2)
         turn(2, True, False)
         weigh(0, 1)
         turn(1, False, False)
-        scale(0, 0)
-        turn(0, False, True)
         for t0, t1 in PARTS:
-            for c in range(t0, t1, P):
-                nc.scalar.copy(staged[:, c : c + P], turned[c // P][:])
+            scale(0, 0, t0, t1)
+        turn(0, False, True)
+        for c0, c1 in TURNS:
+            nc.scalar.copy(staged[:, c0:c1], turned[c0][:])
+            t0 = max(t for t in back if t <= c0)
+            for c in range(c0, c1, P):
                 nc.tensor.transpose(back[t0][:, c - t0 : c - t0 + P], staged[:, c : c + P], ident[:])
         for t0, t1 in PARTS:
             nc.scalar.copy(total[0][:, t0:t1], back[t0][:])
             nc.sync.dma_start(out=out[0:P, t0:t1], in_=total[0][:, t0:t1])
         weigh(1, 2)
-        scale(1, 1, *PARTS[0])
-        weigh(1, 1, *PARTS[1])
         for t0, t1 in PARTS:
-            nc.vector.tensor_tensor(pair[:, t0:t1], term[1, 2][:, t0:t1], term[1, 1][:, t0:t1], ADD)
-        for t0, t1 in PARTS:
+            scale(1, 1, t0, t1)
+        front, rear = (slice(t0, t1) for t0, t1 in PARTS)
+        nc.gpsimd.tensor_tensor(pair[:, front], term[1, 2][:, front], term[1, 1][:, front], ADD)
+        for t0, t1 in reversed(PARTS):
             scale(1, 0, t0, t1)
-        for (t0, t1), queue in zip(PARTS, (nc.sync, nc.scalar)):
-            nc.vector.tensor_tensor(total[1][:, t0:t1], pair[:, t0:t1], term[1, 0][:, t0:t1], ADD)
-            queue.dma_start(out=out[P:N, t0:t1], in_=total[1][:, t0:t1])
+        nc.vector.tensor_tensor(pair[:, rear], term[1, 2][:, rear], term[1, 0][:, rear], ADD)
+        for part, r, queue in ((front, 0, nc.sync), (rear, 1, nc.scalar)):
+            nc.vector.tensor_tensor(total[1][:, part], pair[:, part], term[1, r][:, part], ADD)
+            queue.dma_start(out=out[P:N, part], in_=total[1][:, part])

@@ -252,7 +252,7 @@ def tile_moe_ecr_lin_none_kernel(
             nc.scalar.activation(plain[h, r][:, t0:t1], picked(h, r, t0, t1), COPY)
 
         def scale(h, r, t0, t1):
-            gate_part = gates[r][:, t0:t1] if (r, t0) == (1, 0) else banked_gate(r, t0, t1)
+            gate_part = banked_gate(r, t0, t1) if r == 0 else gates[r][:, t0:t1]
             nc.vector.tensor_tensor(term[h, r][:, t0:t1], plain[h, r][:, t0:t1], gate_part, MULT)
 
         fetch(0, 0)
@@ -275,8 +275,9 @@ def tile_moe_ecr_lin_none_kernel(
                         is_transpose=True,
                     )
 
-        fetch(1, 1)
-        fetch(1, 0)
+        fetch(1, 1, *PARTS[0])
+        for t0, t1 in reversed(PARTS):
+            fetch(1, 0, t0, t1)
         weigh(0, 2)
         turn(2, True, False)
         weigh(0, 1)
@@ -293,13 +294,15 @@ def tile_moe_ecr_lin_none_kernel(
             nc.scalar.copy(total[0][:, t0:t1], back[t0][:])
             nc.sync.dma_start(out=out[0:P, t0:t1], in_=total[0][:, t0:t1])
         weigh(1, 2)
-        for t0, t1 in PARTS:
-            scale(1, 1, t0, t1)
+        scale(1, 1, *PARTS[0])
         front, rear = (slice(t0, t1) for t0, t1 in PARTS)
         nc.gpsimd.tensor_tensor(pair[:, front], term[1, 2][:, front], term[1, 1][:, front], ADD)
         for t0, t1 in reversed(PARTS):
             scale(1, 0, t0, t1)
         nc.vector.tensor_tensor(pair[:, rear], term[1, 2][:, rear], term[1, 0][:, rear], ADD)
-        for part, r, queue in ((front, 0, nc.sync), (rear, 1, nc.scalar)):
-            nc.vector.tensor_tensor(total[1][:, part], pair[:, part], term[1, r][:, part], ADD)
+        t0, t1 = PARTS[1]
+        last_term = keep([P, t1 - t0], F32, "last_term", "plain1_0")
+        nc.vector.tensor_tensor(last_term[:], picked(1, 1, t0, t1), gates[1][:, rear], MULT)
+        for part, rest, queue in ((front, term[1, 0][:, front], nc.sync), (rear, last_term[:], nc.scalar)):
+            nc.vector.tensor_tensor(total[1][:, part], pair[:, part], rest, ADD)
             queue.dma_start(out=out[P:N, part], in_=total[1][:, part])

from contextlib import ExitStack

import concourse.mybir as mybir
from concourse.masks import make_identity

K, T, E, C, N = 2048, 640, 6, 128, 256
TOP = 3
PAD = 64
SLOTS = E * C
FLOPS = 2 * K * N * SLOTS

F32 = mybir.dt.float32
BF16 = mybir.dt.bfloat16
I32 = mybir.dt.int32
U32 = mybir.dt.uint32
U16 = mybir.dt.uint16
U8 = mybir.dt.uint8
FP8X4 = mybir.dt.float8_e4m3fn_x4
FP4X4 = mybir.dt.float4_e2m1fn_x4
MULT = mybir.AluOpType.mult
ADD = mybir.AluOpType.add
COPY = mybir.ActivationFunctionType.Copy

P = 128
PACK = 4
K_PASS = P * PACK
PASSES = K // K_PASS
LAST = PASSES - 1
HALVES = N // P
QUADRANT = 32
PLANE_ROWS = 4
PER_COLUMN = 16
RUN = 4
BANK = 512
WIDE = 1024
LIVE_ROWS = 3 * QUADRANT + PLANE_ROWS

ROUNDS = (
    ((0, 256, "v"), (256, 384, "s"), (384, 512, "g"), (512, 640, "s")),
    ((0, 256, "s"), (256, 512, "g"), (512, 640, "s")),
    ((0, 256, "s"), (256, 512, "g"), (512, 640, "s")),
    ((0, 384, "s"), (384, 640, "g")),
)
BLOCKS = T // P
GATE_STEP = N * T // BLOCKS
SPACING = QUADRANT // PLANE_ROWS
GROUPS = ((0, 3), (3, 5), (5, 6))
BANKED = (GROUPS, ((0, 2), (2, 6)))
SPREAD = {
    5: ((1, 0), (1, 1), (1, 2)),
    7: ((0, 3), (0, 4), (1, 3), (1, 4)),
    6: ((0, 0), (0, 1), (0, 2), (2, 4)),
    0: ((2, 0), (2, 1), (2, 2), (2, 3)),
}
TURNS = ((0, 128), (128, 256), (256, 384), (384, 640))
PARTS = ((0, 384), (384, 640))


def tile_moe_ecr_lin_none_kernel(
    tc, xT, w_words, w_scales, gate, offs, pos1, pos2, pos3, out
):
    nc = tc.nc
    with ExitStack() as ctx:
        held = ctx.enter_context(tc.tile_pool(name="held", bufs=1))
        psum = ctx.enter_context(tc.psum_pool(name="psum", bufs=1))

        def keep(shape, dtype, name, tag=None):
            return held.tile(shape, dtype, name=name, tag=tag or name, align_bytes=64)

        def bank(width, name, number):
            return psum.tile([P, width], F32, name=name, tag="bank%d" % number)

        offs_sb = keep([P, SLOTS // PER_COLUMN], U16, "offs_sb")
        pos_sb = [keep([P, T // PER_COLUMN], U16, "pos_sb%d" % r) for r in range(TOP)]
        early_bytes = keep([P, WIDE], U8, "early_bytes")
        last_bytes = keep([P, WIDE], U8, "last_bytes")
        words = keep([P, LAST * T + WIDE], U32, "words")
        y = [keep([P, SLOTS + PAD], F32, "y%d" % h) for h in range(HALVES)]

        gate_rows = keep([P, P], F32, "gate_rows")
        nc.gpsimd.memset(gate_rows[:], 0.0)
        nc.vector.memset(y[1][:, SLOTS:], 0.0)
        nc.scalar.copy(y[0][:, SLOTS:], y[1][:, SLOTS:])
        nc.vector.memset(early_bytes[:].bitcast(I32), 0)
        nc.vector.memset(last_bytes[:].bitcast(I32), 0)
        nc.vector.memset(words[:, PASSES * T :].bitcast(I32), 0)
        ident = keep([P, P], F32, "ident")
        make_identity(nc, ident[:])

        w_plane = keep([P, E * PASSES * N], U8, "w_plane")
        raw = [keep([P, PACK, T], F32, "raw%d" % a) for a in range(PASSES)]
        for a in range(PASSES):
            rows = xT[a * K_PASS : (a + 1) * K_PASS, :].rearrange("(p j) t -> p j t", j=PACK)
            nc.sync.dma_start(out=raw[a][:], in_=rows)
            if a == LAST - 1:
                nc.sync.dma_start(
                    out=w_plane[0:P:SPACING].bitcast(I32).rearrange("q (m n) -> q m n", m=E * PASSES),
                    in_=w_scales.bitcast(I32).rearrange("e a q n -> q (e a) n"),
                )
            if a == 0:
                nc.sync.dma_start(offs_sb[:], offs)
                pieces = gate.rearrange("r n t -> (r n t)").rearrange("(m s) -> m s", s=GATE_STEP)
                nc.sync.dma_start(out=gate_rows[0 : TOP * BLOCKS], in_=pieces[:, 0:P])

        for tile, entries in zip(pos_sb, (pos1, pos2, pos3)):
            nc.sync.dma_start(tile[:], entries)

        for r in range(1, PLANE_ROWS):
            nc.sync.dma_start(out=w_plane[r:P:QUADRANT].bitcast(I32), in_=w_plane[SPACING * r : P : QUADRANT].bitcast(I32))
        word_rows = w_words.bitcast(I32)

        def load_codes(codes, a):
            nc.sync.dma_start(out=codes.bitcast(I32), in_=word_rows[:, a].rearrange("e p n -> p e n"))

        slot_words = [keep([P, SLOTS], U32, "slot_words%d" % a) for a in range(LAST)]
        last_slot_words = [keep([P, (e1 - e0) * C], U32, "last_slot_words%d" % e0) for e0, e1 in GROUPS]
        early_slot_bytes = keep([P, SLOTS], U8, "early_slot_bytes")
        last_slot_bytes = keep([P, SLOTS], U8, "last_slot_bytes")

        def word_column(a):
            return (LAST - a) * T

        def quantise(a):
            grouped = {}
            for t0, t1, engine in ROUNDS[a]:
                grouped[t0] = keep([P, (t1 - t0) * PACK], BF16, "grouped%d_%d" % (a, t0))
                if engine == "g":
                    dst = grouped[t0][:].rearrange("p (t j) -> p t j", j=PACK)
                    nc.gpsimd.tensor_copy(dst, raw[a][:, :, t0:t1].rearrange("p j t -> p t j"))
                    continue
                dst = grouped[t0][:].rearrange("p (c i j) -> p c j i", i=RUN, j=PACK)
                src = raw[a][:, :, t0:t1].rearrange("p j (c i) -> p c j i", i=RUN)
                if engine == "v":
                    nc.vector.tensor_copy(dst, src)
                else:
                    nc.scalar.copy(dst, src)
            for t0, t1, engine in ROUNDS[a]:
                plane = last_bytes[:, t0:t1] if a == LAST else early_bytes[PLANE_ROWS * a :, t0:t1]
                c0 = word_column(a)
                nc.vector.quantize_mx(out=words[:, c0 + t0 : c0 + t1].bitcast(FP8X4), scales=plane, in_=grouped[t0][:])

        def gather_words(a):
            window = words[:, word_column(a) : word_column(a) + WIDE]
            nc.vector.tensor_copy(slot_words[a][:], window.indirect(offs_sb[:]))

        quantise(0)
        gather_words(0)

        turned_rows = bank(P, "turned_rows", 0)
        nc.tensor.transpose(turned_rows[:], gate_rows[:], ident[:])
        gate_columns = keep([P, TOP * BLOCKS], F32, "gate_columns", "raw0")
        nc.scalar.copy(gate_columns[:], turned_rows[:, 0 : TOP * BLOCKS])
        spread = {number: bank(len(blocks) * P, "spread%d" % number, number) for number, blocks in SPREAD.items()}
        for number, blocks in SPREAD.items():
            for i, (r, b) in enumerate(blocks):
                column = gate_columns[:, r * BLOCKS + b : r * BLOCKS + b + 1]
                nc.tensor.transpose(spread[number][:, i * P : (i + 1) * P], column.to_broadcast([P, P]), ident[:])

        def banked_gate(r, t0, t1):
            number = [n for n, blocks in SPREAD.items() if (r, t0 // P) in blocks][0]
            c = SPREAD[number].index((r, t0 // P)) * P
            return spread[number][:, c : c + t1 - t0]

        quantise(1)
        gather_words(1)
        quantise(2)
        nc.vector.tensor_copy(early_slot_bytes[:], early_bytes[:].indirect(offs_sb[:]))
        gather_words(2)
        gates = {1: keep([P, T], F32, "second_gate", "raw2")}
        for t0, t1 in PARTS:
            nc.scalar.copy(gates[1][:, t0:t1], banked_gate(1, t0, t1))
        quantise(LAST)
        gates[2] = keep([P, T], F32, "third_gate", "raw%d" % LAST)
        for t0, t1 in ((0, BANK), (BANK, T)):
            nc.scalar.copy(gates[2][:, t0:t1], banked_gate(2, t0, t1))

        moved = keep([P, (LAST - 1) * SLOTS], U8, "moved")
        shifted = {a: moved[:, (a - 1) * SLOTS : a * SLOTS] for a in range(1, LAST)}

        def shift(a):
            nc.sync.dma_start(
                out=shifted[a][0:LIVE_ROWS, :].bitcast(I32),
                in_=early_slot_bytes[PLANE_ROWS * a : PLANE_ROWS * a + LIVE_ROWS, :].bitcast(I32),
            )

        w_first = keep([P, 2, E, 2 * N], U8, "w_first", "grouped2_0")
        w_rest = keep([P, 2, E, 2 * N], U8, "w_rest", "early_bytes")
        w_codes = [w_first[:, 0], w_first[:, 1], w_rest[:, 0], w_rest[:, 1]]
        load_codes(w_codes[0], 0)
        load_codes(w_codes[1], 1)
        shift(1)
        load_codes(w_codes[2], 2)
        shift(2)
        load_codes(w_codes[LAST], LAST)

        nc.vector.tensor_copy(last_slot_bytes[:], last_bytes[:].indirect(offs_sb[:]))
        for g, (e0, e1) in enumerate(GROUPS):
            entries = offs_sb[:, e0 * C // PER_COLUMN : e1 * C // PER_COLUMN]
            nc.vector.tensor_copy(last_slot_words[g][:], words[:, 0:T].indirect(entries))

        sums = {
            (h, g): bank((e1 - e0) * C, "sums%d_%d" % (h, g), 1 + len(GROUPS) * h + g)
            for h in range(HALVES)
            for g, (e0, e1) in enumerate(BANKED[h])
        }
        last_words = {e: last_slot_words[g][:, (e - e0) * C : (e - e0 + 1) * C] for g, (e0, e1) in enumerate(GROUPS) for e in range(e0, e1)}

        def multiply(a, h, g):
            e0, e1 = BANKED[h][g]
            for e in range(e0, e1):
                slots = slice(e * C, (e + 1) * C)
                if a == LAST:
                    moving, plane = last_words[e], last_slot_bytes[:, slots]
                else:
                    moving = slot_words[a][:, slots]
                    plane = (early_slot_bytes if a == 0 else shifted[a])[:, slots]
                nc.tensor.matmul_mx(
                    out=sums[h, g][:, (e - e0) * C : (e - e0 + 1) * C],
                    lhsT=w_codes[a][:, e, 2 * P * h : 2 * P * (h + 1)].bitcast(FP4X4),
                    lhsT_scale=w_plane[:, (e * PASSES + a) * N + P * h : (e * PASSES + a) * N + P * (h + 1)],
                    rhs=moving.bitcast(FP8X4),
                    rhs_scale=plane,
                    start=(a == 0 and e == e0),
                    stop=(a == LAST and e == e1 - 1),
                )

        for a in range(LAST):
            for h in range(HALVES):
                for g in range(len(BANKED[h])):
                    multiply(a, h, g)
        for h, g in ((0, 0), (1, 0), (0, 1), (0, 2), (1, 1)):
            multiply(LAST, h, g)

        def empty(h, g, copy):
            e0, e1 = BANKED[h][g]
            copy(y[h][:, e0 * C : e1 * C], sums[h, g][:])

        for g in range(len(GROUPS)):
            empty(0, g, nc.scalar.copy)
        empty(1, 0, nc.vector.tensor_copy)

        term = {(h, r): keep([P, T], F32, "term%d_%d" % (h, r)) for h in range(HALVES) for r in range(TOP)}
        plain = {(h, r): keep([P, T], F32, "plain%d_%d" % (h, r)) for h, r in ((0, 0), (1, 0), (1, 1))}

        def picked(h, r, t0, t1):
            return y[h][:].indirect(pos_sb[r][:, t0 // PER_COLUMN : t1 // PER_COLUMN])

        def weigh(h, r, t0=0, t1=T):
            nc.vector.tensor_tensor(term[h, r][:, t0:t1], picked(h, r, t0, t1), gates[r][:, t0:t1], MULT)

        def fetch(h, r, t0=0, t1=T):
            nc.scalar.activation(plain[h, r][:, t0:t1], picked(h, r, t0, t1), COPY)

        def scale(h, r, t0, t1):
            gate_part = banked_gate(r, t0, t1) if r == 0 else gates[r][:, t0:t1]
            nc.vector.tensor_tensor(term[h, r][:, t0:t1], plain[h, r][:, t0:t1], gate_part, MULT)

        fetch(0, 0)
        empty(1, 1, nc.scalar.copy)
        turned = {c0: bank(c1 - c0, "turned%d" % c0, number) for number, (c0, c1) in enumerate(TURNS)}
        back = {t0: bank(t1 - t0, "back%d" % t0, number) for (t0, t1), number in zip(PARTS, (4, 5))}
        staged = keep([P, T], F32, "staged")
        pair = keep([P, T], F32, "pair")
        total = [keep([P, T], F32, "total%d" % h) for h in range(HALVES)]

        def turn(r, first, last):
            for c0, c1 in TURNS:
                for c in range(c0, c1, P):
                    nc.tensor.matmul(
                        turned[c0][:, c - c0 : c - c0 + P],
                        lhsT=term[0, r][:, c : c + P],
                        rhs=ident[:],
                        start=first and c == c0,
                        stop=last and c + P == c1,
                        is_transpose=True,
                    )

        fetch(1, 1, *PARTS[0])
        for t0, t1 in reversed(PARTS):
            fetch(1, 0, t0, t1)
        weigh(0, 2)
        turn(2, True, False)
        weigh(0, 1)
        turn(1, False, False)
        for t0, t1 in PARTS:
            scale(0, 0, t0, t1)
        turn(0, False, True)
        for c0, c1 in TURNS:
            nc.scalar.copy(staged[:, c0:c1], turned[c0][:])
            t0 = max(t for t in back if t <= c0)
            for c in range(c0, c1, P):
                nc.tensor.transpose(back[t0][:, c - t0 : c - t0 + P], staged[:, c : c + P], ident[:])
        for t0, t1 in PARTS:
            nc.scalar.copy(total[0][:, t0:t1], back[t0][:])
            nc.sync.dma_start(out=out[0:P, t0:t1], in_=total[0][:, t0:t1])
        weigh(1, 2)
        scale(1, 1, *PARTS[0])
        front, rear = (slice(t0, t1) for t0, t1 in PARTS)
        nc.gpsimd.tensor_tensor(pair[:, front], term[1, 2][:, front], term[1, 1][:, front], ADD)
        for t0, t1 in reversed(PARTS):
            scale(1, 0, t0, t1)
        nc.vector.tensor_tensor(pair[:, rear], term[1, 2][:, rear], term[1, 0][:, rear], ADD)
        t0, t1 = PARTS[1]
        last_term = keep([P, t1 - t0], F32, "last_term", "plain1_0")
        nc.vector.tensor_tensor(last_term[:], picked(1, 1, t0, t1), gates[1][:, rear], MULT)
        for part, rest, queue in ((front, term[1, 0][:, front], nc.sync), (rear, last_term[:], nc.scalar)):
            nc.vector.tensor_tensor(total[1][:, part], pair[:, part], rest, ADD)
            queue.dma_start(out=out[P:N, part], in_=total[1][:, part])
